import numpy as np
import ml_dtypes


def mxq(x, axis, fmt="e4m3"):
    dtype, down = {"e4m3": (ml_dtypes.float8_e4m3fn, 7), "e5m2": (ml_dtypes.float8_e5m2, 14)}[fmt]
    v = np.moveaxis(np.asarray(x, np.float32).astype(ml_dtypes.bfloat16).astype(np.float64), axis, -1)
    blocks = v.reshape(v.shape[:-1] + (-1, 32))
    amax = np.abs(blocks).max(-1, keepdims=True)
    byte = np.maximum(np.where(amax > 0, np.frexp(amax)[1] - 1 + 127, 0) - down, 1)
    scale = np.exp2(byte - 127.0)
    codes = (blocks / scale).astype(np.float32).astype(dtype).astype(np.float64)
    return np.moveaxis((codes * scale).reshape(v.shape), -1, axis)


WIDE = False


def mx_kscale(k):
    if not WIDE:
        return np.ones(k)
    levels = np.array([10, -10, 5, -5, 0])
    if k % 512:
        return np.exp2(np.random.permutation(np.resize(levels, k // 32))).repeat(32)
    a = np.empty((k // 512, 16))
    for p in range(k // 512):
        a[p, :8] = np.random.permutation(np.resize(levels, 8))
        for g in range(8):
            far = levels[np.abs(levels - a[p, g]) >= 10]
            a[p, g + 8] = far[np.random.randint(len(far))]
    return np.exp2(a.ravel()).repeat(32)


def f64(x):
    return np.asarray(x).astype(np.float64)


def striped(idx):
    return np.tile(idx.reshape(-1, 16).T, (8, 1)).astype(np.uint16)


def unstriped(offs):
    return offs[:16].T.reshape(-1).astype(np.int64)


E2M1 = np.array([0.0, 0.5, 1.0, 1.5, 2.0, 3.0, 4.0, 6.0, -0.0, -0.5, -1.0, -1.5, -2.0, -3.0, -4.0, -6.0])


def pack_weight(w, fmt):
    k, n = w.shape
    w = f64(np.asarray(w, np.float32).astype(ml_dtypes.bfloat16)).reshape(k // 32, 32, n)
    amax = np.abs(w).max(1)
    if fmt == "e4m3":
        byte = np.frexp(amax)[1] - 1 + 127 - 7
    else:
        mant, ex = np.frexp(amax / 6.0)
        byte = np.where(mant > 0.5, ex, ex - 1) + 127
    byte = np.clip(np.where(amax > 0, byte, 1), 1, 254)
    scaled = (w * np.exp2(127.0 - byte)[:, None, :]).reshape(k, n).astype(np.float32)
    by_word = np.ascontiguousarray(scaled.reshape(k // 512, 128, 4, n).transpose(0, 1, 3, 2))
    if fmt == "e4m3":
        words = by_word.astype(ml_dtypes.float8_e4m3fn).view(np.uint8)
    else:
        c = by_word.astype(ml_dtypes.float4_e2m1fn).view(np.uint8) & 0xF
        words = (c[..., 0::2] | (c[..., 1::2] << 4)).reshape(k // 512, 128, 2 * n)
    return np.ascontiguousarray(words), np.ascontiguousarray(byte.astype(np.uint8).reshape(k // 512, 16, n))


def unpack_weight(words, scales, fmt):
    g, _, n = scales.shape
    words = np.ascontiguousarray(words).reshape(g, 128, n, -1)
    if fmt == "e4m3":
        vals = words.view(ml_dtypes.float8_e4m3fn).astype(np.float64)
    else:
        nib = np.empty((g, 128, n, 4), np.uint8)
        nib[..., 0::2] = words & 0xF
        nib[..., 1::2] = words >> 4
        vals = E2M1[nib]
    vals = vals * np.repeat(np.exp2(scales.astype(np.float64) - 127.0), 8, axis=1)[..., None]
    return vals.transpose(0, 1, 3, 2).reshape(g * 512, n)


def gelu(v):
    return 0.5 * v * (1.0 + np.tanh(np.sqrt(2.0 / np.pi) * (v + 0.044715 * v**3)))


K, K2, H, T, T2, S = 1024, 512, 1024, 2048, 2048, 1024

def setup_inputs():
    n = np.random.standard_normal
    s = mx_kscale(K)[:, None]
    s2 = mx_kscale(K2)[:, None]
    u = mx_kscale(H)[:, None]
    tab_words, tab_scales = pack_weight(n((K, T)) * s, "e4m3")
    wp_words, wp_scales = pack_weight(0.8 * n((K, H)) / np.sqrt(K) / s, "e2m1")
    wr_words, wr_scales = pack_weight(1.5 * n((H, H)) / np.sqrt(H) / u, "e4m3")
    perm = np.random.permutation(T2)
    return {
        "tab_words": tab_words, "tab_scales": tab_scales,
        "offs": striped(np.random.permutation(T)[:S]),
        "xT": (np.round(16 * n((K2, T2))) / 16 * s2).astype(np.float32),
        "offs2": striped(perm[:S]),
        "offs3": striped(perm[-S:]),
        "wp_words": wp_words, "wp_scales": wp_scales,
        "wx": (0.5 * n((K2, H)) / np.sqrt(K2) / s2).astype(np.float32),
        "gain": (np.exp(0.3 * n(H)) * u[:, 0]).astype(np.float32),
        "wr_words": wr_words, "wr_scales": wr_scales,
    }

def reference(tab_words, tab_scales, offs, xT, offs2, offs3, wp_words, wp_scales,
              wx, gain, wr_words, wr_scales):
    v = unpack_weight(tab_words, tab_scales, "e4m3")[:, unstriped(offs)]
    x = f64(xT)[:, unstriped(offs2)] - f64(xT)[:, unstriped(offs3)]
    xq = mxq(x, 0, "e4m3")
    wp = unpack_weight(wp_words, wp_scales, "e2m1")
    wxq = mxq(f64(wx), 0, "e4m3")
    a = wp.T @ v
    b = wxq.T @ xq
    h = f64(gain)[:, None] * np.tanh(a + b)
    hq = mxq(h, 0, "e4m3")
    wr = unpack_weight(wr_words, wr_scales, "e4m3")
    return np.tanh((wr.T @ hq) + b)

@@ -1,0 +1,262 @@
+from contextlib import ExitStack
+
+import concourse.mybir as mybir
+
+K, K2, H, T, S = 1024, 512, 1024, 2048, 1024
+FLOPS = 2 * S * H * (K + K2 + H)
+
+F32 = mybir.dt.float32
+BF16 = mybir.dt.bfloat16
+I32 = mybir.dt.int32
+U32 = mybir.dt.uint32
+U16 = mybir.dt.uint16
+U8 = mybir.dt.uint8
+FP8X4 = mybir.dt.float8_e4m3fn_x4
+FP4X4 = mybir.dt.float4_e2m1fn_x4
+ALU = mybir.AluOpType
+ACT = mybir.ActivationFunctionType
+
+P = 128
+PACK = 4
+W = 512
+HALVES = S // W
+GROUPS = H // (P * PACK)
+PASSES = K // (P * PACK)
+
+
+def tile_list_snowpack_recurrence_kernel(tc, tab_words, tab_scales, offs, xT, offs2, offs3, wp_words,
+                                                   wp_scales, wx, gain, wr_words, wr_scales, out):
+    nc = tc.nc
+    with ExitStack() as ctx:
+        keep = ctx.enter_context(tc.tile_pool(name="keep", bufs=1))
+        ring = ctx.enter_context(tc.tile_pool(name="ring", bufs=2))
+        psum = ctx.enter_context(tc.psum_pool(name="psum", bufs=1))
+
+        list_v = keep.tile([P, S // 16], U16, name="list_v")
+        list_2 = keep.tile([P, S // 16], U16, name="list_2")
+        list_3 = keep.tile([P, S // 16], U16, name="list_3")
+        tab_s = keep.tile([P, T // 4], I32, name="tab_s", align_bytes=64)
+        w_s_raw = keep.tile([P, PASSES, H // 4], I32, name="w_s_raw", align_bytes=64)
+        v_s1 = keep.tile([P, S // 4], I32, name="v_s1", align_bytes=64)
+        warm = keep.tile([P, 8], F32, name="warm")
+        warm_out = keep.tile([P, 8], F32, name="warm_out")
+        nc.vector.memset(w_s_raw[:], 0)
+        nc.vector.memset(tab_s[:], 0)
+        nc.vector.memset(v_s1[:], 0)
+        nc.vector.memset(warm[:], 0.0)
+        nc.scalar.activation(warm_out[:], warm[:], ACT.Tanh)
+
+        wp_raw = keep.tile([P, PASSES, H // 2], I32, name="wp_raw", align_bytes=64)
+        planes = [keep.tile([P, T], F32, name="plane%d" % t, align_bytes=64) for t in range(PACK)]
+        wx_raw = [keep.tile([P, PACK, W], F32, name="wx_raw%d" % g, align_bytes=64) for g in range(GROUPS)]
+        tab_w = [keep.tile([P, T], I32, name="tab_w%d" % a, align_bytes=64) for a in range(PASSES)]
+        wr_raw = [keep.tile([P, H], I32, name="wr_raw%d" % a, align_bytes=64) for a in range(GROUPS)]
+        gain_sb = keep.tile([P, GROUPS, PACK], F32, name="gain_sb")
+        x_rows = xT.rearrange("(p t) n -> t p n", t=PACK)
+        wx_rows = wx.rearrange("(p j) c -> p j c", j=PACK)
+        nc.sync.dma_start(list_3[:], offs3)
+        nc.sync.dma_start(list_2[:], offs2)
+        nc.sync.dma_start(wp_raw[:], wp_words.rearrange("a p n -> p a n").bitcast(I32))
+        for t in range(2):
+            nc.sync.dma_start(planes[t][:], x_rows[t])
+        for q in range(4):
+            nc.sync.dma_start(w_s_raw[32 * q:32 * q + 4],
+                              wp_scales[:, 4 * q:4 * q + 4, :].rearrange("a r n -> r a n").bitcast(I32))
+        nc.sync.dma_start(planes[2][:], x_rows[2])
+        nc.sync.dma_start(wx_raw[0][:], wx_rows[:, :, 0:W])
+        for q in range(4):
+            nc.sync.dma_start(w_s_raw[32 * q + 4:32 * q + 8],
+                              wr_scales[:, 4 * q:4 * q + 4, :].rearrange("a r n -> r a n").bitcast(I32))
+        nc.sync.dma_start(planes[3][:], x_rows[3])
+        nc.sync.dma_start(wx_raw[1][:], wx_rows[:, :, W:2 * W])
+        for q in range(4):
+            nc.sync.dma_start(tab_s[32 * q:32 * q + 8, :], tab_scales[:, 4 * q:4 * q + 4, :].bitcast(I32))
+        nc.sync.dma_start(list_v[:], offs)
+        for a in range(PASSES):
+            nc.sync.dma_start(tab_w[a][:], tab_words[a].rearrange("p n t -> p (n t)").bitcast(I32))
+        nc.sync.dma_start(gain_sb[:], gain.rearrange("(g p t) -> p g t", g=GROUPS, t=PACK))
+        for a in range(GROUPS):
+            nc.sync.dma_start(wr_raw[a][:], wr_words[a].rearrange("p n t -> p (n t)").bitcast(I32))
+
+        wp_c = keep.tile([P, PASSES, 2 * H], U8, name="wp_c", align_bytes=64)
+        w_s = keep.tile([P, PASSES, H], U8, name="w_s", align_bytes=64)
+        wr_c = [keep.tile([P, H], I32, name="wr_c%d" % a, align_bytes=64) for a in range(GROUPS)]
+        wx_c = [keep.tile([P, W], U32, name="wx_c%d" % g, align_bytes=64) for g in range(GROUPS)]
+        wx_s = [keep.tile([P, W], U8, name="wx_s%d" % g, align_bytes=64) for g in range(GROUPS)]
+        nc.vector.tensor_copy(
+            wp_c[:].bitcast(U16).rearrange("p a (g t m) -> p (a g) m t", g=GROUPS, t=PACK),
+            wp_raw[:].bitcast(U16).rearrange("p a (g m t) -> p (a g) m t", g=GROUPS, t=PACK))
+
+        def order_scales():
+            nc.vector.tensor_copy(
+                w_s[:].rearrange("p a (g t m) -> p (a g) m t", g=GROUPS, t=PACK),
+                w_s_raw[:].bitcast(U8).rearrange("p a (g m t) -> p (a g) m t", g=GROUPS, t=PACK))
+
+        def order_wr(a):
+            nc.vector.tensor_copy(
+                wr_c[a][:].rearrange("p (g t m) -> p g m t", g=GROUPS, t=PACK),
+                wr_raw[a][:].rearrange("p (g m t) -> p g m t", g=GROUPS, t=PACK))
+
+        def round_wx(g):
+            wx_b = ring.tile([P, W * PACK], BF16, name="wx_b", align_bytes=64)
+            nc.scalar.copy(wx_b[:].rearrange("p (t m j) -> p m j t", t=PACK, j=PACK),
+                           wx_raw[g][:].rearrange("p j (m t) -> p m j t", t=PACK))
+            return wx_b
+
+        def quantise(src, codes, scales):
+            nc.vector.quantize_mx(out=codes[:].bitcast(FP8X4), scales=scales[:], in_=src[:])
+
+        def entries(lst, h):
+            return lst[:, h * (W // 16):(h + 1) * (W // 16)]
+
+        def gather_x(h, name):
+            minus = keep.tile([P, PACK, W], F32, name=name, align_bytes=64)
+            diff = keep.tile([P, PACK, W], F32, name="diff", align_bytes=64)
+            for t in range(PACK + 1):
+                if t < PACK:
+                    nc.vector.tensor_copy(minus[:, t, :], planes[t][:].indirect(entries(list_3, h)))
+                if t > 0:
+                    nc.vector.tensor_tensor(diff[:, t - 1, :], planes[t - 1][:].indirect(entries(list_2, h)),
+                                            minus[:, t - 1, :], ALU.subtract)
+            return diff
+
+        def round_x(diff, name):
+            x_b = keep.tile([P, W * PACK], BF16, name=name, align_bytes=64)
+            nc.scalar.copy(x_b[:].rearrange("p (c i t) -> p c t i", i=2, t=PACK),
+                           diff[:].rearrange("p t (c i) -> p c t i", i=2))
+            return x_b
+
+        x_c = [keep.tile([P, W], U32, name="x_c%d" % h, align_bytes=64) for h in range(HALVES)]
+        x_s = [keep.tile([P, W], U8, name="x_s%d" % h, align_bytes=64) for h in range(HALVES)]
+        v_c = [keep.tile([P, S], U32, name="v_c%d" % a, align_bytes=64) for a in range(PASSES)]
+        v_s0 = keep.tile([P, S], U8, name="v_s0", align_bytes=64)
+
+        def gather_v():
+            nc.vector.tensor_copy(v_c[0][:], tab_w[0][:].bitcast(U32).indirect(list_v[:]))
+            for h in range(HALVES):
+                nc.vector.tensor_copy(v_c[1][:, h * W:(h + 1) * W],
+                                      tab_w[1][:].bitcast(U32).indirect(entries(list_v, h)))
+
+        def gather_v_scales():
+            nc.vector.tensor_copy(v_s0[:], tab_s[:].bitcast(U8).indirect(list_v[:]))
+            for q in range(4):
+                nc.sync.dma_start(v_s1[32 * q:32 * q + 4, :], v_s0[32 * q + 4:32 * q + 8, :].bitcast(I32))
+
+        def pass_b(bank, h, g, t, stop):
+            cols = slice(t * P, (t + 1) * P)
+            nc.tensor.matmul_mx(bank[:], lhsT=wx_c[g][:, cols].bitcast(FP8X4), lhsT_scale=wx_s[g][:, cols],
+                                rhs=x_c[h][:].bitcast(FP8X4), rhs_scale=x_s[h][:], start=True, stop=stop)
+
+        def passes_a(bank, h, g, t, start):
+            c0 = (g * PACK + t) * P
+            v_s = [v_s0[:], v_s1[:].bitcast(U8)]
+            for a in range(PASSES):
+                nc.tensor.matmul_mx(bank[:], lhsT=wp_c[:, a, 2 * c0:2 * (c0 + P)].bitcast(FP4X4),
+                                    lhsT_scale=w_s[:, a, c0:c0 + P],
+                                    rhs=v_c[a][:, h * W:(h + 1) * W].bitcast(FP8X4), rhs_scale=v_s[a][:, h * W:(h + 1) * W],
+                                    start=(start and a == 0), stop=(a == PASSES - 1))
+
+        def passes_c(bank, g, t, h_c, h_s, start):
+            c0 = (g * PACK + t) * P
+            for a in range(GROUPS):
+                nc.tensor.matmul_mx(bank[:], lhsT=wr_c[a][:, c0:c0 + P].bitcast(FP8X4),
+                                    lhsT_scale=w_s[4:P, a, c0:c0 + P],
+                                    rhs=h_c[a][:].bitcast(FP8X4), rhs_scale=h_s[a][:],
+                                    start=(start and a == 0), stop=(a == GROUPS - 1))
+
+        b_kept = []
+
+        def keep_b(h):
+            for g in range(GROUPS):
+                b_kept.append(keep.tile([P, PACK, W], F32, name="b_kept%d" % g, align_bytes=64))
+                for t in range(PACK):
+                    bank = psum.tile([P, W], F32, name="bank", bufs=8)
+                    pass_b(bank, h, g, t, True)
+                    if g == 0:
+                        nc.scalar.copy(b_kept[g][:, t, :], bank[:])
+                    else:
+                        nc.vector.tensor_copy(b_kept[g][:, t, :], bank[:])
+
+        def sum_with_b(bank, g, t):
+            z = ring.tile([P, W], F32, name="z", bufs=4, align_bytes=64)
+            nc.vector.tensor_tensor(z[:], bank[:], b_kept[g][:, t, :], ALU.add)
+            return z
+
+        def first_state(h, g, kept):
+            th = keep.tile([P, PACK, W], F32, name="th%d_%d" % (h, g), align_bytes=64)
+            for t in range(PACK):
+                bank = psum.tile([P, W], F32, name="bank", bufs=8)
+                if kept:
+                    passes_a(bank, h, g, t, True)
+                    src = sum_with_b(bank, g, t)
+                else:
+                    pass_b(bank, h, g, t, False)
+                    passes_a(bank, h, g, t, False)
+                    src = bank
+                nc.scalar.activation(th[:, t, :], src[:], ACT.Tanh)
+            return th
+
+        def apply_gain(th, g):
+            h_b = ring.tile([P, W * PACK], BF16, name="h_b", align_bytes=64)
+            nc.vector.tensor_tensor(h_b[:].rearrange("p (c i t) -> p c t i", i=2, t=PACK),
+                                    th[:].rearrange("p t (c i) -> p c t i", i=2),
+                                    gain_sb[:, g, :].unsqueeze(1).unsqueeze(3).to_broadcast([P, W // 2, PACK, 2]),
+                                    ALU.mult)
+            return h_b
+
+        def apply_gain_scalar(th, g):
+            h_p = ring.tile([P, PACK, W], BF16, name="h_p", align_bytes=64)
+            for t in range(PACK):
+                nc.scalar.activation(h_p[:, t, :], th[:, t, :], ACT.Copy, scale=gain_sb[:, g, t:t + 1])
+            h_b = ring.tile([P, W * PACK], BF16, name="h_b", align_bytes=64)
+            nc.vector.tensor_copy(h_b[:].rearrange("p (c i t) -> p c t i", i=4, t=PACK),
+                                  h_p[:].rearrange("p t (c i) -> p c t i", i=4))
+            return h_b
+
+        out_rows = out.rearrange("(g p t) j -> g t p j", g=GROUPS, t=PACK)
+
+        def second_state(h, h_c, h_s, kept):
+            for g in range(GROUPS):
+                for t in range(PACK):
+                    bank = psum.tile([P, W], F32, name="bank", bufs=8)
+                    if kept:
+                        passes_c(bank, g, t, h_c, h_s, True)
+                        src = sum_with_b(bank, g, t)
+                    else:
+                        pass_b(bank, h, g, t, False)
+                        passes_c(bank, g, t, h_c, h_s, False)
+                        src = bank
+                    res = ring.tile([P, W], F32, name="res", bufs=4, align_bytes=64)
+                    nc.scalar.activation(res[:], src[:], ACT.Tanh)
+                    nc.sync.dma_start(out_rows[g, t][:, h * W:(h + 1) * W], res[:])
+
+        h_c = [[keep.tile([P, W], U32, name="h_c%d_%d" % (h, g), align_bytes=64) for g in range(GROUPS)]
+               for h in range(HALVES)]
+        h_s = [[keep.tile([P, W], U8, name="h_s%d_%d" % (h, g), align_bytes=64) for g in range(GROUPS)]
+               for h in range(HALVES)]
+
+        wx_b0 = round_wx(0)
+        diff0 = gather_x(0, "minus0")
+        order_scales()
+        x_b0 = round_x(diff0, "x_b0")
+        wx_b1 = round_wx(1)
+        quantise(wx_b0, wx_c[0], wx_s[0])
+        gather_v_scales()
+        quantise(x_b0, x_c[0], x_s[0])
+        quantise(wx_b1, wx_c[1], wx_s[1])
+        gather_v()
+        diff1 = gather_x(1, "tab_w1")
+        order_wr(0)
+        order_wr(1)
+        h_bs = [apply_gain_scalar(first_state(0, g, False), g) for g in range(GROUPS)]
+        x_b1 = round_x(diff1, "th0_1")
+        for g in range(GROUPS):
+            quantise(h_bs[g], h_c[0][g], h_s[0][g])
+        quantise(x_b1, x_c[1], x_s[1])
+        keep_b(1)
+        ths = [first_state(1, g, True) for g in range(GROUPS)]
+        second_state(0, h_c[0], h_s[0], False)
+        h_bs = [apply_gain(ths[g], g) for g in range(GROUPS)]
+        for g in range(GROUPS):
+            quantise(h_bs[g], h_c[1][g], h_s[1][g])
+        second_state(1, h_c[1], h_s[1], True)

@@ -18,10 +18,16 @@ ACT = mybir.ActivationFunctionType
 
 P = 128
 PACK = 4
+QUADRANTS = 4
+STRIPE = 16
 W = 512
 HALVES = S // W
 GROUPS = H // (P * PACK)
 PASSES = K // (P * PACK)
+BANKS = 8
+SUMS_IN_FLIGHT = 6
+STORES_IN_FLIGHT = 8
+GAIN_ON_SCALAR = W // 4
 
 
 def tile_list_snowpack_recurrence_kernel(tc, tab_words, tab_scales, offs, xT, offs2, offs3, wp_words,
@@ -32,231 +38,231 @@ def tile_list_snowpack_recurrence_kernel(tc, tab_words, tab_scales, offs, xT, of
         ring = ctx.enter_context(tc.tile_pool(name="ring", bufs=2))
         psum = ctx.enter_context(tc.psum_pool(name="psum", bufs=1))
 
-        list_v = keep.tile([P, S // 16], U16, name="list_v")
-        list_2 = keep.tile([P, S // 16], U16, name="list_2")
-        list_3 = keep.tile([P, S // 16], U16, name="list_3")
+        list_v = keep.tile([P, S // STRIPE], U16, name="list_v")
+        list_2 = keep.tile([P, S // STRIPE], U16, name="list_2")
+        list_3 = keep.tile([P, S // STRIPE], U16, name="list_3")
+
         tab_s = keep.tile([P, T // 4], I32, name="tab_s", align_bytes=64)
-        w_s_raw = keep.tile([P, PASSES, H // 4], I32, name="w_s_raw", align_bytes=64)
+        w_s_raw = keep.tile([P, H // 4], I32, name="w_s_raw", align_bytes=64)
+        wp_s1 = keep.tile([P, H // 4], I32, name="wp_s1", align_bytes=64)
         v_s1 = keep.tile([P, S // 4], I32, name="v_s1", align_bytes=64)
-        warm = keep.tile([P, 8], F32, name="warm")
-        warm_out = keep.tile([P, 8], F32, name="warm_out")
+        nc.gpsimd.memset(tab_s[:], 0)
         nc.vector.memset(w_s_raw[:], 0)
-        nc.vector.memset(tab_s[:], 0)
         nc.vector.memset(v_s1[:], 0)
-        nc.vector.memset(warm[:], 0.0)
-        nc.scalar.activation(warm_out[:], warm[:], ACT.Tanh)
+        nc.vector.memset(wp_s1[:], 0)
 
         wp_raw = keep.tile([P, PASSES, H // 2], I32, name="wp_raw", align_bytes=64)
         planes = [keep.tile([P, T], F32, name="plane%d" % t, align_bytes=64) for t in range(PACK)]
         wx_raw = [keep.tile([P, PACK, W], F32, name="wx_raw%d" % g, align_bytes=64) for g in range(GROUPS)]
         tab_w = [keep.tile([P, T], I32, name="tab_w%d" % a, align_bytes=64) for a in range(PASSES)]
-        wr_raw = [keep.tile([P, H], I32, name="wr_raw%d" % a, align_bytes=64) for a in range(GROUPS)]
         gain_sb = keep.tile([P, GROUPS, PACK], F32, name="gain_sb")
         x_rows = xT.rearrange("(p t) n -> t p n", t=PACK)
         wx_rows = wx.rearrange("(p j) c -> p j c", j=PACK)
+        for q in range(QUADRANTS):
+            nc.gpsimd.dma_start(tab_s[32 * q:32 * q + 8, :], tab_scales[:, 4 * q:4 * q + 4, :].bitcast(I32))
         nc.sync.dma_start(list_3[:], offs3)
         nc.sync.dma_start(list_2[:], offs2)
         nc.sync.dma_start(wp_raw[:], wp_words.rearrange("a p n -> p a n").bitcast(I32))
-        for t in range(2):
+        for t in range(PACK):
             nc.sync.dma_start(planes[t][:], x_rows[t])
-        for q in range(4):
-            nc.sync.dma_start(w_s_raw[32 * q:32 * q + 4],
-                              wp_scales[:, 4 * q:4 * q + 4, :].rearrange("a r n -> r a n").bitcast(I32))
-        nc.sync.dma_start(planes[2][:], x_rows[2])
         nc.sync.dma_start(wx_raw[0][:], wx_rows[:, :, 0:W])
-        for q in range(4):
-            nc.sync.dma_start(w_s_raw[32 * q + 4:32 * q + 8],
-                              wr_scales[:, 4 * q:4 * q + 4, :].rearrange("a r n -> r a n").bitcast(I32))
-        nc.sync.dma_start(planes[3][:], x_rows[3])
-        nc.sync.dma_start(wx_raw[1][:], wx_rows[:, :, W:2 * W])
-        for q in range(4):
-            nc.sync.dma_start(tab_s[32 * q:32 * q + 8, :], tab_scales[:, 4 * q:4 * q + 4, :].bitcast(I32))
         nc.sync.dma_start(list_v[:], offs)
+        for q in range(QUADRANTS):
+            nc.sync.dma_start(w_s_raw[32 * q:32 * q + 8, :], wp_scales[:, 4 * q:4 * q + 4, :].bitcast(I32))
+        nc.sync.dma_start(wx_raw[1][:], wx_rows[:, :, W:2 * W])
         for a in range(PASSES):
             nc.sync.dma_start(tab_w[a][:], tab_words[a].rearrange("p n t -> p (n t)").bitcast(I32))
+        for q in range(QUADRANTS):
+            nc.sync.dma_start(w_s_raw[32 * q + 8:32 * q + 16, :], wr_scales[:, 4 * q:4 * q + 4, :].bitcast(I32))
         nc.sync.dma_start(gain_sb[:], gain.rearrange("(g p t) -> p g t", g=GROUPS, t=PACK))
-        for a in range(GROUPS):
-            nc.sync.dma_start(wr_raw[a][:], wr_words[a].rearrange("p n t -> p (n t)").bitcast(I32))
 
         wp_c = keep.tile([P, PASSES, 2 * H], U8, name="wp_c", align_bytes=64)
-        w_s = keep.tile([P, PASSES, H], U8, name="w_s", align_bytes=64)
-        wr_c = [keep.tile([P, H], I32, name="wr_c%d" % a, align_bytes=64) for a in range(GROUPS)]
-        wx_c = [keep.tile([P, W], U32, name="wx_c%d" % g, align_bytes=64) for g in range(GROUPS)]
-        wx_s = [keep.tile([P, W], U8, name="wx_s%d" % g, align_bytes=64) for g in range(GROUPS)]
         nc.vector.tensor_copy(
             wp_c[:].bitcast(U16).rearrange("p a (g t m) -> p (a g) m t", g=GROUPS, t=PACK),
             wp_raw[:].bitcast(U16).rearrange("p a (g m t) -> p (a g) m t", g=GROUPS, t=PACK))
 
-        def order_scales():
+        def order_scales(place):
+            ordered = keep.tile([P, H], U8, name=place, align_bytes=64)
             nc.vector.tensor_copy(
-                w_s[:].rearrange("p a (g t m) -> p (a g) m t", g=GROUPS, t=PACK),
-                w_s_raw[:].bitcast(U8).rearrange("p a (g m t) -> p (a g) m t", g=GROUPS, t=PACK))
+                ordered[:].rearrange("p (g t m) -> p g m t", g=GROUPS, t=PACK),
+                w_s_raw[:].bitcast(U8).rearrange("p (g m t) -> p g m t", g=GROUPS, t=PACK))
+            for q in range(QUADRANTS):
+                nc.sync.dma_start(wp_s1[32 * q:32 * q + 4, :], ordered[32 * q + 4:32 * q + 8, :].bitcast(I32))
+            return ordered
 
-        def order_wr(a):
+        def load_wr(place):
+            raw = keep.tile([P, GROUPS, H], I32, name=place, align_bytes=64)
+            nc.sync.dma_start(raw[:], wr_words.rearrange("a p n t -> p a (n t)").bitcast(I32))
+            return raw
+
+        def order_wr(raw, place):
+            ordered = keep.tile([P, GROUPS, H], I32, name=place, align_bytes=64)
             nc.vector.tensor_copy(
-                wr_c[a][:].rearrange("p (g t m) -> p g m t", g=GROUPS, t=PACK),
-                wr_raw[a][:].rearrange("p (g m t) -> p g m t", g=GROUPS, t=PACK))
+                ordered[:].rearrange("p a (g t m) -> p (a g) m t", g=GROUPS, t=PACK),
+                raw[:].rearrange("p a (g m t) -> p (a g) m t", g=GROUPS, t=PACK))
+            return ordered
 
         def round_wx(g):
-            wx_b = ring.tile([P, W * PACK], BF16, name="wx_b", align_bytes=64)
-            nc.scalar.copy(wx_b[:].rearrange("p (t m j) -> p m j t", t=PACK, j=PACK),
+            rounded = ring.tile([P, W * PACK], BF16, name="wx_b", align_bytes=64)
+            nc.scalar.copy(rounded[:].rearrange("p (t m j) -> p m j t", t=PACK, j=PACK),
                            wx_raw[g][:].rearrange("p j (m t) -> p m j t", t=PACK))
-            return wx_b
+            return rounded[:]
 
-        def quantise(src, codes, scales):
-            nc.vector.quantize_mx(out=codes[:].bitcast(FP8X4), scales=scales[:], in_=src[:])
+        def mx_tiles(name):
+            return (keep.tile([P, W], U32, name=name + "_codes", align_bytes=64),
+                    keep.tile([P, W], U8, name=name + "_scales", align_bytes=64))
 
-        def entries(lst, h):
-            return lst[:, h * (W // 16):(h + 1) * (W // 16)]
+        def quantise(rounded, operand):
+            codes, scales = operand
+            nc.vector.quantize_mx(out=codes[:].bitcast(FP8X4), scales=scales[:], in_=rounded)
 
-        def gather_x(h, name):
-            minus = keep.tile([P, PACK, W], F32, name=name, align_bytes=64)
+        def entries(list_tile, half):
+            return list_tile[:, half * (W // STRIPE):(half + 1) * (W // STRIPE)]
+
+        def gather_x(half, place):
+            minus = keep.tile([P, PACK, W], F32, name=place, align_bytes=64)
             diff = keep.tile([P, PACK, W], F32, name="diff", align_bytes=64)
             for t in range(PACK + 1):
                 if t < PACK:
-                    nc.vector.tensor_copy(minus[:, t, :], planes[t][:].indirect(entries(list_3, h)))
+                    nc.vector.tensor_copy(minus[:, t, :], planes[t][:].indirect(entries(list_3, half)))
                 if t > 0:
-                    nc.vector.tensor_tensor(diff[:, t - 1, :], planes[t - 1][:].indirect(entries(list_2, h)),
+                    nc.vector.tensor_tensor(diff[:, t - 1, :], planes[t - 1][:].indirect(entries(list_2, half)),
                                             minus[:, t - 1, :], ALU.subtract)
             return diff
 
-        def round_x(diff, name):
-            x_b = keep.tile([P, W * PACK], BF16, name=name, align_bytes=64)
-            nc.scalar.copy(x_b[:].rearrange("p (c i t) -> p c t i", i=2, t=PACK),
+        def round_x(diff, place):
+            rounded = keep.tile([P, W * PACK], BF16, name=place, align_bytes=64)
+            nc.scalar.copy(rounded[:].rearrange("p (c i t) -> p c t i", i=2, t=PACK),
                            diff[:].rearrange("p t (c i) -> p c t i", i=2))
-            return x_b
+            return rounded[:]
 
-        x_c = [keep.tile([P, W], U32, name="x_c%d" % h, align_bytes=64) for h in range(HALVES)]
-        x_s = [keep.tile([P, W], U8, name="x_s%d" % h, align_bytes=64) for h in range(HALVES)]
-        v_c = [keep.tile([P, S], U32, name="v_c%d" % a, align_bytes=64) for a in range(PASSES)]
-        v_s0 = keep.tile([P, S], U8, name="v_s0", align_bytes=64)
-
-        def gather_v():
-            nc.vector.tensor_copy(v_c[0][:], tab_w[0][:].bitcast(U32).indirect(list_v[:]))
-            for h in range(HALVES):
-                nc.vector.tensor_copy(v_c[1][:, h * W:(h + 1) * W],
-                                      tab_w[1][:].bitcast(U32).indirect(entries(list_v, h)))
+        def gather_v(half, place):
+            words = keep.tile([P, PASSES, W], U32, name=place, align_bytes=64)
+            for a in range(PASSES):
+                nc.vector.tensor_copy(words[:, a, :], tab_w[a][:].bitcast(U32).indirect(entries(list_v, half)))
+            return words
 
         def gather_v_scales():
             nc.vector.tensor_copy(v_s0[:], tab_s[:].bitcast(U8).indirect(list_v[:]))
-            for q in range(4):
+            for q in range(QUADRANTS):
                 nc.sync.dma_start(v_s1[32 * q:32 * q + 4, :], v_s0[32 * q + 4:32 * q + 8, :].bitcast(I32))
 
-        def pass_b(bank, h, g, t, stop):
-            cols = slice(t * P, (t + 1) * P)
-            nc.tensor.matmul_mx(bank[:], lhsT=wx_c[g][:, cols].bitcast(FP8X4), lhsT_scale=wx_s[g][:, cols],
-                                rhs=x_c[h][:].bitcast(FP8X4), rhs_scale=x_s[h][:], start=True, stop=stop)
+        def new_bank():
+            return psum.tile([P, W], F32, name="bank", bufs=BANKS)
 
-        def passes_a(bank, h, g, t, start):
+        def pass_b(bank, half, g, t, stop):
+            cols = slice(t * P, (t + 1) * P)
+            wx_codes, wx_scales = wx_q[g]
+            x_codes, x_scales = x_q[half]
+            nc.tensor.matmul_mx(bank[:], lhsT=wx_codes[:, cols].bitcast(FP8X4), lhsT_scale=wx_scales[:, cols],
+                                rhs=x_codes[:].bitcast(FP8X4), rhs_scale=x_scales[:], start=True, stop=stop)
+
+        def passes_wp(bank, half, g, t, start):
             c0 = (g * PACK + t) * P
             v_s = [v_s0[:], v_s1[:].bitcast(U8)]
+            wp_s = [w_s[:], wp_s1[:].bitcast(U8)]
             for a in range(PASSES):
                 nc.tensor.matmul_mx(bank[:], lhsT=wp_c[:, a, 2 * c0:2 * (c0 + P)].bitcast(FP4X4),
-                                    lhsT_scale=w_s[:, a, c0:c0 + P],
-                                    rhs=v_c[a][:, h * W:(h + 1) * W].bitcast(FP8X4), rhs_scale=v_s[a][:, h * W:(h + 1) * W],
+                                    lhsT_scale=wp_s[a][:, c0:c0 + P],
+                                    rhs=v_c[half][:, a, :].bitcast(FP8X4),
+                                    rhs_scale=v_s[a][:, half * W:(half + 1) * W],
                                     start=(start and a == 0), stop=(a == PASSES - 1))
 
-        def passes_c(bank, g, t, h_c, h_s, start):
+        def passes_wr(bank, half, g, t, start):
             c0 = (g * PACK + t) * P
             for a in range(GROUPS):
-                nc.tensor.matmul_mx(bank[:], lhsT=wr_c[a][:, c0:c0 + P].bitcast(FP8X4),
-                                    lhsT_scale=w_s[4:P, a, c0:c0 + P],
-                                    rhs=h_c[a][:].bitcast(FP8X4), rhs_scale=h_s[a][:],
+                h_codes, h_scales = h_q[half][a]
+                nc.tensor.matmul_mx(bank[:], lhsT=wr_c[:, a, c0:c0 + P].bitcast(FP8X4),
+                                    lhsT_scale=w_s[8 + 4 * a:P, c0:c0 + P],
+                                    rhs=h_codes[:].bitcast(FP8X4), rhs_scale=h_scales[:],
                                     start=(start and a == 0), stop=(a == GROUPS - 1))
 
-        b_kept = []
-
-        def keep_b(h):
+        def keep_b(half):
+            kept = []
             for g in range(GROUPS):
-                b_kept.append(keep.tile([P, PACK, W], F32, name="b_kept%d" % g, align_bytes=64))
+                kept.append(keep.tile([P, PACK, W], F32, name="b_kept%d" % g, align_bytes=64))
                 for t in range(PACK):
-                    bank = psum.tile([P, W], F32, name="bank", bufs=8)
-                    pass_b(bank, h, g, t, True)
-                    if g == 0:
-                        nc.scalar.copy(b_kept[g][:, t, :], bank[:])
-                    else:
-                        nc.vector.tensor_copy(b_kept[g][:, t, :], bank[:])
+                    bank = new_bank()
+                    pass_b(bank, half, g, t, True)
+                    nc.scalar.copy(kept[g][:, t, :], bank[:])
+            return kept
 
-        def sum_with_b(bank, g, t):
-            z = ring.tile([P, W], F32, name="z", bufs=4, align_bytes=64)
-            nc.vector.tensor_tensor(z[:], bank[:], b_kept[g][:, t, :], ALU.add)
-            return z
+        def product_plus_b(passes, half, g, t, b_kept):
+            bank = new_bank()
+            if b_kept is None:
+                pass_b(bank, half, g, t, False)
+                passes(bank, half, g, t, False)
+                return bank
+            passes(bank, half, g, t, True)
+            total = ring.tile([P, W], F32, name="total", bufs=SUMS_IN_FLIGHT, align_bytes=64)
+            nc.vector.tensor_tensor(total[:], bank[:], b_kept[g][:, t, :], ALU.add)
+            return total
 
-        def first_state(h, g, kept):
-            th = keep.tile([P, PACK, W], F32, name="th%d_%d" % (h, g), align_bytes=64)
+        def first_step(half, g, b_kept):
+            th = keep.tile([P, PACK, W], F32, name="th%d_%d" % (half, g), align_bytes=64)
             for t in range(PACK):
-                bank = psum.tile([P, W], F32, name="bank", bufs=8)
-                if kept:
-                    passes_a(bank, h, g, t, True)
-                    src = sum_with_b(bank, g, t)
-                else:
-                    pass_b(bank, h, g, t, False)
-                    passes_a(bank, h, g, t, False)
-                    src = bank
-                nc.scalar.activation(th[:, t, :], src[:], ACT.Tanh)
+                nc.scalar.activation(th[:, t, :], product_plus_b(passes_wp, half, g, t, b_kept)[:], ACT.Tanh)
             return th
 
-        def apply_gain(th, g):
-            h_b = ring.tile([P, W * PACK], BF16, name="h_b", align_bytes=64)
-            nc.vector.tensor_tensor(h_b[:].rearrange("p (c i t) -> p c t i", i=2, t=PACK),
-                                    th[:].rearrange("p t (c i) -> p c t i", i=2),
-                                    gain_sb[:, g, :].unsqueeze(1).unsqueeze(3).to_broadcast([P, W // 2, PACK, 2]),
-                                    ALU.mult)
-            return h_b
+        def apply_gain(th, g, on_scalar):
+            rounded = keep.tile([P, W, PACK], BF16, name="h_b%d" % g, align_bytes=64)
+            if on_scalar > 0:
+                by_tile = ring.tile([P, PACK, on_scalar], BF16, name="h_by_tile", align_bytes=64)
+                for t in range(PACK):
+                    nc.scalar.activation(by_tile[:, t, :], th[:, t, 0:on_scalar], ACT.Copy,
+                                         scale=gain_sb[:, g, t:t + 1])
+                nc.vector.tensor_copy(rounded[:, 0:on_scalar, :].rearrange("p (c i) t -> p c t i", i=4),
+                                      by_tile[:].rearrange("p t (c i) -> p c t i", i=4))
+            if on_scalar < W:
+                pairs = (W - on_scalar) // 2
+                nc.vector.tensor_tensor(rounded[:, on_scalar:W, :].rearrange("p (c i) t -> p c t i", i=2),
+                                        th[:, :, on_scalar:W].rearrange("p t (c i) -> p c t i", i=2),
+                                        gain_sb[:, g, :].unsqueeze(1).unsqueeze(3).to_broadcast([P, pairs, PACK, 2]),
+                                        ALU.mult)
+            return rounded[:].rearrange("p j t -> p (j t)")
 
-        def apply_gain_scalar(th, g):
-            h_p = ring.tile([P, PACK, W], BF16, name="h_p", align_bytes=64)
-            for t in range(PACK):
-                nc.scalar.activation(h_p[:, t, :], th[:, t, :], ACT.Copy, scale=gain_sb[:, g, t:t + 1])
-            h_b = ring.tile([P, W * PACK], BF16, name="h_b", align_bytes=64)
-            nc.vector.tensor_copy(h_b[:].rearrange("p (c i t) -> p c t i", i=4, t=PACK),
-                                  h_p[:].rearrange("p t (c i) -> p c t i", i=4))
-            return h_b
-
-        out_rows = out.rearrange("(g p t) j -> g t p j", g=GROUPS, t=PACK)
-
-        def second_state(h, h_c, h_s, kept):
+        def second_step(half, b_kept):
+            out_rows = out.rearrange("(g p t) j -> g t p j", g=GROUPS, t=PACK)
             for g in range(GROUPS):
                 for t in range(PACK):
-                    bank = psum.tile([P, W], F32, name="bank", bufs=8)
-                    if kept:
-                        passes_c(bank, g, t, h_c, h_s, True)
-                        src = sum_with_b(bank, g, t)
-                    else:
-                        pass_b(bank, h, g, t, False)
-                        passes_c(bank, g, t, h_c, h_s, False)
-                        src = bank
-                    res = ring.tile([P, W], F32, name="res", bufs=4, align_bytes=64)
-                    nc.scalar.activation(res[:], src[:], ACT.Tanh)
-                    nc.sync.dma_start(out_rows[g, t][:, h * W:(h + 1) * W], res[:])
+                    total = product_plus_b(passes_wr, half, g, t, b_kept)
+                    result = ring.tile([P, W], F32, name="result", bufs=STORES_IN_FLIGHT, align_bytes=64)
+                    nc.scalar.activation(result[:], total[:], ACT.Tanh)
+                    nc.sync.dma_start(out_rows[g, t][:, half * W:(half + 1) * W], result[:])
 
-        h_c = [[keep.tile([P, W], U32, name="h_c%d_%d" % (h, g), align_bytes=64) for g in range(GROUPS)]
-               for h in range(HALVES)]
-        h_s = [[keep.tile([P, W], U8, name="h_s%d_%d" % (h, g), align_bytes=64) for g in range(GROUPS)]
-               for h in range(HALVES)]
+        wx_q = [mx_tiles("wx%d" % g) for g in range(GROUPS)]
+        x_q = [mx_tiles("x%d" % half) for half in range(HALVES)]
+        h_q = [[mx_tiles("h%d_%d" % (half, g)) for g in range(GROUPS)] for half in range(HALVES)]
+        v_s0 = keep.tile([P, S], U8, name="v_s0", align_bytes=64)
+        v_c = []
 
         wx_b0 = round_wx(0)
         diff0 = gather_x(0, "minus0")
-        order_scales()
-        x_b0 = round_x(diff0, "x_b0")
-        wx_b1 = round_wx(1)
-        quantise(wx_b0, wx_c[0], wx_s[0])
+        x_b0 = round_x(diff0, "wx_raw0")
         gather_v_scales()
-        quantise(x_b0, x_c[0], x_s[0])
-        quantise(wx_b1, wx_c[1], wx_s[1])
-        gather_v()
-        diff1 = gather_x(1, "tab_w1")
-        order_wr(0)
-        order_wr(1)
-        h_bs = [apply_gain_scalar(first_state(0, g, False), g) for g in range(GROUPS)]
-        x_b1 = round_x(diff1, "th0_1")
+        quantise(wx_b0, wx_q[0])
+        quantise(x_b0, x_q[0])
+        quantise(round_wx(1), wx_q[1])
+        v_c.append(gather_v(0, "v_c0"))
+        w_s = order_scales("minus0")
+
+        diff1 = gather_x(1, "w_s_raw")
+        wr_raw = load_wr("w_s_raw")
+
+        h_b0 = apply_gain(first_step(0, 0, None), 0, W)
+        th1 = first_step(0, 1, None)
+        x_b1 = round_x(diff1, "th0_0")
+        quantise(h_b0, h_q[0][0])
+        quantise(x_b1, x_q[1])
+
+        v_c.append(gather_v(1, "th0_0"))
+        wr_c = order_wr(wr_raw, "diff")
+        quantise(apply_gain(th1, 1, GAIN_ON_SCALAR), h_q[0][1])
+
+        b_second = keep_b(1)
+        ths = [first_step(1, g, b_second) for g in range(GROUPS)]
+        second_step(0, None)
+        h_bs = [apply_gain(ths[g], g, 0) for g in range(GROUPS)]
         for g in range(GROUPS):
-            quantise(h_bs[g], h_c[0][g], h_s[0][g])
-        quantise(x_b1, x_c[1], x_s[1])
-        keep_b(1)
-        ths = [first_state(1, g, True) for g in range(GROUPS)]
-        second_state(0, h_c[0], h_s[0], False)
-        h_bs = [apply_gain(ths[g], g) for g in range(GROUPS)]
-        for g in range(GROUPS):
-            quantise(h_bs[g], h_c[1][g], h_s[1][g])
-        second_state(1, h_c[1], h_s[1], True)
+            quantise(h_bs[g], h_q[1][g])
+        second_step(1, b_second)

@@ -43,13 +43,13 @@ def tile_list_snowpack_recurrence_kernel(tc, tab_words, tab_scales, offs, xT, of
         list_3 = keep.tile([P, S // STRIPE], U16, name="list_3")
 
         tab_s = keep.tile([P, T // 4], I32, name="tab_s", align_bytes=64)
-        w_s_raw = keep.tile([P, H // 4], I32, name="w_s_raw", align_bytes=64)
-        wp_s1 = keep.tile([P, H // 4], I32, name="wp_s1", align_bytes=64)
+        wp_s_raw = keep.tile([P, PASSES, H // 4], I32, name="wp_s_raw", align_bytes=64)
+        wr_s_raw = keep.tile([P, H // 4], I32, name="wr_s_raw", align_bytes=64)
         v_s1 = keep.tile([P, S // 4], I32, name="v_s1", align_bytes=64)
         nc.gpsimd.memset(tab_s[:], 0)
-        nc.vector.memset(w_s_raw[:], 0)
+        nc.vector.memset(wp_s_raw[:], 0)
+        nc.vector.memset(wr_s_raw[:], 0)
         nc.vector.memset(v_s1[:], 0)
-        nc.vector.memset(wp_s1[:], 0)
 
         wp_raw = keep.tile([P, PASSES, H // 2], I32, name="wp_raw", align_bytes=64)
         planes = [keep.tile([P, T], F32, name="plane%d" % t, align_bytes=64) for t in range(PACK)]
@@ -58,42 +58,41 @@ def tile_list_snowpack_recurrence_kernel(tc, tab_words, tab_scales, offs, xT, of
         gain_sb = keep.tile([P, GROUPS, PACK], F32, name="gain_sb")
         x_rows = xT.rearrange("(p t) n -> t p n", t=PACK)
         wx_rows = wx.rearrange("(p j) c -> p j c", j=PACK)
-        for q in range(QUADRANTS):
-            nc.gpsimd.dma_start(tab_s[32 * q:32 * q + 8, :], tab_scales[:, 4 * q:4 * q + 4, :].bitcast(I32))
+        nc.sync.dma_start(list_v[:], offs)
         nc.sync.dma_start(list_3[:], offs3)
         nc.sync.dma_start(list_2[:], offs2)
         nc.sync.dma_start(wp_raw[:], wp_words.rearrange("a p n -> p a n").bitcast(I32))
-        for t in range(PACK):
-            nc.sync.dma_start(planes[t][:], x_rows[t])
-        nc.sync.dma_start(wx_raw[0][:], wx_rows[:, :, 0:W])
-        nc.sync.dma_start(list_v[:], offs)
+        nc.sync.dma_start(planes[0][:], x_rows[0])
         for q in range(QUADRANTS):
-            nc.sync.dma_start(w_s_raw[32 * q:32 * q + 8, :], wp_scales[:, 4 * q:4 * q + 4, :].bitcast(I32))
+            nc.sync.dma_start(tab_s[32 * q:32 * q + 8, :], tab_scales[:, 4 * q:4 * q + 4, :].bitcast(I32))
+        v_s0 = keep.tile([P, S], U8, name="v_s0", align_bytes=64)
+        nc.vector.tensor_copy(v_s0[:], tab_s[:].bitcast(U8).indirect(list_v[:]))
+        for q in range(QUADRANTS):
+            nc.gpsimd.dma_start(v_s1[32 * q:32 * q + 4, :], v_s0[32 * q + 4:32 * q + 8, :].bitcast(I32))
+        nc.sync.dma_start(planes[1][:], x_rows[1])
+        nc.sync.dma_start(planes[2][:], x_rows[2])
+        nc.sync.dma_start(planes[3][:], x_rows[3])
+        nc.sync.dma_start(wx_raw[0][:], wx_rows[:, :, 0:W])
+        for q in range(QUADRANTS):
+            nc.sync.dma_start(wp_s_raw[32 * q:32 * q + 4, :, :],
+                              wp_scales[:, 4 * q:4 * q + 4, :].rearrange("a r n -> r a n").bitcast(I32))
         nc.sync.dma_start(wx_raw[1][:], wx_rows[:, :, W:2 * W])
         for a in range(PASSES):
             nc.sync.dma_start(tab_w[a][:], tab_words[a].rearrange("p n t -> p (n t)").bitcast(I32))
-        for q in range(QUADRANTS):
-            nc.sync.dma_start(w_s_raw[32 * q + 8:32 * q + 16, :], wr_scales[:, 4 * q:4 * q + 4, :].bitcast(I32))
         nc.sync.dma_start(gain_sb[:], gain.rearrange("(g p t) -> p g t", g=GROUPS, t=PACK))
+        for q in range(QUADRANTS):
+            nc.sync.dma_start(wr_s_raw[32 * q:32 * q + 8, :], wr_scales[:, 4 * q:4 * q + 4, :].bitcast(I32))
 
         wp_c = keep.tile([P, PASSES, 2 * H], U8, name="wp_c", align_bytes=64)
         nc.vector.tensor_copy(
             wp_c[:].bitcast(U16).rearrange("p a (g t m) -> p (a g) m t", g=GROUPS, t=PACK),
             wp_raw[:].bitcast(U16).rearrange("p a (g m t) -> p (a g) m t", g=GROUPS, t=PACK))
 
-        def order_scales(place):
-            ordered = keep.tile([P, H], U8, name=place, align_bytes=64)
-            nc.vector.tensor_copy(
-                ordered[:].rearrange("p (g t m) -> p g m t", g=GROUPS, t=PACK),
-                w_s_raw[:].bitcast(U8).rearrange("p (g m t) -> p g m t", g=GROUPS, t=PACK))
-            for q in range(QUADRANTS):
-                nc.sync.dma_start(wp_s1[32 * q:32 * q + 4, :], ordered[32 * q + 4:32 * q + 8, :].bitcast(I32))
+        def order_scales(raw, columns, place):
+            ordered = keep.tile([P, columns], U8, name=place, align_bytes=64)
+            nc.vector.tensor_copy(ordered[:].rearrange("p (g t m) -> p g m t", m=P, t=PACK),
+                                  raw.bitcast(U8).rearrange("p (g m t) -> p g m t", m=P, t=PACK))
             return ordered
-
-        def load_wr(place):
-            raw = keep.tile([P, GROUPS, H], I32, name=place, align_bytes=64)
-            nc.sync.dma_start(raw[:], wr_words.rearrange("a p n t -> p a (n t)").bitcast(I32))
-            return raw
 
         def order_wr(raw, place):
             ordered = keep.tile([P, GROUPS, H], I32, name=place, align_bytes=64)
@@ -102,8 +101,8 @@ def tile_list_snowpack_recurrence_kernel(tc, tab_words, tab_scales, offs, xT, of
                 raw[:].rearrange("p a (g m t) -> p (a g) m t", g=GROUPS, t=PACK))
             return ordered
 
-        def round_wx(g):
-            rounded = ring.tile([P, W * PACK], BF16, name="wx_b", align_bytes=64)
+        def round_wx(g, place):
+            rounded = keep.tile([P, W * PACK], BF16, name=place, align_bytes=64)
             nc.scalar.copy(rounded[:].rearrange("p (t m j) -> p m j t", t=PACK, j=PACK),
                            wx_raw[g][:].rearrange("p j (m t) -> p m j t", t=PACK))
             return rounded[:]
@@ -130,6 +129,20 @@ def tile_list_snowpack_recurrence_kernel(tc, tab_words, tab_scales, offs, xT, of
                                             minus[:, t - 1, :], ALU.subtract)
             return diff
 
+        def gather_x_apart(half, place):
+            both = keep.tile([P, 2, PACK, W], F32, name=place, align_bytes=64)
+            for t in range(PACK):
+                nc.vector.tensor_copy(both[:, 0, t, :], planes[t][:].indirect(entries(list_3, half)))
+                nc.vector.tensor_copy(both[:, 1, t, :], planes[t][:].indirect(entries(list_2, half)))
+            return both[:, 1, :, :], both[:, 0, :, :]
+
+        def subtract_x(plus, minus, place):
+            rounded = keep.tile([P, W * PACK], BF16, name=place, align_bytes=64)
+            nc.vector.tensor_tensor(rounded[:].rearrange("p (c i t) -> p c t i", i=2, t=PACK),
+                                    plus.rearrange("p t (c i) -> p c t i", i=2),
+                                    minus.rearrange("p t (c i) -> p c t i", i=2), ALU.subtract)
+            return rounded[:]
+
         def round_x(diff, place):
             rounded = keep.tile([P, W * PACK], BF16, name=place, align_bytes=64)
             nc.scalar.copy(rounded[:].rearrange("p (c i t) -> p c t i", i=2, t=PACK),
@@ -141,11 +154,6 @@ def tile_list_snowpack_recurrence_kernel(tc, tab_words, tab_scales, offs, xT, of
             for a in range(PASSES):
                 nc.vector.tensor_copy(words[:, a, :], tab_w[a][:].bitcast(U32).indirect(entries(list_v, half)))
             return words
-
-        def gather_v_scales():
-            nc.vector.tensor_copy(v_s0[:], tab_s[:].bitcast(U8).indirect(list_v[:]))
-            for q in range(QUADRANTS):
-                nc.sync.dma_start(v_s1[32 * q:32 * q + 4, :], v_s0[32 * q + 4:32 * q + 8, :].bitcast(I32))
 
         def new_bank():
             return psum.tile([P, W], F32, name="bank", bufs=BANKS)
@@ -160,10 +168,9 @@ def tile_list_snowpack_recurrence_kernel(tc, tab_words, tab_scales, offs, xT, of
         def passes_wp(bank, half, g, t, start):
             c0 = (g * PACK + t) * P
             v_s = [v_s0[:], v_s1[:].bitcast(U8)]
-            wp_s = [w_s[:], wp_s1[:].bitcast(U8)]
             for a in range(PASSES):
                 nc.tensor.matmul_mx(bank[:], lhsT=wp_c[:, a, 2 * c0:2 * (c0 + P)].bitcast(FP4X4),
-                                    lhsT_scale=wp_s[a][:, c0:c0 + P],
+                                    lhsT_scale=wp_s[:, a * H + c0:a * H + c0 + P],
                                     rhs=v_c[half][:, a, :].bitcast(FP8X4),
                                     rhs_scale=v_s[a][:, half * W:(half + 1) * W],
                                     start=(start and a == 0), stop=(a == PASSES - 1))
@@ -173,7 +180,7 @@ def tile_list_snowpack_recurrence_kernel(tc, tab_words, tab_scales, offs, xT, of
             for a in range(GROUPS):
                 h_codes, h_scales = h_q[half][a]
                 nc.tensor.matmul_mx(bank[:], lhsT=wr_c[:, a, c0:c0 + P].bitcast(FP8X4),
-                                    lhsT_scale=w_s[8 + 4 * a:P, c0:c0 + P],
+                                    lhsT_scale=wr_s[4 * a:P, c0:c0 + P],
                                     rhs=h_codes[:].bitcast(FP8X4), rhs_scale=h_scales[:],
                                     start=(start and a == 0), stop=(a == GROUPS - 1))
 
@@ -199,7 +206,7 @@ def tile_list_snowpack_recurrence_kernel(tc, tab_words, tab_scales, offs, xT, of
             return total
 
         def first_step(half, g, b_kept):
-            th = keep.tile([P, PACK, W], F32, name="th%d_%d" % (half, g), align_bytes=64)
+            th = keep.tile([P, PACK, W], F32, name="th%d" % g, align_bytes=64)
             for t in range(PACK):
                 nc.scalar.activation(th[:, t, :], product_plus_b(passes_wp, half, g, t, b_kept)[:], ACT.Tanh)
             return th
@@ -221,6 +228,12 @@ def tile_list_snowpack_recurrence_kernel(tc, tab_words, tab_scales, offs, xT, of
                                         ALU.mult)
             return rounded[:].rearrange("p j t -> p (j t)")
 
+        def gain_on_gpsimd(th, g):
+            rounded = keep.tile([P, W, PACK], BF16, name="h_b%d" % g, align_bytes=64)
+            nc.gpsimd.tensor_tensor(rounded[:], th[:].rearrange("p t c -> p c t"),
+                                    gain_sb[:, g, :].unsqueeze(1).to_broadcast([P, W, PACK]), ALU.mult)
+            return rounded[:].rearrange("p j t -> p (j t)")
+
         def second_step(half, b_kept):
             out_rows = out.rearrange("(g p t) j -> g t p j", g=GROUPS, t=PACK)
             for g in range(GROUPS):
@@ -233,31 +246,28 @@ def tile_list_snowpack_recurrence_kernel(tc, tab_words, tab_scales, offs, xT, of
         wx_q = [mx_tiles("wx%d" % g) for g in range(GROUPS)]
         x_q = [mx_tiles("x%d" % half) for half in range(HALVES)]
         h_q = [[mx_tiles("h%d_%d" % (half, g)) for g in range(GROUPS)] for half in range(HALVES)]
-        v_s0 = keep.tile([P, S], U8, name="v_s0", align_bytes=64)
         v_c = []
 
-        wx_b0 = round_wx(0)
+        wx_b0 = round_wx(0, "wx_b0")
         diff0 = gather_x(0, "minus0")
         x_b0 = round_x(diff0, "wx_raw0")
-        gather_v_scales()
+        wp_s = order_scales(wp_s_raw[:].rearrange("p a n -> p (a n)"), PASSES * H, "wp_s")
         quantise(wx_b0, wx_q[0])
-        quantise(x_b0, x_q[0])
-        quantise(round_wx(1), wx_q[1])
+        quantise(round_wx(1, "wx_b1"), wx_q[1])
         v_c.append(gather_v(0, "v_c0"))
-        w_s = order_scales("minus0")
+        quantise(x_b0, x_q[0])
+        v_c.append(gather_v(1, "wx_raw0"))
+        wr_raw = keep.tile([P, GROUPS, H], I32, name="tab_w0", align_bytes=64)
+        nc.sync.dma_start(wr_raw[:], wr_words.rearrange("a p n t -> p a (n t)").bitcast(I32))
+        plus1, minus1 = gather_x_apart(1, "tab_w1")
 
-        diff1 = gather_x(1, "w_s_raw")
-        wr_raw = load_wr("w_s_raw")
-
-        h_b0 = apply_gain(first_step(0, 0, None), 0, W)
-        th1 = first_step(0, 1, None)
-        x_b1 = round_x(diff1, "th0_0")
+        h_b0 = gain_on_gpsimd(first_step(0, 0, None), 0)
+        h_b1 = apply_gain(first_step(0, 1, None), 1, W)
+        quantise(subtract_x(plus1, minus1, "diff"), x_q[1])
         quantise(h_b0, h_q[0][0])
-        quantise(x_b1, x_q[1])
-
-        v_c.append(gather_v(1, "th0_0"))
-        wr_c = order_wr(wr_raw, "diff")
-        quantise(apply_gain(th1, 1, GAIN_ON_SCALAR), h_q[0][1])
+        wr_c = order_wr(wr_raw, "tab_w1")
+        wr_s = order_scales(wr_s_raw[:], H, "diff")
+        quantise(h_b1, h_q[0][1])
 
         b_second = keep_b(1)
         ths = [first_step(1, g, b_second) for g in range(GROUPS)]

@@ -25,8 +25,6 @@ HALVES = S // W
 GROUPS = H // (P * PACK)
 PASSES = K // (P * PACK)
 BANKS = 8
-SUMS_IN_FLIGHT = 6
-STORES_IN_FLIGHT = 8
 GAIN_ON_SCALAR = W // 4
 
 
@@ -43,13 +41,12 @@ def tile_list_snowpack_recurrence_kernel(tc, tab_words, tab_scales, offs, xT, of
         list_3 = keep.tile([P, S // STRIPE], U16, name="list_3")
 
         tab_s = keep.tile([P, T // 4], I32, name="tab_s", align_bytes=64)
-        wp_s_raw = keep.tile([P, PASSES, H // 4], I32, name="wp_s_raw", align_bytes=64)
-        wr_s_raw = keep.tile([P, H // 4], I32, name="wr_s_raw", align_bytes=64)
-        v_s1 = keep.tile([P, S // 4], I32, name="v_s1", align_bytes=64)
-        nc.gpsimd.memset(tab_s[:], 0)
-        nc.vector.memset(wp_s_raw[:], 0)
-        nc.vector.memset(wr_s_raw[:], 0)
-        nc.vector.memset(v_s1[:], 0)
+        w_s_raw = keep.tile([P, PASSES, H // 4], I32, name="w_s_raw", align_bytes=64)
+        v_s = keep.tile([P, PASSES, S // 4], I32, name="v_s", align_bytes=64)
+        nc.gpsimd.memset(tab_s[32:64, :], 0)
+        nc.gpsimd.memset(tab_s[64:P, :], 0)
+        nc.vector.memset(w_s_raw[:], 0)
+        nc.vector.memset(v_s[:], 0)
 
         wp_raw = keep.tile([P, PASSES, H // 2], I32, name="wp_raw", align_bytes=64)
         planes = [keep.tile([P, T], F32, name="plane%d" % t, align_bytes=64) for t in range(PACK)]
@@ -58,30 +55,33 @@ def tile_list_snowpack_recurrence_kernel(tc, tab_words, tab_scales, offs, xT, of
         gain_sb = keep.tile([P, GROUPS, PACK], F32, name="gain_sb")
         x_rows = xT.rearrange("(p t) n -> t p n", t=PACK)
         wx_rows = wx.rearrange("(p j) c -> p j c", j=PACK)
+
+        def load_weight_scales(scales, first_row):
+            for q in range(QUADRANTS):
+                row = 32 * q + first_row
+                nc.sync.dma_start(w_s_raw[row:row + 4, :, :],
+                                  scales[:, 4 * q:4 * q + 4, :].rearrange("a r n -> r a n").bitcast(I32))
+
         nc.sync.dma_start(list_v[:], offs)
+        nc.sync.dma_start(tab_s[0:32, :], tab_scales.rearrange("a q n -> (a q) n").bitcast(I32))
         nc.sync.dma_start(list_3[:], offs3)
         nc.sync.dma_start(list_2[:], offs2)
         nc.sync.dma_start(wp_raw[:], wp_words.rearrange("a p n -> p a n").bitcast(I32))
-        nc.sync.dma_start(planes[0][:], x_rows[0])
-        for q in range(QUADRANTS):
-            nc.sync.dma_start(tab_s[32 * q:32 * q + 8, :], tab_scales[:, 4 * q:4 * q + 4, :].bitcast(I32))
-        v_s0 = keep.tile([P, S], U8, name="v_s0", align_bytes=64)
-        nc.vector.tensor_copy(v_s0[:], tab_s[:].bitcast(U8).indirect(list_v[:]))
-        for q in range(QUADRANTS):
-            nc.gpsimd.dma_start(v_s1[32 * q:32 * q + 4, :], v_s0[32 * q + 4:32 * q + 8, :].bitcast(I32))
-        nc.sync.dma_start(planes[1][:], x_rows[1])
-        nc.sync.dma_start(planes[2][:], x_rows[2])
-        nc.sync.dma_start(planes[3][:], x_rows[3])
+        v_s_rows = keep.tile([P, S], U8, name="v_s_rows", align_bytes=64)
+        nc.vector.tensor_copy(v_s_rows[:], tab_s[:].bitcast(U8).indirect(list_v[:]))
+        for a in range(PASSES):
+            for q in range(QUADRANTS):
+                row = 16 * a + 4 * q
+                nc.gpsimd.dma_start(v_s[32 * q:32 * q + 4, a, :], v_s_rows[row:row + 4, :].bitcast(I32))
+        for t in range(PACK):
+            nc.sync.dma_start(planes[t][:], x_rows[t])
+        load_weight_scales(wp_scales, 0)
         nc.sync.dma_start(wx_raw[0][:], wx_rows[:, :, 0:W])
-        for q in range(QUADRANTS):
-            nc.sync.dma_start(wp_s_raw[32 * q:32 * q + 4, :, :],
-                              wp_scales[:, 4 * q:4 * q + 4, :].rearrange("a r n -> r a n").bitcast(I32))
-        nc.sync.dma_start(wx_raw[1][:], wx_rows[:, :, W:2 * W])
+        load_weight_scales(wr_scales, 4)
         for a in range(PASSES):
             nc.sync.dma_start(tab_w[a][:], tab_words[a].rearrange("p n t -> p (n t)").bitcast(I32))
+        nc.sync.dma_start(wx_raw[1][:], wx_rows[:, :, W:2 * W])
         nc.sync.dma_start(gain_sb[:], gain.rearrange("(g p t) -> p g t", g=GROUPS, t=PACK))
-        for q in range(QUADRANTS):
-            nc.sync.dma_start(wr_s_raw[32 * q:32 * q + 8, :], wr_scales[:, 4 * q:4 * q + 4, :].bitcast(I32))
 
         wp_c = keep.tile([P, PASSES, 2 * H], U8, name="wp_c", align_bytes=64)
         nc.vector.tensor_copy(
@@ -96,9 +96,9 @@ def tile_list_snowpack_recurrence_kernel(tc, tab_words, tab_scales, offs, xT, of
 
         def order_wr(raw, place):
             ordered = keep.tile([P, GROUPS, H], I32, name=place, align_bytes=64)
-            nc.vector.tensor_copy(
-                ordered[:].rearrange("p a (g t m) -> p (a g) m t", g=GROUPS, t=PACK),
-                raw[:].rearrange("p a (g m t) -> p (a g) m t", g=GROUPS, t=PACK))
+            nc.gpsimd.tensor_copy(
+                ordered[:].rearrange("p a (g t m) -> p (a g) t m", g=GROUPS, t=PACK),
+                raw[:].rearrange("p a (g m t) -> p (a g) t m", g=GROUPS, t=PACK))
             return ordered
 
         def round_wx(g, place):
@@ -129,12 +129,11 @@ def tile_list_snowpack_recurrence_kernel(tc, tab_words, tab_scales, offs, xT, of
                                             minus[:, t - 1, :], ALU.subtract)
             return diff
 
-        def gather_x_apart(half, place):
-            both = keep.tile([P, 2, PACK, W], F32, name=place, align_bytes=64)
+        def gather_planes(list_tile, half, place):
+            picked = keep.tile([P, PACK, W], F32, name=place, align_bytes=64)
             for t in range(PACK):
-                nc.vector.tensor_copy(both[:, 0, t, :], planes[t][:].indirect(entries(list_3, half)))
-                nc.vector.tensor_copy(both[:, 1, t, :], planes[t][:].indirect(entries(list_2, half)))
-            return both[:, 1, :, :], both[:, 0, :, :]
+                nc.vector.tensor_copy(picked[:, t, :], planes[t][:].indirect(entries(list_tile, half)))
+            return picked[:]
 
         def subtract_x(plus, minus, place):
             rounded = keep.tile([P, W * PACK], BF16, name=place, align_bytes=64)
@@ -149,10 +148,9 @@ def tile_list_snowpack_recurrence_kernel(tc, tab_words, tab_scales, offs, xT, of
                            diff[:].rearrange("p t (c i) -> p c t i", i=2))
             return rounded[:]
 
-        def gather_v(half, place):
-            words = keep.tile([P, PASSES, W], U32, name=place, align_bytes=64)
-            for a in range(PASSES):
-                nc.vector.tensor_copy(words[:, a, :], tab_w[a][:].bitcast(U32).indirect(entries(list_v, half)))
+        def gather_v(a, offsets, place):
+            words = keep.tile([P, offsets.shape[1] * STRIPE], U32, name=place, align_bytes=64)
+            nc.vector.tensor_copy(words[:], tab_w[a][:].bitcast(U32).indirect(offsets))
             return words
 
         def new_bank():
@@ -167,52 +165,51 @@ def tile_list_snowpack_recurrence_kernel(tc, tab_words, tab_scales, offs, xT, of
 
         def passes_wp(bank, half, g, t, start):
             c0 = (g * PACK + t) * P
-            v_s = [v_s0[:], v_s1[:].bitcast(U8)]
-            for a in range(PASSES):
+            for a in reversed(range(PASSES)):
                 nc.tensor.matmul_mx(bank[:], lhsT=wp_c[:, a, 2 * c0:2 * (c0 + P)].bitcast(FP4X4),
-                                    lhsT_scale=wp_s[:, a * H + c0:a * H + c0 + P],
-                                    rhs=v_c[half][:, a, :].bitcast(FP8X4),
-                                    rhs_scale=v_s[a][:, half * W:(half + 1) * W],
-                                    start=(start and a == 0), stop=(a == PASSES - 1))
+                                    lhsT_scale=w_s[:, a * H + c0:a * H + c0 + P],
+                                    rhs=v_c[half][a].bitcast(FP8X4),
+                                    rhs_scale=v_s[:, a, :].bitcast(U8)[:, half * W:(half + 1) * W],
+                                    start=(start and a == PASSES - 1), stop=(a == 0))
 
         def passes_wr(bank, half, g, t, start):
             c0 = (g * PACK + t) * P
             for a in range(GROUPS):
                 h_codes, h_scales = h_q[half][a]
                 nc.tensor.matmul_mx(bank[:], lhsT=wr_c[:, a, c0:c0 + P].bitcast(FP8X4),
-                                    lhsT_scale=wr_s[4 * a:P, c0:c0 + P],
+                                    lhsT_scale=w_s[4:P, a * H + c0:a * H + c0 + P],
                                     rhs=h_codes[:].bitcast(FP8X4), rhs_scale=h_scales[:],
                                     start=(start and a == 0), stop=(a == GROUPS - 1))
 
-        def keep_b(half):
-            kept = []
-            for g in range(GROUPS):
-                kept.append(keep.tile([P, PACK, W], F32, name="b_kept%d" % g, align_bytes=64))
-                for t in range(PACK):
-                    bank = new_bank()
-                    pass_b(bank, half, g, t, True)
-                    nc.scalar.copy(kept[g][:, t, :], bank[:])
+        def keep_b(half, g):
+            kept = keep.tile([P, PACK, W], F32, name="b_kept%d" % g, align_bytes=64)
+            for t in range(PACK):
+                bank = new_bank()
+                pass_b(bank, half, g, t, True)
+                nc.scalar.copy(kept[:, t, :], bank[:])
             return kept
 
-        def product_plus_b(passes, half, g, t, b_kept):
+        def product_plus_b(passes, half, g, t, b_kept, total):
             bank = new_bank()
             if b_kept is None:
                 pass_b(bank, half, g, t, False)
                 passes(bank, half, g, t, False)
-                return bank
+                return bank[:]
             passes(bank, half, g, t, True)
-            total = ring.tile([P, W], F32, name="total", bufs=SUMS_IN_FLIGHT, align_bytes=64)
-            nc.vector.tensor_tensor(total[:], bank[:], b_kept[g][:, t, :], ALU.add)
-            return total
+            nc.vector.tensor_tensor(total[:, t, :], bank[:], b_kept[g][:, t, :], ALU.add)
+            return total[:, t, :]
 
-        def first_step(half, g, b_kept):
-            th = keep.tile([P, PACK, W], F32, name="th%d" % g, align_bytes=64)
+        def group_tile(place):
+            return keep.tile([P, PACK, W], F32, name=place, align_bytes=64)
+
+        def first_step(half, g, b_kept, total, place):
+            th = group_tile(place)
             for t in range(PACK):
-                nc.scalar.activation(th[:, t, :], product_plus_b(passes_wp, half, g, t, b_kept)[:], ACT.Tanh)
+                nc.scalar.activation(th[:, t, :], product_plus_b(passes_wp, half, g, t, b_kept, total), ACT.Tanh)
             return th
 
-        def apply_gain(th, g, on_scalar):
-            rounded = keep.tile([P, W, PACK], BF16, name="h_b%d" % g, align_bytes=64)
+        def apply_gain(th, g, on_scalar, place):
+            rounded = keep.tile([P, W, PACK], BF16, name=place, align_bytes=64)
             if on_scalar > 0:
                 by_tile = ring.tile([P, PACK, on_scalar], BF16, name="h_by_tile", align_bytes=64)
                 for t in range(PACK):
@@ -228,20 +225,65 @@ def tile_list_snowpack_recurrence_kernel(tc, tab_words, tab_scales, offs, xT, of
                                         ALU.mult)
             return rounded[:].rearrange("p j t -> p (j t)")
 
-        def gain_on_gpsimd(th, g):
-            rounded = keep.tile([P, W, PACK], BF16, name="h_b%d" % g, align_bytes=64)
-            nc.gpsimd.tensor_tensor(rounded[:], th[:].rearrange("p t c -> p c t"),
-                                    gain_sb[:, g, :].unsqueeze(1).to_broadcast([P, W, PACK]), ALU.mult)
+        def gain_beside_gathers(th, g, on_gpsimd, place):
+            rounded = keep.tile([P, W, PACK], BF16, name=place, align_bytes=64)
+            nc.gpsimd.tensor_tensor(rounded[:, 0:on_gpsimd, :], th[:, :, 0:on_gpsimd].rearrange("p t c -> p c t"),
+                                    gain_sb[:, g, :].unsqueeze(1).to_broadcast([P, on_gpsimd, PACK]), ALU.mult)
+            if on_gpsimd < W:
+                by_tile = keep.tile([P, PACK, W - on_gpsimd], BF16, name="h_by_tile", align_bytes=64)
+                for t in range(PACK):
+                    nc.scalar.activation(by_tile[:, t, :], th[:, t, on_gpsimd:W], ACT.Copy,
+                                         scale=gain_sb[:, g, t:t + 1])
+                nc.scalar.copy(rounded[:, on_gpsimd:W, :].rearrange("p (c i) t -> p c t i", i=4),
+                               by_tile[:].rearrange("p t (c i) -> p c t i", i=4))
             return rounded[:].rearrange("p j t -> p (j t)")
 
-        def second_step(half, b_kept):
+        def second_step(half, g, b_kept, total, place):
             out_rows = out.rearrange("(g p t) j -> g t p j", g=GROUPS, t=PACK)
-            for g in range(GROUPS):
-                for t in range(PACK):
-                    total = product_plus_b(passes_wr, half, g, t, b_kept)
-                    result = ring.tile([P, W], F32, name="result", bufs=STORES_IN_FLIGHT, align_bytes=64)
-                    nc.scalar.activation(result[:], total[:], ACT.Tanh)
-                    nc.sync.dma_start(out_rows[g, t][:, half * W:(half + 1) * W], result[:])
+            result = group_tile(place)
+            for t in range(PACK):
+                nc.scalar.activation(result[:, t, :], product_plus_b(passes_wr, half, g, t, b_kept, total), ACT.Tanh)
+                nc.sync.dma_start(out_rows[g, t][:, half * W:(half + 1) * W], result[:, t, :])
+
+        def last_step(b_kept, ths):
+            run = W // 2
+            out_rows = out.rearrange("(g p t) j -> g p t j", g=GROUPS, t=PACK)
+            first = apply_gain(ths[0], 0, 0, "h_b0")
+            rounded = keep.tile([P, W, PACK], BF16, name="h_b1", align_bytes=64)
+            codes, scales = h_q[1][1]
+            for r in range(2):
+                cols = slice(r * run, (r + 1) * run)
+                nc.vector.tensor_tensor(rounded[:, cols, :].rearrange("p (c i) t -> p c t i", i=2),
+                                        ths[1][:, :, cols].rearrange("p t (c i) -> p c t i", i=2),
+                                        gain_sb[:, 1, :].unsqueeze(1).unsqueeze(3).to_broadcast([P, run // 2, PACK, 2]),
+                                        ALU.mult)
+                if r == 0:
+                    quantise(first, h_q[1][0])
+                nc.vector.quantize_mx(out=codes[:, cols].bitcast(FP8X4), scales=scales[:, cols],
+                                      in_=rounded[:, cols, :].rearrange("p j t -> p (j t)"))
+            totals = [group_tile("sum0"), group_tile("plane2")]
+            results = [group_tile("plane1"), group_tile("plane3")]
+            for r in range(2):
+                cols = slice(r * run, (r + 1) * run)
+                for g in range(GROUPS):
+                    for t0 in range(0, PACK, 2):
+                        bank = new_bank()
+                        for t in range(t0, t0 + 2):
+                            c0 = (g * PACK + t) * P
+                            for a in range(GROUPS):
+                                h_codes, h_scales = h_q[1][a]
+                                nc.tensor.matmul_mx(bank[:, (t - t0) * run:(t - t0 + 1) * run],
+                                                    lhsT=wr_c[:, a, c0:c0 + P].bitcast(FP8X4),
+                                                    lhsT_scale=w_s[4:P, a * H + c0:a * H + c0 + P],
+                                                    rhs=h_codes[:, cols].bitcast(FP8X4), rhs_scale=h_scales[:, cols],
+                                                    start=(a == 0), stop=(a == GROUPS - 1))
+                        k = 2 * g + t0 // 2
+                        total = totals[r][:, k, :].rearrange("p (t j) -> p t j", t=2)
+                        nc.vector.tensor_tensor(total, bank[:].rearrange("p (t j) -> p t j", t=2),
+                                                b_kept[g][:, t0:t0 + 2, cols], ALU.add)
+                        nc.scalar.activation(results[r][:, k, :], totals[r][:, k, :], ACT.Tanh)
+                        nc.sync.dma_start(out_rows[g][:, t0:t0 + 2, W + r * run:W + (r + 1) * run],
+                                          results[r][:, k, :].rearrange("p (t j) -> p t j", t=2))
 
         wx_q = [mx_tiles("wx%d" % g) for g in range(GROUPS)]
         x_q = [mx_tiles("x%d" % half) for half in range(HALVES)]
@@ -250,29 +292,32 @@ def tile_list_snowpack_recurrence_kernel(tc, tab_words, tab_scales, offs, xT, of
 
         wx_b0 = round_wx(0, "wx_b0")
         diff0 = gather_x(0, "minus0")
-        x_b0 = round_x(diff0, "wx_raw0")
-        wp_s = order_scales(wp_s_raw[:].rearrange("p a n -> p (a n)"), PASSES * H, "wp_s")
+        w_s = order_scales(w_s_raw[:].rearrange("p a n -> p (a n)"), PASSES * H, "w_s")
+        v_00 = gather_v(0, entries(list_v, 0), "v_00")
         quantise(wx_b0, wx_q[0])
-        quantise(round_wx(1, "wx_b1"), wx_q[1])
-        v_c.append(gather_v(0, "v_c0"))
-        quantise(x_b0, x_q[0])
-        v_c.append(gather_v(1, "wx_raw0"))
-        wr_raw = keep.tile([P, GROUPS, H], I32, name="tab_w0", align_bytes=64)
+        v_1 = gather_v(1, list_v[:], "v_1")
+        v_c.append([v_00[:], v_1[:, 0:W]])
+        quantise(round_x(diff0, "wx_raw0"), x_q[0])
+        wr_raw = keep.tile([P, GROUPS, H], I32, name="diff", align_bytes=64)
         nc.sync.dma_start(wr_raw[:], wr_words.rearrange("a p n t -> p a (n t)").bitcast(I32))
-        plus1, minus1 = gather_x_apart(1, "tab_w1")
+        wr_c = order_wr(wr_raw, "minus0")
+        minus1 = gather_planes(list_3, 1, "tab_w1")
+        quantise(round_wx(1, "wx_b1"), wx_q[1])
+        plus1 = gather_planes(list_2, 1, "wx_b1")
 
-        h_b0 = gain_on_gpsimd(first_step(0, 0, None), 0)
-        h_b1 = apply_gain(first_step(0, 1, None), 1, W)
+        th_first = [first_step(0, g, None, None, "th_first%d" % g) for g in range(GROUPS)]
+        h_b0 = gain_beside_gathers(th_first[0], 0, 3 * W // 4, "h_first")
         quantise(subtract_x(plus1, minus1, "diff"), x_q[1])
-        quantise(h_b0, h_q[0][0])
-        wr_c = order_wr(wr_raw, "tab_w1")
-        wr_s = order_scales(wr_s_raw[:], H, "diff")
-        quantise(h_b1, h_q[0][1])
+        v_c.append([gather_v(0, entries(list_v, 1), "wx_b1")[:], v_1[:, W:2 * W]])
+        h_b1 = gain_beside_gathers(th_first[1], 1, W, "diff")
 
-        b_second = keep_b(1)
-        ths = [first_step(1, g, b_second) for g in range(GROUPS)]
-        second_step(0, None)
-        h_bs = [apply_gain(ths[g], g, 0) for g in range(GROUPS)]
+        b_second, ths = [], []
         for g in range(GROUPS):
-            quantise(h_bs[g], h_q[1][g])
-        second_step(1, b_second)
+            b_second.append(keep_b(1, g))
+            ths.append(first_step(1, g, b_second, group_tile("sum%d" % g), "plane%d" % g))
+        h_q[0][0] = (keep.tile([P, W], U32, name="th_first1", align_bytes=64), h_q[0][0][1])
+        quantise(h_b0, h_q[0][0])
+        quantise(h_b1, h_q[0][1])
+        second_step(0, 0, None, None, "sum1")
+        second_step(0, 1, None, None, "th_first0")
+        last_step(b_second, ths)

@@ -96,9 +96,9 @@ def tile_list_snowpack_recurrence_kernel(tc, tab_words, tab_scales, offs, xT, of
 
         def order_wr(raw, place):
             ordered = keep.tile([P, GROUPS, H], I32, name=place, align_bytes=64)
-            nc.gpsimd.tensor_copy(
-                ordered[:].rearrange("p a (g t m) -> p (a g) t m", g=GROUPS, t=PACK),
-                raw[:].rearrange("p a (g m t) -> p (a g) t m", g=GROUPS, t=PACK))
+            nc.vector.tensor_copy(
+                ordered[:].rearrange("p a (g t m) -> p (a g) m t", g=GROUPS, t=PACK),
+                raw[:].rearrange("p a (g m t) -> p (a g) m t", g=GROUPS, t=PACK))
             return ordered
 
         def round_wx(g, place):
@@ -300,14 +300,14 @@ def tile_list_snowpack_recurrence_kernel(tc, tab_words, tab_scales, offs, xT, of
         quantise(round_x(diff0, "wx_raw0"), x_q[0])
         wr_raw = keep.tile([P, GROUPS, H], I32, name="diff", align_bytes=64)
         nc.sync.dma_start(wr_raw[:], wr_words.rearrange("a p n t -> p a (n t)").bitcast(I32))
-        wr_c = order_wr(wr_raw, "minus0")
         minus1 = gather_planes(list_3, 1, "tab_w1")
         quantise(round_wx(1, "wx_b1"), wx_q[1])
         plus1 = gather_planes(list_2, 1, "wx_b1")
 
         th_first = [first_step(0, g, None, None, "th_first%d" % g) for g in range(GROUPS)]
         h_b0 = gain_beside_gathers(th_first[0], 0, 3 * W // 4, "h_first")
-        quantise(subtract_x(plus1, minus1, "diff"), x_q[1])
+        quantise(subtract_x(plus1, minus1, "minus0"), x_q[1])
+        wr_c = order_wr(wr_raw, "tab_w1")
         v_c.append([gather_v(0, entries(list_v, 1), "wx_b1")[:], v_1[:, W:2 * W]])
         h_b1 = gain_beside_gathers(th_first[1], 1, W, "diff")
 

@@ -56,11 +56,17 @@ def tile_list_snowpack_recurrence_kernel(tc, tab_words, tab_scales, offs, xT, of
         x_rows = xT.rearrange("(p t) n -> t p n", t=PACK)
         wx_rows = wx.rearrange("(p j) c -> p j c", j=PACK)
 
-        def load_weight_scales(scales, first_row):
-            for q in range(QUADRANTS):
-                row = 32 * q + first_row
-                nc.sync.dma_start(w_s_raw[row:row + 4, :, :],
-                                  scales[:, 4 * q:4 * q + 4, :].rearrange("a r n -> r a n").bitcast(I32))
+        def load_weight_scales(scales, first_row, q):
+            row = 32 * q + first_row
+            nc.sync.dma_start(w_s_raw[row:row + 4, :, :],
+                              scales[:, 4 * q:4 * q + 4, :].rearrange("a r n -> r a n").bitcast(I32))
+
+        def move_v_scales(queue, a, q):
+            row = 16 * a + 4 * q
+            queue.dma_start(v_s[32 * q:32 * q + 4, a, :], v_s_rows[row:row + 4, :].bitcast(I32))
+
+        def load_table(a):
+            nc.sync.dma_start(tab_w[a][:], tab_words[a].rearrange("p n t -> p (n t)").bitcast(I32))
 
         nc.sync.dma_start(list_v[:], offs)
         nc.sync.dma_start(tab_s[0:32, :], tab_scales.rearrange("a q n -> (a q) n").bitcast(I32))
@@ -69,17 +75,25 @@ def tile_list_snowpack_recurrence_kernel(tc, tab_words, tab_scales, offs, xT, of
         nc.sync.dma_start(wp_raw[:], wp_words.rearrange("a p n -> p a n").bitcast(I32))
         v_s_rows = keep.tile([P, S], U8, name="v_s_rows", align_bytes=64)
         nc.vector.tensor_copy(v_s_rows[:], tab_s[:].bitcast(U8).indirect(list_v[:]))
-        for a in range(PASSES):
-            for q in range(QUADRANTS):
-                row = 16 * a + 4 * q
-                nc.gpsimd.dma_start(v_s[32 * q:32 * q + 4, a, :], v_s_rows[row:row + 4, :].bitcast(I32))
-        for t in range(PACK):
-            nc.sync.dma_start(planes[t][:], x_rows[t])
-        load_weight_scales(wp_scales, 0)
+        nc.sync.dma_start(planes[0][:], x_rows[0])
+        nc.sync.dma_start(planes[1][:], x_rows[1])
+        for q in range(3):
+            load_weight_scales(wp_scales, 0, q)
+        nc.sync.dma_start(planes[2][:], x_rows[2])
+        load_weight_scales(wp_scales, 0, 3)
+        load_weight_scales(wr_scales, 4, 0)
+        load_weight_scales(wr_scales, 4, 1)
+        nc.sync.dma_start(planes[3][:], x_rows[3])
+        load_weight_scales(wr_scales, 4, 2)
+        load_weight_scales(wr_scales, 4, 3)
+        move_v_scales(nc.sync, 0, 0)
         nc.sync.dma_start(wx_raw[0][:], wx_rows[:, :, 0:W])
-        load_weight_scales(wr_scales, 4)
+        for q in range(1, QUADRANTS):
+            move_v_scales(nc.sync, 0, q)
+        for q in range(QUADRANTS):
+            move_v_scales(nc.gpsimd, 1, q)
         for a in range(PASSES):
-            nc.sync.dma_start(tab_w[a][:], tab_words[a].rearrange("p n t -> p (n t)").bitcast(I32))
+            load_table(a)
         nc.sync.dma_start(wx_raw[1][:], wx_rows[:, :, W:2 * W])
         nc.sync.dma_start(gain_sb[:], gain.rearrange("(g p t) -> p g t", g=GROUPS, t=PACK))
 
@@ -156,56 +170,58 @@ def tile_list_snowpack_recurrence_kernel(tc, tab_words, tab_scales, offs, xT, of
         def new_bank():
             return psum.tile([P, W], F32, name="bank", bufs=BANKS)
 
-        def pass_b(bank, half, g, t, stop):
+        def pass_b(bank, half, g, t, start, stop):
             cols = slice(t * P, (t + 1) * P)
             wx_codes, wx_scales = wx_q[g]
             x_codes, x_scales = x_q[half]
             nc.tensor.matmul_mx(bank[:], lhsT=wx_codes[:, cols].bitcast(FP8X4), lhsT_scale=wx_scales[:, cols],
-                                rhs=x_codes[:].bitcast(FP8X4), rhs_scale=x_scales[:], start=True, stop=stop)
+                                rhs=x_codes[:].bitcast(FP8X4), rhs_scale=x_scales[:], start=start, stop=stop)
 
-        def passes_wp(bank, half, g, t, start):
+        def pass_wp(bank, half, g, t, a, start, stop):
             c0 = (g * PACK + t) * P
-            for a in reversed(range(PASSES)):
-                nc.tensor.matmul_mx(bank[:], lhsT=wp_c[:, a, 2 * c0:2 * (c0 + P)].bitcast(FP4X4),
-                                    lhsT_scale=w_s[:, a * H + c0:a * H + c0 + P],
-                                    rhs=v_c[half][a].bitcast(FP8X4),
-                                    rhs_scale=v_s[:, a, :].bitcast(U8)[:, half * W:(half + 1) * W],
-                                    start=(start and a == PASSES - 1), stop=(a == 0))
+            nc.tensor.matmul_mx(bank[:], lhsT=wp_c[:, a, 2 * c0:2 * (c0 + P)].bitcast(FP4X4),
+                                lhsT_scale=w_s[:, a * H + c0:a * H + c0 + P],
+                                rhs=v_c[half][a].bitcast(FP8X4),
+                                rhs_scale=v_s[:, a, :].bitcast(U8)[:, half * W:(half + 1) * W],
+                                start=start, stop=stop)
 
-        def passes_wr(bank, half, g, t, start):
+        def pass_wr(bank, half, g, t, a, start, stop):
             c0 = (g * PACK + t) * P
-            for a in range(GROUPS):
-                h_codes, h_scales = h_q[half][a]
-                nc.tensor.matmul_mx(bank[:], lhsT=wr_c[:, a, c0:c0 + P].bitcast(FP8X4),
-                                    lhsT_scale=w_s[4:P, a * H + c0:a * H + c0 + P],
-                                    rhs=h_codes[:].bitcast(FP8X4), rhs_scale=h_scales[:],
-                                    start=(start and a == 0), stop=(a == GROUPS - 1))
+            h_codes, h_scales = h_q[half][a]
+            nc.tensor.matmul_mx(bank[:], lhsT=wr_c[:, a, c0:c0 + P].bitcast(FP8X4),
+                                lhsT_scale=w_s[4:P, a * H + c0:a * H + c0 + P],
+                                rhs=h_codes[:].bitcast(FP8X4), rhs_scale=h_scales[:], start=start, stop=stop)
 
-        def keep_b(half, g):
+        def keep_b(half, g, on_scalar):
             kept = keep.tile([P, PACK, W], F32, name="b_kept%d" % g, align_bytes=64)
             for t in range(PACK):
                 bank = new_bank()
-                pass_b(bank, half, g, t, True)
-                nc.scalar.copy(kept[:, t, :], bank[:])
+                pass_b(bank, half, g, t, True, True)
+                if t < on_scalar:
+                    nc.scalar.copy(kept[:, t, :], bank[:])
+                else:
+                    nc.vector.tensor_copy(kept[:, t, :], bank[:])
             return kept
 
-        def product_plus_b(passes, half, g, t, b_kept, total):
+        def product_plus_b(product, order, half, g, t, b_kept, total):
             bank = new_bank()
+            for i, a in enumerate(order):
+                if a is None:
+                    pass_b(bank, half, g, t, i == 0, i == len(order) - 1)
+                else:
+                    product(bank, half, g, t, a, i == 0, i == len(order) - 1)
             if b_kept is None:
-                pass_b(bank, half, g, t, False)
-                passes(bank, half, g, t, False)
                 return bank[:]
-            passes(bank, half, g, t, True)
             nc.vector.tensor_tensor(total[:, t, :], bank[:], b_kept[g][:, t, :], ALU.add)
             return total[:, t, :]
 
         def group_tile(place):
             return keep.tile([P, PACK, W], F32, name=place, align_bytes=64)
 
-        def first_step(half, g, b_kept, total, place):
+        def first_step(half, g, order, b_kept, total, place):
             th = group_tile(place)
             for t in range(PACK):
-                nc.scalar.activation(th[:, t, :], product_plus_b(passes_wp, half, g, t, b_kept, total), ACT.Tanh)
+                nc.scalar.activation(th[:, t, :], product_plus_b(pass_wp, order, half, g, t, b_kept, total), ACT.Tanh)
             return th
 
         def apply_gain(th, g, on_scalar, place):
@@ -225,43 +241,41 @@ def tile_list_snowpack_recurrence_kernel(tc, tab_words, tab_scales, offs, xT, of
                                         ALU.mult)
             return rounded[:].rearrange("p j t -> p (j t)")
 
-        def gain_beside_gathers(th, g, on_gpsimd, place):
-            rounded = keep.tile([P, W, PACK], BF16, name=place, align_bytes=64)
-            nc.gpsimd.tensor_tensor(rounded[:, 0:on_gpsimd, :], th[:, :, 0:on_gpsimd].rearrange("p t c -> p c t"),
-                                    gain_sb[:, g, :].unsqueeze(1).to_broadcast([P, on_gpsimd, PACK]), ALU.mult)
-            if on_gpsimd < W:
-                by_tile = keep.tile([P, PACK, W - on_gpsimd], BF16, name="h_by_tile", align_bytes=64)
-                for t in range(PACK):
-                    nc.scalar.activation(by_tile[:, t, :], th[:, t, on_gpsimd:W], ACT.Copy,
-                                         scale=gain_sb[:, g, t:t + 1])
-                nc.scalar.copy(rounded[:, on_gpsimd:W, :].rearrange("p (c i) t -> p c t i", i=4),
-                               by_tile[:].rearrange("p t (c i) -> p c t i", i=4))
-            return rounded[:].rearrange("p j t -> p (j t)")
+        def gain_on_gpsimd(th, g, rounded, cols):
+            count = cols.stop - cols.start
+            nc.gpsimd.tensor_tensor(rounded, th[:, :, cols].rearrange("p t c -> p c t"),
+                                    gain_sb[:, g, :].unsqueeze(1).to_broadcast([P, count, PACK]), ALU.mult)
+
+        def h_tile(place):
+            return keep.tile([P, W, PACK], BF16, name=place, align_bytes=64)
 
         def second_step(half, g, b_kept, total, place):
             out_rows = out.rearrange("(g p t) j -> g t p j", g=GROUPS, t=PACK)
             result = group_tile(place)
             for t in range(PACK):
-                nc.scalar.activation(result[:, t, :], product_plus_b(passes_wr, half, g, t, b_kept, total), ACT.Tanh)
+                nc.scalar.activation(result[:, t, :], product_plus_b(pass_wr, (None, 0, 1), half, g, t, b_kept, total), ACT.Tanh)
                 nc.sync.dma_start(out_rows[g, t][:, half * W:(half + 1) * W], result[:, t, :])
 
         def last_step(b_kept, ths):
             run = W // 2
             out_rows = out.rearrange("(g p t) j -> g p t j", g=GROUPS, t=PACK)
-            first = apply_gain(ths[0], 0, 0, "h_b0")
-            rounded = keep.tile([P, W, PACK], BF16, name="h_b1", align_bytes=64)
-            codes, scales = h_q[1][1]
-            for r in range(2):
-                cols = slice(r * run, (r + 1) * run)
-                nc.vector.tensor_tensor(rounded[:, cols, :].rearrange("p (c i) t -> p c t i", i=2),
-                                        ths[1][:, :, cols].rearrange("p t (c i) -> p c t i", i=2),
-                                        gain_sb[:, 1, :].unsqueeze(1).unsqueeze(3).to_broadcast([P, run // 2, PACK, 2]),
+            spans = [slice(r * run, (r + 1) * run) for r in range(2)]
+            rounded = [keep.tile([P, GROUPS, run, PACK], BF16, name=place, align_bytes=64)
+                       for place in ("plane2", "wx_raw1")]
+            h_runs = [mx_tiles("h_run%d" % r) for r in range(2)]
+
+            def gain_on_vector(g, r):
+                nc.vector.tensor_tensor(rounded[r][:, g, :, :].rearrange("p (c i) t -> p c t i", i=2),
+                                        ths[g][:, :, spans[r]].rearrange("p t (c i) -> p c t i", i=2),
+                                        gain_sb[:, g, :].unsqueeze(1).unsqueeze(3).to_broadcast([P, run // 2, PACK, 2]),
                                         ALU.mult)
-                if r == 0:
-                    quantise(first, h_q[1][0])
-                nc.vector.quantize_mx(out=codes[:, cols].bitcast(FP8X4), scales=scales[:, cols],
-                                      in_=rounded[:, cols, :].rearrange("p j t -> p (j t)"))
-            totals = [group_tile("sum0"), group_tile("plane2")]
+
+            gain_on_gpsimd(ths[0], 0, rounded[0][:, 0, :, :], spans[0])
+            gain_on_vector(0, 1)
+            for r in range(2):
+                gain_on_vector(1, r)
+                quantise(rounded[r][:].rearrange("p g j t -> p (g j t)"), h_runs[r])
+            totals = [group_tile("sum0"), group_tile("tab_w0")]
             results = [group_tile("plane1"), group_tile("plane3")]
             for r in range(2):
                 cols = slice(r * run, (r + 1) * run)
@@ -271,11 +285,12 @@ def tile_list_snowpack_recurrence_kernel(tc, tab_words, tab_scales, offs, xT, of
                         for t in range(t0, t0 + 2):
                             c0 = (g * PACK + t) * P
                             for a in range(GROUPS):
-                                h_codes, h_scales = h_q[1][a]
+                                h_codes, h_scales = h_runs[r]
+                                own = slice(a * run, (a + 1) * run)
                                 nc.tensor.matmul_mx(bank[:, (t - t0) * run:(t - t0 + 1) * run],
                                                     lhsT=wr_c[:, a, c0:c0 + P].bitcast(FP8X4),
                                                     lhsT_scale=w_s[4:P, a * H + c0:a * H + c0 + P],
-                                                    rhs=h_codes[:, cols].bitcast(FP8X4), rhs_scale=h_scales[:, cols],
+                                                    rhs=h_codes[:, own].bitcast(FP8X4), rhs_scale=h_scales[:, own],
                                                     start=(a == 0), stop=(a == GROUPS - 1))
                         k = 2 * g + t0 // 2
                         total = totals[r][:, k, :].rearrange("p (t j) -> p t j", t=2)
@@ -287,7 +302,7 @@ def tile_list_snowpack_recurrence_kernel(tc, tab_words, tab_scales, offs, xT, of
 
         wx_q = [mx_tiles("wx%d" % g) for g in range(GROUPS)]
         x_q = [mx_tiles("x%d" % half) for half in range(HALVES)]
-        h_q = [[mx_tiles("h%d_%d" % (half, g)) for g in range(GROUPS)] for half in range(HALVES)]
+        h_q = [[mx_tiles("h0_%d" % g) for g in range(GROUPS)]]
         v_c = []
 
         wx_b0 = round_wx(0, "wx_b0")
@@ -295,29 +310,40 @@ def tile_list_snowpack_recurrence_kernel(tc, tab_words, tab_scales, offs, xT, of
         w_s = order_scales(w_s_raw[:].rearrange("p a n -> p (a n)"), PASSES * H, "w_s")
         v_00 = gather_v(0, entries(list_v, 0), "v_00")
         quantise(wx_b0, wx_q[0])
-        v_1 = gather_v(1, list_v[:], "v_1")
-        v_c.append([v_00[:], v_1[:, 0:W]])
+        v_c.append([v_00[:], gather_v(1, entries(list_v, 0), "v_01")[:]])
         quantise(round_x(diff0, "wx_raw0"), x_q[0])
         wr_raw = keep.tile([P, GROUPS, H], I32, name="diff", align_bytes=64)
         nc.sync.dma_start(wr_raw[:], wr_words.rearrange("a p n t -> p a (n t)").bitcast(I32))
-        minus1 = gather_planes(list_3, 1, "tab_w1")
+        minus1 = gather_planes(list_3, 1, "wx_raw0")
         quantise(round_wx(1, "wx_b1"), wx_q[1])
-        plus1 = gather_planes(list_2, 1, "wx_b1")
+        diff1 = group_tile("wx_b1")
+        for t in range(PACK):
+            nc.vector.tensor_tensor(diff1[:, t, :], planes[t][:].indirect(entries(list_2, 1)), minus1[:, t, :],
+                                    ALU.subtract)
 
-        th_first = [first_step(0, g, None, None, "th_first%d" % g) for g in range(GROUPS)]
-        h_b0 = gain_beside_gathers(th_first[0], 0, 3 * W // 4, "h_first")
-        quantise(subtract_x(plus1, minus1, "minus0"), x_q[1])
-        wr_c = order_wr(wr_raw, "tab_w1")
-        v_c.append([gather_v(0, entries(list_v, 1), "wx_b1")[:], v_1[:, W:2 * W]])
-        h_b1 = gain_beside_gathers(th_first[1], 1, W, "diff")
+        th_first0 = first_step(0, 0, (0, 1, None), None, None, "wx_raw1")
+        by_tile = keep.tile([P, PACK, W], BF16, name="by_tile", align_bytes=64)
+        for t in range(PACK):
+            nc.scalar.activation(by_tile[:, t, :], th_first0[:, t, :], ACT.Copy, scale=gain_sb[:, 0, t:t + 1])
+        th_first1 = first_step(0, 1, (0, 1, None), None, None, "th_first1")
+        wr_c = order_wr(wr_raw, "wx_raw0")
+        h_b0 = h_tile("plane2")
+        nc.vector.tensor_copy(h_b0[:].rearrange("p (c i) t -> p c t i", i=4),
+                              by_tile[:].rearrange("p t (c i) -> p c t i", i=4))
+        quantise(round_x(diff1, "wx_raw1"), x_q[1])
+        h_q[0][0] = (keep.tile([P, W], U32, name="wx_b1", align_bytes=64), h_q[0][0][1])
+        quantise(h_b0[:].rearrange("p j t -> p (j t)"), h_q[0][0])
+        v_second = keep.tile([P, PASSES, W], U32, name="wx_raw1", align_bytes=64)
+        for a in range(PASSES):
+            nc.vector.tensor_copy(v_second[:, a, :], tab_w[a][:].bitcast(U32).indirect(entries(list_v, 1)))
+        v_c.append([v_second[:, a, :] for a in range(PASSES)])
+        h_b1 = h_tile("plane2")
+        gain_on_gpsimd(th_first1, 1, h_b1[:], slice(0, W))
 
-        b_second, ths = [], []
-        for g in range(GROUPS):
-            b_second.append(keep_b(1, g))
-            ths.append(first_step(1, g, b_second, group_tile("sum%d" % g), "plane%d" % g))
-        h_q[0][0] = (keep.tile([P, W], U32, name="th_first1", align_bytes=64), h_q[0][0][1])
-        quantise(h_b0, h_q[0][0])
-        quantise(h_b1, h_q[0][1])
-        second_step(0, 0, None, None, "sum1")
-        second_step(0, 1, None, None, "th_first0")
+        b_second = [keep_b(1, 0, PACK), keep_b(1, 1, PACK // 2)]
+        ths = [first_step(1, 0, (0, 1), b_second, group_tile("sum0"), "plane0")]
+        quantise(h_b1[:].rearrange("p j t -> p (j t)"), h_q[0][1])
+        ths.append(first_step(1, 1, (0, 1), b_second, group_tile("th_first1"), "plane1"))
+        second_step(0, 0, None, None, "th_first1")
+        second_step(0, 1, None, None, "plane0")
         last_step(b_second, ths)

@@ -43,8 +43,8 @@ def tile_list_snowpack_recurrence_kernel(tc, tab_words, tab_scales, offs, xT, of
         tab_s = keep.tile([P, T // 4], I32, name="tab_s", align_bytes=64)
         w_s_raw = keep.tile([P, PASSES, H // 4], I32, name="w_s_raw", align_bytes=64)
         v_s = keep.tile([P, PASSES, S // 4], I32, name="v_s", align_bytes=64)
-        nc.gpsimd.memset(tab_s[32:64, :], 0)
-        nc.gpsimd.memset(tab_s[64:P, :], 0)
+        nc.vector.memset(tab_s[32:64, :], 0)
+        nc.vector.memset(tab_s[64:P, :], 0)
         nc.vector.memset(w_s_raw[:], 0)
         nc.vector.memset(v_s[:], 0)
 
@@ -192,8 +192,8 @@ def tile_list_snowpack_recurrence_kernel(tc, tab_words, tab_scales, offs, xT, of
                                 lhsT_scale=w_s[4:P, a * H + c0:a * H + c0 + P],
                                 rhs=h_codes[:].bitcast(FP8X4), rhs_scale=h_scales[:], start=start, stop=stop)
 
-        def keep_b(half, g, on_scalar):
-            kept = keep.tile([P, PACK, W], F32, name="b_kept%d" % g, align_bytes=64)
+        def keep_b(half, g, on_scalar, place):
+            kept = keep.tile([P, PACK, W], F32, name=place, align_bytes=64)
             for t in range(PACK):
                 bank = new_bank()
                 pass_b(bank, half, g, t, True, True)
@@ -217,6 +217,20 @@ def tile_list_snowpack_recurrence_kernel(tc, tab_words, tab_scales, offs, xT, of
 
         def group_tile(place):
             return keep.tile([P, PACK, W], F32, name=place, align_bytes=64)
+
+        def table_passes(half, g, t):
+            bank = new_bank()
+            for a in range(PASSES):
+                pass_wp(bank, half, g, t, a, a == 0, a == PASSES - 1)
+            return bank
+
+        def add_and_tanh(banks, b_kept, total, place):
+            th = group_tile(place)
+            for t0 in range(0, PACK, 2):
+                for t in range(t0, t0 + 2):
+                    nc.vector.tensor_tensor(total[:, t, :], banks[t][:], b_kept[:, t, :], ALU.add)
+                nc.scalar.activation(th[:, t0:t0 + 2, :], total[:, t0:t0 + 2, :], ACT.Tanh)
+            return th
 
         def first_step(half, g, order, b_kept, total, place):
             th = group_tile(place)
@@ -249,11 +263,16 @@ def tile_list_snowpack_recurrence_kernel(tc, tab_words, tab_scales, offs, xT, of
         def h_tile(place):
             return keep.tile([P, W, PACK], BF16, name=place, align_bytes=64)
 
-        def second_step(half, g, b_kept, total, place):
+        def second_step(half, g, place):
             out_rows = out.rearrange("(g p t) j -> g t p j", g=GROUPS, t=PACK)
             result = group_tile(place)
+            banks = [new_bank() for t in range(PACK)]
             for t in range(PACK):
-                nc.scalar.activation(result[:, t, :], product_plus_b(pass_wr, (None, 0, 1), half, g, t, b_kept, total), ACT.Tanh)
+                pass_b(banks[t], half, g, t, True, False)
+                pass_wr(banks[t], half, g, t, 0, False, False)
+            for t in range(PACK):
+                pass_wr(banks[t], half, g, t, 1, False, True)
+                nc.scalar.activation(result[:, t, :], banks[t][:], ACT.Tanh)
                 nc.sync.dma_start(out_rows[g, t][:, half * W:(half + 1) * W], result[:, t, :])
 
         def last_step(b_kept, ths):
@@ -261,7 +280,7 @@ def tile_list_snowpack_recurrence_kernel(tc, tab_words, tab_scales, offs, xT, of
             out_rows = out.rearrange("(g p t) j -> g p t j", g=GROUPS, t=PACK)
             spans = [slice(r * run, (r + 1) * run) for r in range(2)]
             rounded = [keep.tile([P, GROUPS, run, PACK], BF16, name=place, align_bytes=64)
-                       for place in ("plane2", "wx_raw1")]
+                       for place in ("wx_raw1", "th_first1")]
             h_runs = [mx_tiles("h_run%d" % r) for r in range(2)]
 
             def gain_on_vector(g, r):
@@ -270,12 +289,12 @@ def tile_list_snowpack_recurrence_kernel(tc, tab_words, tab_scales, offs, xT, of
                                         gain_sb[:, g, :].unsqueeze(1).unsqueeze(3).to_broadcast([P, run // 2, PACK, 2]),
                                         ALU.mult)
 
-            gain_on_gpsimd(ths[0], 0, rounded[0][:, 0, :, :], spans[0])
+            gain_on_vector(0, 0)
             gain_on_vector(0, 1)
             for r in range(2):
                 gain_on_vector(1, r)
                 quantise(rounded[r][:].rearrange("p g j t -> p (g j t)"), h_runs[r])
-            totals = [group_tile("sum0"), group_tile("tab_w0")]
+            totals = [group_tile("by_tile"), group_tile("tab_w0")]
             results = [group_tile("plane1"), group_tile("plane3")]
             for r in range(2):
                 cols = slice(r * run, (r + 1) * run)
@@ -293,12 +312,16 @@ def tile_list_snowpack_recurrence_kernel(tc, tab_words, tab_scales, offs, xT, of
                                                     rhs=h_codes[:, own].bitcast(FP8X4), rhs_scale=h_scales[:, own],
                                                     start=(a == 0), stop=(a == GROUPS - 1))
                         k = 2 * g + t0 // 2
-                        total = totals[r][:, k, :].rearrange("p (t j) -> p t j", t=2)
-                        nc.vector.tensor_tensor(total, bank[:].rearrange("p (t j) -> p t j", t=2),
-                                                b_kept[g][:, t0:t0 + 2, cols], ALU.add)
-                        nc.scalar.activation(results[r][:, k, :], totals[r][:, k, :], ACT.Tanh)
-                        nc.sync.dma_start(out_rows[g][:, t0:t0 + 2, W + r * run:W + (r + 1) * run],
-                                          results[r][:, k, :].rearrange("p (t j) -> p t j", t=2))
+                        last = r == 1 and k == 3
+                        for u in ((0, 1) if last else (None,)):
+                            rows = slice(t0, t0 + 2) if u is None else slice(t0 + u, t0 + u + 1)
+                            part = slice(0, W) if u is None else slice(u * run, (u + 1) * run)
+                            total = totals[r][:, k, part].rearrange("p (t j) -> p t j", j=run)
+                            nc.vector.tensor_tensor(total, bank[:, part].rearrange("p (t j) -> p t j", j=run),
+                                                    b_kept[g][:, rows, cols], ALU.add)
+                            nc.scalar.activation(results[r][:, k, part], totals[r][:, k, part], ACT.Tanh)
+                            nc.sync.dma_start(out_rows[g][:, rows, W + r * run:W + (r + 1) * run],
+                                              results[r][:, k, part].rearrange("p (t j) -> p t j", j=run))
 
         wx_q = [mx_tiles("wx%d" % g) for g in range(GROUPS)]
         x_q = [mx_tiles("x%d" % half) for half in range(HALVES)]
@@ -326,24 +349,21 @@ def tile_list_snowpack_recurrence_kernel(tc, tab_words, tab_scales, offs, xT, of
         for t in range(PACK):
             nc.scalar.activation(by_tile[:, t, :], th_first0[:, t, :], ACT.Copy, scale=gain_sb[:, 0, t:t + 1])
         th_first1 = first_step(0, 1, (0, 1, None), None, None, "th_first1")
-        wr_c = order_wr(wr_raw, "wx_raw0")
-        h_b0 = h_tile("plane2")
+        v_c.append([gather_v(a, entries(list_v, 1), "plane%d" % (2 + a))[:] for a in range(PASSES)])
+        quantise(round_x(diff1, "wx_raw1"), x_q[1])
+        wr_c = order_wr(wr_raw, "wx_b1")
+        h_b0 = h_tile("wx_raw1")
         nc.vector.tensor_copy(h_b0[:].rearrange("p (c i) t -> p c t i", i=4),
                               by_tile[:].rearrange("p t (c i) -> p c t i", i=4))
-        quantise(round_x(diff1, "wx_raw1"), x_q[1])
-        h_q[0][0] = (keep.tile([P, W], U32, name="wx_b1", align_bytes=64), h_q[0][0][1])
         quantise(h_b0[:].rearrange("p j t -> p (j t)"), h_q[0][0])
-        v_second = keep.tile([P, PASSES, W], U32, name="wx_raw1", align_bytes=64)
-        for a in range(PASSES):
-            nc.vector.tensor_copy(v_second[:, a, :], tab_w[a][:].bitcast(U32).indirect(entries(list_v, 1)))
-        v_c.append([v_second[:, a, :] for a in range(PASSES)])
-        h_b1 = h_tile("plane2")
+        h_b1 = h_tile("wx_raw1")
         gain_on_gpsimd(th_first1, 1, h_b1[:], slice(0, W))
 
-        b_second = [keep_b(1, 0, PACK), keep_b(1, 1, PACK // 2)]
-        ths = [first_step(1, 0, (0, 1), b_second, group_tile("sum0"), "plane0")]
+        early = [table_passes(1, 0, t) for t in range(PACK)]
+        b_second = [keep_b(1, 0, PACK, "b_kept0"), keep_b(1, 1, PACK, "b_kept1")]
+        ths = [add_and_tanh(early, b_second[0], group_tile("by_tile"), "plane0")]
+        ths.append(add_and_tanh([table_passes(1, 1, t) for t in range(PACK)], b_second[1], group_tile("sum1"), "plane1"))
         quantise(h_b1[:].rearrange("p j t -> p (j t)"), h_q[0][1])
-        ths.append(first_step(1, 1, (0, 1), b_second, group_tile("th_first1"), "plane1"))
-        second_step(0, 0, None, None, "th_first1")
-        second_step(0, 1, None, None, "plane0")
+        second_step(0, 0, "sum1")
+        second_step(0, 1, "plane0")
         last_step(b_second, ths)

@@ -57,13 +57,11 @@ def tile_list_snowpack_recurrence_kernel(tc, tab_words, tab_scales, offs, xT, of
         wx_rows = wx.rearrange("(p j) c -> p j c", j=PACK)
 
         def load_weight_scales(scales, first_row, q):
-            row = 32 * q + first_row
-            nc.sync.dma_start(w_s_raw[row:row + 4, :, :],
-                              scales[:, 4 * q:4 * q + 4, :].rearrange("a r n -> r a n").bitcast(I32))
+            nc.sync.dma_start(w_s_raw[first_row + q:P:32, :, :],
+                              scales.rearrange("a (u r) n -> r u a n", r=4)[q].bitcast(I32))
 
         def move_v_scales(queue, a, q):
-            row = 16 * a + 4 * q
-            queue.dma_start(v_s[32 * q:32 * q + 4, a, :], v_s_rows[row:row + 4, :].bitcast(I32))
+            queue.dma_start(v_s[q:P:32, a, :], v_s_rows[16 * a + q:16 * a + 16:4, :].bitcast(I32))
 
         def load_table(a):
             nc.sync.dma_start(tab_w[a][:], tab_words[a].rearrange("p n t -> p (n t)").bitcast(I32))

@@ -195,7 +195,7 @@ def tile_list_snowpack_recurrence_kernel(tc, tab_words, tab_scales, offs, xT, of
             for t in range(PACK):
                 bank = new_bank()
                 pass_b(bank, half, g, t, True, True)
-                if t < on_scalar:
+                if t >= PACK - on_scalar:
                     nc.scalar.copy(kept[:, t, :], bank[:])
                 else:
                     nc.vector.tensor_copy(kept[:, t, :], bank[:])
@@ -278,7 +278,7 @@ def tile_list_snowpack_recurrence_kernel(tc, tab_words, tab_scales, offs, xT, of
             out_rows = out.rearrange("(g p t) j -> g p t j", g=GROUPS, t=PACK)
             spans = [slice(r * run, (r + 1) * run) for r in range(2)]
             rounded = [keep.tile([P, GROUPS, run, PACK], BF16, name=place, align_bytes=64)
-                       for place in ("wx_raw1", "th_first1")]
+                       for place in ("wx_b1", "plane3")]
             h_runs = [mx_tiles("h_run%d" % r) for r in range(2)]
 
             def gain_on_vector(g, r):
@@ -287,7 +287,7 @@ def tile_list_snowpack_recurrence_kernel(tc, tab_words, tab_scales, offs, xT, of
                                         gain_sb[:, g, :].unsqueeze(1).unsqueeze(3).to_broadcast([P, run // 2, PACK, 2]),
                                         ALU.mult)
 
-            gain_on_vector(0, 0)
+            gain_on_gpsimd(ths[0], 0, rounded[0][:, 0, :, :], spans[0])
             gain_on_vector(0, 1)
             for r in range(2):
                 gain_on_vector(1, r)
@@ -348,20 +348,27 @@ def tile_list_snowpack_recurrence_kernel(tc, tab_words, tab_scales, offs, xT, of
             nc.scalar.activation(by_tile[:, t, :], th_first0[:, t, :], ACT.Copy, scale=gain_sb[:, 0, t:t + 1])
         th_first1 = first_step(0, 1, (0, 1, None), None, None, "th_first1")
         v_c.append([gather_v(a, entries(list_v, 1), "plane%d" % (2 + a))[:] for a in range(PASSES)])
+        spans = [slice(r * W // 2, (r + 1) * W // 2) for r in range(2)]
+        h_b1 = [keep.tile([P, W // 2, PACK], BF16, name="wx_raw0", align_bytes=64)]
+        gain_on_gpsimd(th_first1, 1, h_b1[0][:], spans[0])
         quantise(round_x(diff1, "wx_raw1"), x_q[1])
-        wr_c = order_wr(wr_raw, "wx_b1")
-        h_b0 = h_tile("wx_raw1")
-        nc.vector.tensor_copy(h_b0[:].rearrange("p (c i) t -> p c t i", i=4),
-                              by_tile[:].rearrange("p t (c i) -> p c t i", i=4))
+        wr_c = order_wr(wr_raw, "wx_raw1")
+        h_b0 = h_tile("wx_b1")
+        nc.scalar.copy(h_b0[:].rearrange("p (c i) t -> p c t i", i=4),
+                       by_tile[:].rearrange("p t (c i) -> p c t i", i=4))
         quantise(h_b0[:].rearrange("p j t -> p (j t)"), h_q[0][0])
-        h_b1 = h_tile("wx_raw1")
-        gain_on_gpsimd(th_first1, 1, h_b1[:], slice(0, W))
+        h_b1.append(keep.tile([P, W // 2, PACK], BF16, name="wx_b1", align_bytes=64))
+        gain_on_gpsimd(th_first1, 1, h_b1[1][:], spans[1])
 
         early = [table_passes(1, 0, t) for t in range(PACK)]
-        b_second = [keep_b(1, 0, PACK, "b_kept0"), keep_b(1, 1, PACK, "b_kept1")]
+        b_second = [keep_b(1, 0, PACK, "b_kept0")]
         ths = [add_and_tanh(early, b_second[0], group_tile("by_tile"), "plane0")]
-        ths.append(add_and_tanh([table_passes(1, 1, t) for t in range(PACK)], b_second[1], group_tile("sum1"), "plane1"))
-        quantise(h_b1[:].rearrange("p j t -> p (j t)"), h_q[0][1])
-        second_step(0, 0, "sum1")
+        b_second.append(keep_b(1, 1, PACK // 2, "b_kept1"))
+        for r in range(2):
+            nc.vector.quantize_mx(out=h_q[0][1][0][:, spans[r]].bitcast(FP8X4), scales=h_q[0][1][1][:, spans[r]],
+                                  in_=h_b1[r][:].rearrange("p j t -> p (j t)"))
+        late = [table_passes(1, 1, t) for t in range(PACK)]
+        ths.append(add_and_tanh(late, b_second[1], group_tile("th_first1"), "plane1"))
+        second_step(0, 0, "th_first1")
         second_step(0, 1, "plane0")
         last_step(b_second, ths)

@@ -25,6 +25,7 @@ HALVES = S // W
 GROUPS = H // (P * PACK)
 PASSES = K // (P * PACK)
 BANKS = 8
+EARLY_TILES = 2
 GAIN_ON_SCALAR = W // 4
 
 
@@ -261,14 +262,16 @@ def tile_list_snowpack_recurrence_kernel(tc, tab_words, tab_scales, offs, xT, of
         def h_tile(place):
             return keep.tile([P, W, PACK], BF16, name=place, align_bytes=64)
 
-        def second_step(half, g, place):
-            out_rows = out.rearrange("(g p t) j -> g t p j", g=GROUPS, t=PACK)
-            result = group_tile(place)
-            banks = [new_bank() for t in range(PACK)]
-            for t in range(PACK):
+        def open_second_step(half, g, tiles):
+            banks = {t: new_bank() for t in tiles}
+            for t in tiles:
                 pass_b(banks[t], half, g, t, True, False)
                 pass_wr(banks[t], half, g, t, 0, False, False)
-            for t in range(PACK):
+            return banks
+
+        def close_second_step(half, g, banks, tiles, result):
+            out_rows = out.rearrange("(g p t) j -> g t p j", g=GROUPS, t=PACK)
+            for t in tiles:
                 pass_wr(banks[t], half, g, t, 1, False, True)
                 nc.scalar.activation(result[:, t, :], banks[t][:], ACT.Tanh)
                 nc.sync.dma_start(out_rows[g, t][:, half * W:(half + 1) * W], result[:, t, :])
@@ -368,7 +371,11 @@ def tile_list_snowpack_recurrence_kernel(tc, tab_words, tab_scales, offs, xT, of
             nc.vector.quantize_mx(out=h_q[0][1][0][:, spans[r]].bitcast(FP8X4), scales=h_q[0][1][1][:, spans[r]],
                                   in_=h_b1[r][:].rearrange("p j t -> p (j t)"))
         late = [table_passes(1, 1, t) for t in range(PACK)]
+        early_result = group_tile("b_early")
+        for t in range(EARLY_TILES):
+            close_second_step(0, 0, open_second_step(0, 0, [t]), [t], early_result)
         ths.append(add_and_tanh(late, b_second[1], group_tile("th_first1"), "plane1"))
-        second_step(0, 0, "th_first1")
-        second_step(0, 1, "plane0")
+        rest = range(EARLY_TILES, PACK)
+        close_second_step(0, 0, open_second_step(0, 0, rest), rest, group_tile("th_first1"))
+        close_second_step(0, 1, open_second_step(0, 1, range(PACK)), range(PACK), group_tile("plane0"))
         last_step(b_second, ths)

@@ -25,7 +25,7 @@ HALVES = S // W
 GROUPS = H // (P * PACK)
 PASSES = K // (P * PACK)
 BANKS = 8
-EARLY_TILES = 2
+EARLY_TILES = 1
 GAIN_ON_SCALAR = W // 4
 
 

@@ -25,8 +25,8 @@ HALVES = S // W
 GROUPS = H // (P * PACK)
 PASSES = K // (P * PACK)
 BANKS = 8
-EARLY_TILES = 1
-GAIN_ON_SCALAR = W // 4
+RUN = W // 2
+COPIES_ON_VECTOR = 2
 
 
 def tile_list_snowpack_recurrence_kernel(tc, tab_words, tab_scales, offs, xT, offs2, offs3, wp_words,
@@ -34,140 +34,88 @@ def tile_list_snowpack_recurrence_kernel(tc, tab_words, tab_scales, offs, xT, of
     nc = tc.nc
     with ExitStack() as ctx:
         keep = ctx.enter_context(tc.tile_pool(name="keep", bufs=1))
-        ring = ctx.enter_context(tc.tile_pool(name="ring", bufs=2))
         psum = ctx.enter_context(tc.psum_pool(name="psum", bufs=1))
+
+        def sbuf(shape, dtype, place):
+            return keep.tile([P] + shape, dtype, name=place, align_bytes=64)
+
+        def group_tile(place):
+            return sbuf([PACK, W], F32, place)
 
         list_v = keep.tile([P, S // STRIPE], U16, name="list_v")
         list_2 = keep.tile([P, S // STRIPE], U16, name="list_2")
         list_3 = keep.tile([P, S // STRIPE], U16, name="list_3")
 
-        tab_s = keep.tile([P, T // 4], I32, name="tab_s", align_bytes=64)
-        w_s_raw = keep.tile([P, PASSES, H // 4], I32, name="w_s_raw", align_bytes=64)
-        v_s = keep.tile([P, PASSES, S // 4], I32, name="v_s", align_bytes=64)
+        ROW = H // 4
+        tab_s = sbuf([T // 4], I32, "tab_s")
+        w_s_raw = sbuf([ROW], I32, "w_s_raw")
+        scales = sbuf([5 * ROW], I32, "scales")
         nc.vector.memset(tab_s[32:64, :], 0)
         nc.vector.memset(tab_s[64:P, :], 0)
-        nc.vector.memset(w_s_raw[:], 0)
-        nc.vector.memset(v_s[:], 0)
+        nc.vector.memset(w_s_raw[64:P, :], 0)
+        nc.vector.memset(scales[:], 0)
+        scale_bytes = scales[:].bitcast(U8)
 
-        wp_raw = keep.tile([P, PASSES, H // 2], I32, name="wp_raw", align_bytes=64)
-        planes = [keep.tile([P, T], F32, name="plane%d" % t, align_bytes=64) for t in range(PACK)]
-        wx_raw = [keep.tile([P, PACK, W], F32, name="wx_raw%d" % g, align_bytes=64) for g in range(GROUPS)]
-        tab_w = [keep.tile([P, T], I32, name="tab_w%d" % a, align_bytes=64) for a in range(PASSES)]
+        wp_raw = sbuf([PASSES, H // 2], I32, "wp_raw")
+        planes = [sbuf([T], F32, "plane%d" % t) for t in range(PACK)]
+        wx_raw = [group_tile("wx_raw%d" % g) for g in range(GROUPS)]
+        tab_w = [sbuf([T], I32, "tab_w%d" % a) for a in range(PASSES)]
+        wr_raw = sbuf([GROUPS, H], I32, "wr_raw")
         gain_sb = keep.tile([P, GROUPS, PACK], F32, name="gain_sb")
         x_rows = xT.rearrange("(p t) n -> t p n", t=PACK)
         wx_rows = wx.rearrange("(p j) c -> p j c", j=PACK)
-
-        def load_weight_scales(scales, first_row, q):
-            nc.sync.dma_start(w_s_raw[first_row + q:P:32, :, :],
-                              scales.rearrange("a (u r) n -> r u a n", r=4)[q].bitcast(I32))
-
-        def move_v_scales(queue, a, q):
-            queue.dma_start(v_s[q:P:32, a, :], v_s_rows[16 * a + q:16 * a + 16:4, :].bitcast(I32))
-
-        def load_table(a):
-            nc.sync.dma_start(tab_w[a][:], tab_words[a].rearrange("p n t -> p (n t)").bitcast(I32))
-
-        nc.sync.dma_start(list_v[:], offs)
-        nc.sync.dma_start(tab_s[0:32, :], tab_scales.rearrange("a q n -> (a q) n").bitcast(I32))
-        nc.sync.dma_start(list_3[:], offs3)
-        nc.sync.dma_start(list_2[:], offs2)
-        nc.sync.dma_start(wp_raw[:], wp_words.rearrange("a p n -> p a n").bitcast(I32))
-        v_s_rows = keep.tile([P, S], U8, name="v_s_rows", align_bytes=64)
-        nc.vector.tensor_copy(v_s_rows[:], tab_s[:].bitcast(U8).indirect(list_v[:]))
-        nc.sync.dma_start(planes[0][:], x_rows[0])
-        nc.sync.dma_start(planes[1][:], x_rows[1])
-        for q in range(3):
-            load_weight_scales(wp_scales, 0, q)
-        nc.sync.dma_start(planes[2][:], x_rows[2])
-        load_weight_scales(wp_scales, 0, 3)
-        load_weight_scales(wr_scales, 4, 0)
-        load_weight_scales(wr_scales, 4, 1)
-        nc.sync.dma_start(planes[3][:], x_rows[3])
-        load_weight_scales(wr_scales, 4, 2)
-        load_weight_scales(wr_scales, 4, 3)
-        move_v_scales(nc.sync, 0, 0)
-        nc.sync.dma_start(wx_raw[0][:], wx_rows[:, :, 0:W])
-        for q in range(1, QUADRANTS):
-            move_v_scales(nc.sync, 0, q)
-        for q in range(QUADRANTS):
-            move_v_scales(nc.gpsimd, 1, q)
-        for a in range(PASSES):
-            load_table(a)
-        nc.sync.dma_start(wx_raw[1][:], wx_rows[:, :, W:2 * W])
-        nc.sync.dma_start(gain_sb[:], gain.rearrange("(g p t) -> p g t", g=GROUPS, t=PACK))
-
-        wp_c = keep.tile([P, PASSES, 2 * H], U8, name="wp_c", align_bytes=64)
-        nc.vector.tensor_copy(
-            wp_c[:].bitcast(U16).rearrange("p a (g t m) -> p (a g) m t", g=GROUPS, t=PACK),
-            wp_raw[:].bitcast(U16).rearrange("p a (g m t) -> p (a g) m t", g=GROUPS, t=PACK))
-
-        def order_scales(raw, columns, place):
-            ordered = keep.tile([P, columns], U8, name=place, align_bytes=64)
-            nc.vector.tensor_copy(ordered[:].rearrange("p (g t m) -> p g m t", m=P, t=PACK),
-                                  raw.bitcast(U8).rearrange("p (g m t) -> p g m t", m=P, t=PACK))
-            return ordered
-
-        def order_wr(raw, place):
-            ordered = keep.tile([P, GROUPS, H], I32, name=place, align_bytes=64)
-            nc.vector.tensor_copy(
-                ordered[:].rearrange("p a (g t m) -> p (a g) m t", g=GROUPS, t=PACK),
-                raw[:].rearrange("p a (g m t) -> p (a g) m t", g=GROUPS, t=PACK))
-            return ordered
-
-        def round_wx(g, place):
-            rounded = keep.tile([P, W * PACK], BF16, name=place, align_bytes=64)
-            nc.scalar.copy(rounded[:].rearrange("p (t m j) -> p m j t", t=PACK, j=PACK),
-                           wx_raw[g][:].rearrange("p j (m t) -> p m j t", t=PACK))
-            return rounded[:]
-
-        def mx_tiles(name):
-            return (keep.tile([P, W], U32, name=name + "_codes", align_bytes=64),
-                    keep.tile([P, W], U8, name=name + "_scales", align_bytes=64))
-
-        def quantise(rounded, operand):
-            codes, scales = operand
-            nc.vector.quantize_mx(out=codes[:].bitcast(FP8X4), scales=scales[:], in_=rounded)
+        v_s_rows = sbuf([S], U8, "v_s_rows")
+        stage = sbuf([2 * ROW], I32, "stage")
 
         def entries(list_tile, half):
             return list_tile[:, half * (W // STRIPE):(half + 1) * (W // STRIPE)]
 
-        def gather_x(half, place):
-            minus = keep.tile([P, PACK, W], F32, name=place, align_bytes=64)
-            diff = keep.tile([P, PACK, W], F32, name="diff", align_bytes=64)
-            for t in range(PACK + 1):
-                if t < PACK:
-                    nc.vector.tensor_copy(minus[:, t, :], planes[t][:].indirect(entries(list_3, half)))
-                if t > 0:
-                    nc.vector.tensor_tensor(diff[:, t - 1, :], planes[t - 1][:].indirect(entries(list_2, half)),
-                                            minus[:, t - 1, :], ALU.subtract)
-            return diff
+        minus = [group_tile("minus%d" % half) for half in range(HALVES)]
 
-        def gather_planes(list_tile, half, place):
-            picked = keep.tile([P, PACK, W], F32, name=place, align_bytes=64)
-            for t in range(PACK):
-                nc.vector.tensor_copy(picked[:, t, :], planes[t][:].indirect(entries(list_tile, half)))
-            return picked[:]
+        def gather_minus(half, t):
+            nc.vector.tensor_copy(minus[half][:, t, :], planes[t][:].indirect(entries(list_3, half)))
 
-        def subtract_x(plus, minus, place):
-            rounded = keep.tile([P, W * PACK], BF16, name=place, align_bytes=64)
-            nc.vector.tensor_tensor(rounded[:].rearrange("p (c i t) -> p c t i", i=2, t=PACK),
-                                    plus.rearrange("p t (c i) -> p c t i", i=2),
-                                    minus.rearrange("p t (c i) -> p c t i", i=2), ALU.subtract)
+        def gather_diff(diff, half, t):
+            nc.vector.tensor_tensor(diff[:, t, :], planes[t][:].indirect(entries(list_2, half)),
+                                    minus[half][:, t, :], ALU.subtract)
+
+        def move_table_scales(queue, a, q):
+            queue.dma_start(scales[q:P:32, 2 * a * ROW:2 * (a + 1) * ROW], stage[16 * a + q:16 * a + 16:4, :])
+
+        def move_wr_scales(a, q):
+            nc.sync.dma_start(scales[4 * a + q:P:32, 4 * ROW:5 * ROW],
+                              stage[32 + 16 * a + q:32 + 16 * a + 16:4, ROW:2 * ROW])
+
+        def load_plane(t):
+            nc.sync.dma_start(planes[t][:], x_rows[t])
+
+        def load_wx(g):
+            nc.sync.dma_start(wx_raw[g][:], wx_rows[:, :, g * W:(g + 1) * W])
+
+        def round_wx(g):
+            rounded = sbuf([W * PACK], BF16, "wx_b%d" % g)
+            nc.scalar.copy(rounded[:].rearrange("p (t m j) -> p m j t", t=PACK, j=PACK),
+                           wx_raw[g][:].rearrange("p j (m t) -> p m j t", t=PACK))
             return rounded[:]
 
+        def mx_tiles(name, codes_place=None):
+            return sbuf([W], U32, codes_place or name + "_codes"), sbuf([W], U8, name + "_scales")
+
+        def quantise(rounded, operand):
+            codes, block_scales = operand
+            nc.vector.quantize_mx(out=codes[:].bitcast(FP8X4), scales=block_scales[:], in_=rounded)
+
         def round_x(diff, place):
-            rounded = keep.tile([P, W * PACK], BF16, name=place, align_bytes=64)
+            rounded = sbuf([W * PACK], BF16, place)
             nc.scalar.copy(rounded[:].rearrange("p (c i t) -> p c t i", i=2, t=PACK),
                            diff[:].rearrange("p t (c i) -> p c t i", i=2))
             return rounded[:]
 
-        def gather_v(a, offsets, place):
-            words = keep.tile([P, offsets.shape[1] * STRIPE], U32, name=place, align_bytes=64)
-            nc.vector.tensor_copy(words[:], tab_w[a][:].bitcast(U32).indirect(offsets))
-            return words
+        def gather_v(words, half, a):
+            nc.vector.tensor_copy(words[:, a, :], tab_w[a][:].bitcast(U32).indirect(entries(list_v, half)))
 
-        def new_bank():
-            return psum.tile([P, W], F32, name="bank", bufs=BANKS)
+        def new_bank(k):
+            return psum.tile([P, W], F32, name="bank%d" % k)
 
         def pass_b(bank, half, g, t, start, stop):
             cols = slice(t * P, (t + 1) * P)
@@ -178,204 +126,207 @@ def tile_list_snowpack_recurrence_kernel(tc, tab_words, tab_scales, offs, xT, of
 
         def pass_wp(bank, half, g, t, a, start, stop):
             c0 = (g * PACK + t) * P
+            v_col, wp_col = 2 * a * H + half * W, (2 * a + 1) * H + c0
             nc.tensor.matmul_mx(bank[:], lhsT=wp_c[:, a, 2 * c0:2 * (c0 + P)].bitcast(FP4X4),
-                                lhsT_scale=w_s[:, a * H + c0:a * H + c0 + P],
-                                rhs=v_c[half][a].bitcast(FP8X4),
-                                rhs_scale=v_s[:, a, :].bitcast(U8)[:, half * W:(half + 1) * W],
+                                lhsT_scale=scale_bytes[:, wp_col:wp_col + P],
+                                rhs=v_c[half][:, a, :].bitcast(FP8X4), rhs_scale=scale_bytes[:, v_col:v_col + W],
                                 start=start, stop=stop)
 
-        def pass_wr(bank, half, g, t, a, start, stop):
+        def pass_wr(sums, g, t, a, h_codes, h_scales, start, stop):
             c0 = (g * PACK + t) * P
-            h_codes, h_scales = h_q[half][a]
-            nc.tensor.matmul_mx(bank[:], lhsT=wr_c[:, a, c0:c0 + P].bitcast(FP8X4),
-                                lhsT_scale=w_s[4:P, a * H + c0:a * H + c0 + P],
-                                rhs=h_codes[:].bitcast(FP8X4), rhs_scale=h_scales[:], start=start, stop=stop)
-
-        def keep_b(half, g, on_scalar, place):
-            kept = keep.tile([P, PACK, W], F32, name=place, align_bytes=64)
-            for t in range(PACK):
-                bank = new_bank()
-                pass_b(bank, half, g, t, True, True)
-                if t >= PACK - on_scalar:
-                    nc.scalar.copy(kept[:, t, :], bank[:])
-                else:
-                    nc.vector.tensor_copy(kept[:, t, :], bank[:])
-            return kept
-
-        def product_plus_b(product, order, half, g, t, b_kept, total):
-            bank = new_bank()
-            for i, a in enumerate(order):
-                if a is None:
-                    pass_b(bank, half, g, t, i == 0, i == len(order) - 1)
-                else:
-                    product(bank, half, g, t, a, i == 0, i == len(order) - 1)
-            if b_kept is None:
-                return bank[:]
-            nc.vector.tensor_tensor(total[:, t, :], bank[:], b_kept[g][:, t, :], ALU.add)
-            return total[:, t, :]
-
-        def group_tile(place):
-            return keep.tile([P, PACK, W], F32, name=place, align_bytes=64)
-
-        def table_passes(half, g, t):
-            bank = new_bank()
-            for a in range(PASSES):
-                pass_wp(bank, half, g, t, a, a == 0, a == PASSES - 1)
-            return bank
-
-        def add_and_tanh(banks, b_kept, total, place):
-            th = group_tile(place)
-            for t0 in range(0, PACK, 2):
-                for t in range(t0, t0 + 2):
-                    nc.vector.tensor_tensor(total[:, t, :], banks[t][:], b_kept[:, t, :], ALU.add)
-                nc.scalar.activation(th[:, t0:t0 + 2, :], total[:, t0:t0 + 2, :], ACT.Tanh)
-            return th
-
-        def first_step(half, g, order, b_kept, total, place):
-            th = group_tile(place)
-            for t in range(PACK):
-                nc.scalar.activation(th[:, t, :], product_plus_b(pass_wp, order, half, g, t, b_kept, total), ACT.Tanh)
-            return th
-
-        def apply_gain(th, g, on_scalar, place):
-            rounded = keep.tile([P, W, PACK], BF16, name=place, align_bytes=64)
-            if on_scalar > 0:
-                by_tile = ring.tile([P, PACK, on_scalar], BF16, name="h_by_tile", align_bytes=64)
-                for t in range(PACK):
-                    nc.scalar.activation(by_tile[:, t, :], th[:, t, 0:on_scalar], ACT.Copy,
-                                         scale=gain_sb[:, g, t:t + 1])
-                nc.vector.tensor_copy(rounded[:, 0:on_scalar, :].rearrange("p (c i) t -> p c t i", i=4),
-                                      by_tile[:].rearrange("p t (c i) -> p c t i", i=4))
-            if on_scalar < W:
-                pairs = (W - on_scalar) // 2
-                nc.vector.tensor_tensor(rounded[:, on_scalar:W, :].rearrange("p (c i) t -> p c t i", i=2),
-                                        th[:, :, on_scalar:W].rearrange("p t (c i) -> p c t i", i=2),
-                                        gain_sb[:, g, :].unsqueeze(1).unsqueeze(3).to_broadcast([P, pairs, PACK, 2]),
-                                        ALU.mult)
-            return rounded[:].rearrange("p j t -> p (j t)")
+            nc.tensor.matmul_mx(sums, lhsT=wr_c[:, a, c0:c0 + P].bitcast(FP8X4),
+                                lhsT_scale=scale_bytes[4 * a:P, 4 * H + c0:4 * H + c0 + P],
+                                rhs=h_codes.bitcast(FP8X4), rhs_scale=h_scales, start=start, stop=stop)
 
         def gain_on_gpsimd(th, g, rounded, cols):
             count = cols.stop - cols.start
             nc.gpsimd.tensor_tensor(rounded, th[:, :, cols].rearrange("p t c -> p c t"),
                                     gain_sb[:, g, :].unsqueeze(1).to_broadcast([P, count, PACK]), ALU.mult)
 
-        def h_tile(place):
-            return keep.tile([P, W, PACK], BF16, name=place, align_bytes=64)
+        def gain_on_vector(th, g, rounded, cols):
+            pairs = (cols.stop - cols.start) // 2
+            nc.vector.tensor_tensor(rounded.rearrange("p (c i) t -> p c t i", i=2),
+                                    th[:, :, cols].rearrange("p t (c i) -> p c t i", i=2),
+                                    gain_sb[:, g, :].unsqueeze(1).unsqueeze(3).to_broadcast([P, pairs, PACK, 2]),
+                                    ALU.mult)
 
-        def open_second_step(half, g, tiles):
-            banks = {t: new_bank() for t in tiles}
-            for t in tiles:
-                pass_b(banks[t], half, g, t, True, False)
-                pass_wr(banks[t], half, g, t, 0, False, False)
-            return banks
-
-        def close_second_step(half, g, banks, tiles, result):
-            out_rows = out.rearrange("(g p t) j -> g t p j", g=GROUPS, t=PACK)
-            for t in tiles:
-                pass_wr(banks[t], half, g, t, 1, False, True)
-                nc.scalar.activation(result[:, t, :], banks[t][:], ACT.Tanh)
-                nc.sync.dma_start(out_rows[g, t][:, half * W:(half + 1) * W], result[:, t, :])
-
-        def last_step(b_kept, ths):
-            run = W // 2
-            out_rows = out.rearrange("(g p t) j -> g p t j", g=GROUPS, t=PACK)
-            spans = [slice(r * run, (r + 1) * run) for r in range(2)]
-            rounded = [keep.tile([P, GROUPS, run, PACK], BF16, name=place, align_bytes=64)
-                       for place in ("wx_b1", "plane3")]
-            h_runs = [mx_tiles("h_run%d" % r) for r in range(2)]
-
-            def gain_on_vector(g, r):
-                nc.vector.tensor_tensor(rounded[r][:, g, :, :].rearrange("p (c i) t -> p c t i", i=2),
-                                        ths[g][:, :, spans[r]].rearrange("p t (c i) -> p c t i", i=2),
-                                        gain_sb[:, g, :].unsqueeze(1).unsqueeze(3).to_broadcast([P, run // 2, PACK, 2]),
-                                        ALU.mult)
-
-            gain_on_gpsimd(ths[0], 0, rounded[0][:, 0, :, :], spans[0])
-            gain_on_vector(0, 1)
-            for r in range(2):
-                gain_on_vector(1, r)
-                quantise(rounded[r][:].rearrange("p g j t -> p (g j t)"), h_runs[r])
-            totals = [group_tile("by_tile"), group_tile("tab_w0")]
-            results = [group_tile("plane1"), group_tile("plane3")]
-            for r in range(2):
-                cols = slice(r * run, (r + 1) * run)
-                for g in range(GROUPS):
-                    for t0 in range(0, PACK, 2):
-                        bank = new_bank()
-                        for t in range(t0, t0 + 2):
-                            c0 = (g * PACK + t) * P
-                            for a in range(GROUPS):
-                                h_codes, h_scales = h_runs[r]
-                                own = slice(a * run, (a + 1) * run)
-                                nc.tensor.matmul_mx(bank[:, (t - t0) * run:(t - t0 + 1) * run],
-                                                    lhsT=wr_c[:, a, c0:c0 + P].bitcast(FP8X4),
-                                                    lhsT_scale=w_s[4:P, a * H + c0:a * H + c0 + P],
-                                                    rhs=h_codes[:, own].bitcast(FP8X4), rhs_scale=h_scales[:, own],
-                                                    start=(a == 0), stop=(a == GROUPS - 1))
-                        k = 2 * g + t0 // 2
-                        last = r == 1 and k == 3
-                        for u in ((0, 1) if last else (None,)):
-                            rows = slice(t0, t0 + 2) if u is None else slice(t0 + u, t0 + u + 1)
-                            part = slice(0, W) if u is None else slice(u * run, (u + 1) * run)
-                            total = totals[r][:, k, part].rearrange("p (t j) -> p t j", j=run)
-                            nc.vector.tensor_tensor(total, bank[:, part].rearrange("p (t j) -> p t j", j=run),
-                                                    b_kept[g][:, rows, cols], ALU.add)
-                            nc.scalar.activation(results[r][:, k, part], totals[r][:, k, part], ACT.Tanh)
-                            nc.sync.dma_start(out_rows[g][:, rows, W + r * run:W + (r + 1) * run],
-                                              results[r][:, k, part].rearrange("p (t j) -> p t j", j=run))
-
+        spans = [slice(r * RUN, (r + 1) * RUN) for r in range(2)]
+        out_rows = out.rearrange("(g p t) j -> g p t j", g=GROUPS, t=PACK)
         wx_q = [mx_tiles("wx%d" % g) for g in range(GROUPS)]
         x_q = [mx_tiles("x%d" % half) for half in range(HALVES)]
-        h_q = [[mx_tiles("h0_%d" % g) for g in range(GROUPS)]]
-        v_c = []
 
-        wx_b0 = round_wx(0, "wx_b0")
-        diff0 = gather_x(0, "minus0")
-        w_s = order_scales(w_s_raw[:].rearrange("p a n -> p (a n)"), PASSES * H, "w_s")
-        v_00 = gather_v(0, entries(list_v, 0), "v_00")
-        quantise(wx_b0, wx_q[0])
-        v_c.append([v_00[:], gather_v(1, entries(list_v, 0), "v_01")[:]])
-        quantise(round_x(diff0, "wx_raw0"), x_q[0])
-        wr_raw = keep.tile([P, GROUPS, H], I32, name="diff", align_bytes=64)
+        nc.sync.dma_start(list_v[:], offs)
+        nc.sync.dma_start(tab_s[0:32, :], tab_scales.rearrange("a q n -> (a q) n").bitcast(I32))
+        nc.sync.dma_start(list_3[:], offs3)
+        load_plane(0)
+        nc.sync.dma_start(list_2[:], offs2)
+        nc.sync.dma_start(w_s_raw[0:32, :], wp_scales.rearrange("a q n -> (a q) n").bitcast(I32))
+        nc.sync.dma_start(w_s_raw[32:64, :], wr_scales.rearrange("a q n -> (a q) n").bitcast(I32))
+        nc.vector.tensor_copy(v_s_rows[:], tab_s[:].bitcast(U8).indirect(list_v[:]))
+        load_plane(1)
+        load_wx(0)
+        load_plane(2)
+        diff0 = group_tile("diff0")
+        gather_minus(0, 0)
+        nc.vector.tensor_copy(stage[:, ROW:2 * ROW].bitcast(U8).rearrange("p (g t m) -> p g m t", m=P, t=PACK),
+                              w_s_raw[:].bitcast(U8).rearrange("p (g m t) -> p g m t", m=P, t=PACK))
+        nc.vector.tensor_copy(stage[:, 0:ROW], v_s_rows[:].bitcast(I32))
+        move_table_scales(nc.sync, 0, 0)
+        move_table_scales(nc.sync, 0, 1)
+        move_wr_scales(0, 0)
+        for q in range(QUADRANTS):
+            move_table_scales(nc.gpsimd, 1, q)
+        load_wx(1)
+        nc.sync.dma_start(wp_raw[:], wp_words.rearrange("a p n -> p a n").bitcast(I32))
+        move_table_scales(nc.sync, 0, 2)
+        move_table_scales(nc.sync, 0, 3)
+        move_wr_scales(0, 1)
+        load_plane(3)
+        for a in range(PASSES):
+            nc.sync.dma_start(tab_w[a][:], tab_words[a].rearrange("p n t -> p (n t)").bitcast(I32))
+        move_wr_scales(0, 2)
+        move_wr_scales(0, 3)
+        for q in range(QUADRANTS):
+            move_wr_scales(1, q)
+        nc.sync.dma_start(gain_sb[:], gain.rearrange("(g p t) -> p g t", g=GROUPS, t=PACK))
         nc.sync.dma_start(wr_raw[:], wr_words.rearrange("a p n t -> p a (n t)").bitcast(I32))
-        minus1 = gather_planes(list_3, 1, "wx_raw0")
-        quantise(round_wx(1, "wx_b1"), wx_q[1])
-        diff1 = group_tile("wx_b1")
-        for t in range(PACK):
-            nc.vector.tensor_tensor(diff1[:, t, :], planes[t][:].indirect(entries(list_2, 1)), minus1[:, t, :],
-                                    ALU.subtract)
 
-        th_first0 = first_step(0, 0, (0, 1, None), None, None, "wx_raw1")
-        by_tile = keep.tile([P, PACK, W], BF16, name="by_tile", align_bytes=64)
+        gather_minus(1, 0)
+        gather_diff(diff0, 0, 0)
+        for t in range(1, PACK - 1):
+            gather_minus(0, t)
+            gather_minus(1, t)
+            gather_diff(diff0, 0, t)
+            quantise(round_wx(t - 1), wx_q[t - 1])
+        wp_c = sbuf([PASSES, 2 * H], U8, "wp_c")
+        nc.scalar.copy(wp_c[:].bitcast(U16).rearrange("p a (g t m) -> p (a g) t m", g=GROUPS, t=PACK),
+                       wp_raw[:].bitcast(U16).rearrange("p a (g m t) -> p (a g) t m", g=GROUPS, t=PACK))
+        gather_minus(0, PACK - 1)
+        gather_diff(diff0, 0, PACK - 1)
+        gather_minus(1, PACK - 1)
+        v_c = [sbuf([PASSES, W], U32, "v_0")]
+        gather_v(v_c[0], 0, 0)
+        quantise(round_x(diff0, "x_b0"), x_q[0])
+        gather_v(v_c[0], 0, 1)
+        diff1 = group_tile("stage")
         for t in range(PACK):
-            nc.scalar.activation(by_tile[:, t, :], th_first0[:, t, :], ACT.Copy, scale=gain_sb[:, 0, t:t + 1])
-        th_first1 = first_step(0, 1, (0, 1, None), None, None, "th_first1")
-        v_c.append([gather_v(a, entries(list_v, 1), "plane%d" % (2 + a))[:] for a in range(PASSES)])
-        spans = [slice(r * W // 2, (r + 1) * W // 2) for r in range(2)]
-        h_b1 = [keep.tile([P, W // 2, PACK], BF16, name="wx_raw0", align_bytes=64)]
-        gain_on_gpsimd(th_first1, 1, h_b1[0][:], spans[0])
-        quantise(round_x(diff1, "wx_raw1"), x_q[1])
-        wr_c = order_wr(wr_raw, "wx_raw1")
-        h_b0 = h_tile("wx_b1")
-        nc.scalar.copy(h_b0[:].rearrange("p (c i) t -> p c t i", i=4),
-                       by_tile[:].rearrange("p t (c i) -> p c t i", i=4))
-        quantise(h_b0[:].rearrange("p j t -> p (j t)"), h_q[0][0])
-        h_b1.append(keep.tile([P, W // 2, PACK], BF16, name="wx_b1", align_bytes=64))
-        gain_on_gpsimd(th_first1, 1, h_b1[1][:], spans[1])
+            gather_diff(diff1, 1, t)
 
-        early = [table_passes(1, 0, t) for t in range(PACK)]
-        b_second = [keep_b(1, 0, PACK, "b_kept0")]
-        ths = [add_and_tanh(early, b_second[0], group_tile("by_tile"), "plane0")]
-        b_second.append(keep_b(1, 1, PACK // 2, "b_kept1"))
+        th_first = [group_tile("wx_raw%d" % g) for g in range(GROUPS)]
+        for t in range(PACK):
+            bank = new_bank(t)
+            pass_wp(bank, 0, 0, t, 0, True, False)
+            pass_b(bank, 0, 0, t, False, False)
+            pass_wp(bank, 0, 0, t, 1, False, True)
+            nc.scalar.activation(th_first[0][:, t, :], bank[:], ACT.Tanh)
+        by_tile = sbuf([PACK, RUN], BF16, "wx_b0")
+        for t in range(PACK):
+            nc.scalar.activation(by_tile[:, t, :], th_first[0][:, t, spans[1]], ACT.Copy,
+                                 scale=gain_sb[:, 0, t:t + 1])
+        banks = [new_bank(PACK + t) for t in range(PACK)]
+        for t in range(PACK):
+            for a in range(PASSES):
+                pass_wp(banks[t], 0, 1, t, a, a == 0, False)
+        x_b1 = round_x(diff1, "v_0")
+        for t in range(PACK):
+            pass_b(banks[t], 0, 1, t, False, True)
+            nc.scalar.activation(th_first[1][:, t, :], banks[t][:], ACT.Tanh)
+
+        v_c.append(sbuf([PASSES, W], U32, "plane3"))
+        for a in range(PASSES):
+            gather_v(v_c[1], 1, a)
+        h_b0 = sbuf([W, PACK], BF16, "minus1")
+        gain_on_gpsimd(th_first[0], 0, h_b0[:, spans[0], :], spans[0])
+        nc.vector.tensor_copy(h_b0[:, spans[1], :].rearrange("p (c i) t -> p c t i", i=4),
+                              by_tile[:].rearrange("p t (c i) -> p c t i", i=4))
+        quantise(x_b1, x_q[1])
+        wr_c = sbuf([GROUPS, H], I32, "v_0")
+        nc.vector.tensor_copy(wr_c[:].rearrange("p a (g t m) -> p (a g) m t", g=GROUPS, t=PACK),
+                              wr_raw[:].rearrange("p a (g m t) -> p (a g) m t", g=GROUPS, t=PACK))
+        h_first = [mx_tiles("h0", "wr_raw"), mx_tiles("h1")]
+        quantise(h_b0[:].rearrange("p j t -> p (j t)"), h_first[0])
+        h_b1 = sbuf([W, PACK], BF16, "minus1")
         for r in range(2):
-            nc.vector.quantize_mx(out=h_q[0][1][0][:, spans[r]].bitcast(FP8X4), scales=h_q[0][1][1][:, spans[r]],
-                                  in_=h_b1[r][:].rearrange("p j t -> p (j t)"))
-        late = [table_passes(1, 1, t) for t in range(PACK)]
-        early_result = group_tile("b_early")
-        for t in range(EARLY_TILES):
-            close_second_step(0, 0, open_second_step(0, 0, [t]), [t], early_result)
-        ths.append(add_and_tanh(late, b_second[1], group_tile("th_first1"), "plane1"))
-        rest = range(EARLY_TILES, PACK)
-        close_second_step(0, 0, open_second_step(0, 0, rest), rest, group_tile("th_first1"))
-        close_second_step(0, 1, open_second_step(0, 1, range(PACK)), range(PACK), group_tile("plane0"))
-        last_step(b_second, ths)
+            gain_on_gpsimd(th_first[1], 1, h_b1[:, spans[r], :], spans[r])
+
+        def table_passes(g):
+            sums = [new_bank(t) for t in range(PACK)]
+            for t in range(PACK):
+                for a in range(PASSES):
+                    pass_wp(sums[t], 1, g, t, a, a == 0, a == PASSES - 1)
+            return sums
+
+        def keep_b(g, on_vector):
+            kept = group_tile("b_kept%d" % g)
+            for t in range(PACK):
+                bank = new_bank(PACK + t)
+                pass_b(bank, 1, g, t, True, True)
+                if t < on_vector:
+                    nc.vector.tensor_copy(kept[:, t, :], bank[:])
+                else:
+                    nc.scalar.copy(kept[:, t, :], bank[:])
+            return kept
+
+        def add_and_tanh(sums, kept, total, th):
+            for t0 in range(0, PACK, 2):
+                for t in range(t0, t0 + 2):
+                    nc.vector.tensor_tensor(total[:, t, :], sums[t][:], kept[:, t, :], ALU.add)
+                nc.scalar.activation(th[:, t0:t0 + 2, :], total[:, t0:t0 + 2, :], ACT.Tanh)
+            return th
+
+        early = table_passes(0)
+        b_kept = [keep_b(0, COPIES_ON_VECTOR), keep_b(1, 0)]
+        th_second = [add_and_tanh(early, b_kept[0], group_tile("plane0"), group_tile("plane2"))]
+        late = table_passes(1)
+        th_second.append(add_and_tanh(late, b_kept[1], group_tile("plane1"), group_tile("minus0")))
+        quantise(h_b1[:].rearrange("p j t -> p (j t)"), h_first[1])
+
+        def open_second_step(bank, g, t):
+            pass_b(bank, 0, g, t, True, False)
+            pass_wr(bank[:], g, t, 0, h_first[0][0][:], h_first[0][1][:], False, False)
+
+        def close_second_step(bank, g, t, result):
+            pass_wr(bank[:], g, t, 1, h_first[1][0][:], h_first[1][1][:], False, True)
+            nc.scalar.activation(result[:, t, :], bank[:], ACT.Tanh)
+            nc.sync.dma_start(out_rows[g][:, t, 0:W], result[:, t, :])
+
+        banks = [new_bank(PACK + t) for t in range(PACK)]
+        result = group_tile("diff0")
+        for t in range(PACK):
+            open_second_step(banks[t], 0, t)
+        for t in range(PACK):
+            close_second_step(banks[t], 0, t, result)
+        result = group_tile("tab_w0")
+        for t in range(PACK):
+            bank = new_bank(t)
+            open_second_step(bank, 1, t)
+            close_second_step(bank, 1, t, result)
+
+        rounded = sbuf([2, GROUPS, RUN, PACK], BF16, "minus1")
+        h_runs = [mx_tiles("h_run%d" % r) for r in range(2)]
+        for r in range(2):
+            gain_on_vector(th_second[0], 0, rounded[:, r, 0, :, :], spans[r])
+        for r in range(2):
+            gain_on_vector(th_second[1], 1, rounded[:, r, 1, :, :], spans[r])
+            quantise(rounded[:, r, :, :, :].rearrange("p g j t -> p (g j t)"), h_runs[r])
+        totals = [group_tile("tab_w1"), group_tile("wx_raw0")]
+        results = [group_tile("plane0"), group_tile("plane1")]
+        for r in range(2):
+            h_codes, h_scales = h_runs[r]
+            for k in range(PACK):
+                g, t0 = k // 2, 2 * (k % 2)
+                bank = new_bank((1 - r) * PACK + k)
+                for t in range(t0, t0 + 2):
+                    for a in range(GROUPS):
+                        pass_wr(bank[:, spans[t - t0]], g, t, a, h_codes[:, spans[a]], h_scales[:, spans[a]],
+                                a == 0, a == GROUPS - 1)
+                last = r == 1 and k == PACK - 1
+                for u in ((0, 1) if last else (None,)):
+                    rows = slice(t0, t0 + 2) if u is None else slice(t0 + u, t0 + u + 1)
+                    part = slice(0, W) if u is None else spans[u]
+                    total = totals[r][:, k, part].rearrange("p (t j) -> p t j", j=RUN)
+                    nc.vector.tensor_tensor(total, bank[:, part].rearrange("p (t j) -> p t j", j=RUN),
+                                            b_kept[g][:, rows, spans[r]], ALU.add)
+                    nc.scalar.activation(results[r][:, k, part], totals[r][:, k, part], ACT.Tanh)
+                    nc.sync.dma_start(out_rows[g][:, rows, W + r * RUN:W + (r + 1) * RUN],
+                                      results[r][:, k, part].rearrange("p (t j) -> p t j", j=RUN))

@@ -26,7 +26,7 @@ GROUPS = H // (P * PACK)
 PASSES = K // (P * PACK)
 BANKS = 8
 RUN = W // 2
-COPIES_ON_VECTOR = 2
+COPIES_ON_VECTOR = 1
 
 
 def tile_list_snowpack_recurrence_kernel(tc, tab_words, tab_scales, offs, xT, offs2, offs3, wp_words,
@@ -34,10 +34,14 @@ def tile_list_snowpack_recurrence_kernel(tc, tab_words, tab_scales, offs, xT, of
     nc = tc.nc
     with ExitStack() as ctx:
         keep = ctx.enter_context(tc.tile_pool(name="keep", bufs=1))
+        arena = ctx.enter_context(tc.tile_pool(name="arena", bufs=1))
         psum = ctx.enter_context(tc.psum_pool(name="psum", bufs=1))
 
+        def placed(shape, dtype, name, kib):
+            return arena.tile([P] + shape, dtype, name=name, align_bytes=256, offset=kib * 1024)
+
         def sbuf(shape, dtype, place):
-            return keep.tile([P] + shape, dtype, name=place, align_bytes=64)
+            return keep.tile([P] + shape, dtype, name=place, align_bytes=256)
 
         def group_tile(place):
             return sbuf([PACK, W], F32, place)
@@ -49,14 +53,15 @@ def tile_list_snowpack_recurrence_kernel(tc, tab_words, tab_scales, offs, xT, of
         ROW = H // 4
         tab_s = sbuf([T // 4], I32, "tab_s")
         w_s_raw = sbuf([ROW], I32, "w_s_raw")
-        scales = sbuf([5 * ROW], I32, "scales")
+        pass_s = [sbuf([2 * ROW], I32, "pass_s%d" % a) for a in range(PASSES)]
+        wr_s = sbuf([ROW], I32, "wr_s")
         nc.vector.memset(tab_s[32:64, :], 0)
         nc.vector.memset(tab_s[64:P, :], 0)
         nc.vector.memset(w_s_raw[64:P, :], 0)
-        nc.vector.memset(scales[:], 0)
-        scale_bytes = scales[:].bitcast(U8)
+        for plane in pass_s + [wr_s]:
+            nc.vector.memset(plane[:], 0)
 
-        wp_raw = sbuf([PASSES, H // 2], I32, "wp_raw")
+        wp_raw = placed([PASSES, H // 2], I32, "wp_raw", 7)
         planes = [sbuf([T], F32, "plane%d" % t) for t in range(PACK)]
         wx_raw = [group_tile("wx_raw%d" % g) for g in range(GROUPS)]
         tab_w = [sbuf([T], I32, "tab_w%d" % a) for a in range(PASSES)]
@@ -70,20 +75,21 @@ def tile_list_snowpack_recurrence_kernel(tc, tab_words, tab_scales, offs, xT, of
         def entries(list_tile, half):
             return list_tile[:, half * (W // STRIPE):(half + 1) * (W // STRIPE)]
 
-        minus = [group_tile("minus%d" % half) for half in range(HALVES)]
+        minus = {}
 
-        def gather_minus(half, t):
-            nc.vector.tensor_copy(minus[half][:, t, :], planes[t][:].indirect(entries(list_3, half)))
+        def gather_minus(half, t, place):
+            minus[half, t] = sbuf([W], F32, place)[:]
+            nc.vector.tensor_copy(minus[half, t], planes[t][:].indirect(entries(list_3, half)))
 
         def gather_diff(diff, half, t):
             nc.vector.tensor_tensor(diff[:, t, :], planes[t][:].indirect(entries(list_2, half)),
-                                    minus[half][:, t, :], ALU.subtract)
+                                    minus[half, t], ALU.subtract)
 
         def move_table_scales(queue, a, q):
-            queue.dma_start(scales[q:P:32, 2 * a * ROW:2 * (a + 1) * ROW], stage[16 * a + q:16 * a + 16:4, :])
+            queue.dma_start(pass_s[a][q:P:32, :], stage[16 * a + q:16 * a + 16:4, :])
 
         def move_wr_scales(a, q):
-            nc.sync.dma_start(scales[4 * a + q:P:32, 4 * ROW:5 * ROW],
+            nc.sync.dma_start(wr_s[4 * a + q:P:32, :],
                               stage[32 + 16 * a + q:32 + 16 * a + 16:4, ROW:2 * ROW])
 
         def load_plane(t):
@@ -98,21 +104,20 @@ def tile_list_snowpack_recurrence_kernel(tc, tab_words, tab_scales, offs, xT, of
                            wx_raw[g][:].rearrange("p j (m t) -> p m j t", t=PACK))
             return rounded[:]
 
-        def mx_tiles(name, codes_place=None):
-            return sbuf([W], U32, codes_place or name + "_codes"), sbuf([W], U8, name + "_scales")
+        def mx_tiles(name):
+            return sbuf([W], U32, name + "_codes"), sbuf([W], U8, name + "_scales")
 
         def quantise(rounded, operand):
             codes, block_scales = operand
             nc.vector.quantize_mx(out=codes[:].bitcast(FP8X4), scales=block_scales[:], in_=rounded)
 
-        def round_x(diff, place):
-            rounded = sbuf([W * PACK], BF16, place)
+        def round_x(diff, rounded):
             nc.scalar.copy(rounded[:].rearrange("p (c i t) -> p c t i", i=2, t=PACK),
                            diff[:].rearrange("p t (c i) -> p c t i", i=2))
             return rounded[:]
 
         def gather_v(words, half, a):
-            nc.vector.tensor_copy(words[:, a, :], tab_w[a][:].bitcast(U32).indirect(entries(list_v, half)))
+            nc.vector.tensor_copy(words[a], tab_w[a][:].bitcast(U32).indirect(entries(list_v, half)))
 
         def new_bank(k):
             return psum.tile([P, W], F32, name="bank%d" % k)
@@ -126,16 +131,16 @@ def tile_list_snowpack_recurrence_kernel(tc, tab_words, tab_scales, offs, xT, of
 
         def pass_wp(bank, half, g, t, a, start, stop):
             c0 = (g * PACK + t) * P
-            v_col, wp_col = 2 * a * H + half * W, (2 * a + 1) * H + c0
+            scale_bytes = pass_s[a][:].bitcast(U8)
             nc.tensor.matmul_mx(bank[:], lhsT=wp_c[:, a, 2 * c0:2 * (c0 + P)].bitcast(FP4X4),
-                                lhsT_scale=scale_bytes[:, wp_col:wp_col + P],
-                                rhs=v_c[half][:, a, :].bitcast(FP8X4), rhs_scale=scale_bytes[:, v_col:v_col + W],
+                                lhsT_scale=scale_bytes[:, S + c0:S + c0 + P],
+                                rhs=v_c[half][a].bitcast(FP8X4), rhs_scale=scale_bytes[:, half * W:(half + 1) * W],
                                 start=start, stop=stop)
 
         def pass_wr(sums, g, t, a, h_codes, h_scales, start, stop):
             c0 = (g * PACK + t) * P
             nc.tensor.matmul_mx(sums, lhsT=wr_c[:, a, c0:c0 + P].bitcast(FP8X4),
-                                lhsT_scale=scale_bytes[4 * a:P, 4 * H + c0:4 * H + c0 + P],
+                                lhsT_scale=wr_s[:].bitcast(U8)[4 * a:P, c0:c0 + P],
                                 rhs=h_codes.bitcast(FP8X4), rhs_scale=h_scales, start=start, stop=stop)
 
         def gain_on_gpsimd(th, g, rounded, cols):
@@ -157,115 +162,49 @@ def tile_list_snowpack_recurrence_kernel(tc, tab_words, tab_scales, offs, xT, of
 
         nc.sync.dma_start(list_v[:], offs)
         nc.sync.dma_start(tab_s[0:32, :], tab_scales.rearrange("a q n -> (a q) n").bitcast(I32))
+        nc.sync.dma_start(w_s_raw[0:32, :], wp_scales.rearrange("a q n -> (a q) n").bitcast(I32))
+        nc.sync.dma_start(w_s_raw[32:64, :], wr_scales.rearrange("a q n -> (a q) n").bitcast(I32))
         nc.sync.dma_start(list_3[:], offs3)
         load_plane(0)
         nc.sync.dma_start(list_2[:], offs2)
-        nc.sync.dma_start(w_s_raw[0:32, :], wp_scales.rearrange("a q n -> (a q) n").bitcast(I32))
-        nc.sync.dma_start(w_s_raw[32:64, :], wr_scales.rearrange("a q n -> (a q) n").bitcast(I32))
         nc.vector.tensor_copy(v_s_rows[:], tab_s[:].bitcast(U8).indirect(list_v[:]))
         load_plane(1)
-        load_wx(0)
         load_plane(2)
+        load_plane(3)
         diff0 = group_tile("diff0")
-        gather_minus(0, 0)
+        gather_minus(0, 0, "minus00")
         nc.vector.tensor_copy(stage[:, ROW:2 * ROW].bitcast(U8).rearrange("p (g t m) -> p g m t", m=P, t=PACK),
                               w_s_raw[:].bitcast(U8).rearrange("p (g m t) -> p g m t", m=P, t=PACK))
         nc.vector.tensor_copy(stage[:, 0:ROW], v_s_rows[:].bitcast(I32))
-        move_table_scales(nc.sync, 0, 0)
-        move_table_scales(nc.sync, 0, 1)
-        move_wr_scales(0, 0)
         for q in range(QUADRANTS):
-            move_table_scales(nc.gpsimd, 1, q)
-        load_wx(1)
+            move_table_scales(nc.sync, 0, q)
+        for q in range(2):
+            move_table_scales(nc.sync, 1, q)
+        load_wx(0)
+        for q in range(2, QUADRANTS):
+            move_table_scales(nc.sync, 1, q)
         nc.sync.dma_start(wp_raw[:], wp_words.rearrange("a p n -> p a n").bitcast(I32))
-        move_table_scales(nc.sync, 0, 2)
-        move_table_scales(nc.sync, 0, 3)
-        move_wr_scales(0, 1)
-        load_plane(3)
         for a in range(PASSES):
             nc.sync.dma_start(tab_w[a][:], tab_words[a].rearrange("p n t -> p (n t)").bitcast(I32))
-        move_wr_scales(0, 2)
-        move_wr_scales(0, 3)
-        for q in range(QUADRANTS):
-            move_wr_scales(1, q)
+        load_wx(1)
         nc.sync.dma_start(gain_sb[:], gain.rearrange("(g p t) -> p g t", g=GROUPS, t=PACK))
         nc.sync.dma_start(wr_raw[:], wr_words.rearrange("a p n t -> p a (n t)").bitcast(I32))
-
-        gather_minus(1, 0)
-        gather_diff(diff0, 0, 0)
-        for t in range(1, PACK - 1):
-            gather_minus(0, t)
-            gather_minus(1, t)
-            gather_diff(diff0, 0, t)
-            quantise(round_wx(t - 1), wx_q[t - 1])
-        wp_c = sbuf([PASSES, 2 * H], U8, "wp_c")
-        nc.scalar.copy(wp_c[:].bitcast(U16).rearrange("p a (g t m) -> p (a g) t m", g=GROUPS, t=PACK),
-                       wp_raw[:].bitcast(U16).rearrange("p a (g m t) -> p (a g) t m", g=GROUPS, t=PACK))
-        gather_minus(0, PACK - 1)
-        gather_diff(diff0, 0, PACK - 1)
-        gather_minus(1, PACK - 1)
-        v_c = [sbuf([PASSES, W], U32, "v_0")]
-        gather_v(v_c[0], 0, 0)
-        quantise(round_x(diff0, "x_b0"), x_q[0])
-        gather_v(v_c[0], 0, 1)
-        diff1 = group_tile("stage")
-        for t in range(PACK):
-            gather_diff(diff1, 1, t)
-
-        th_first = [group_tile("wx_raw%d" % g) for g in range(GROUPS)]
-        for t in range(PACK):
-            bank = new_bank(t)
-            pass_wp(bank, 0, 0, t, 0, True, False)
-            pass_b(bank, 0, 0, t, False, False)
-            pass_wp(bank, 0, 0, t, 1, False, True)
-            nc.scalar.activation(th_first[0][:, t, :], bank[:], ACT.Tanh)
-        by_tile = sbuf([PACK, RUN], BF16, "wx_b0")
-        for t in range(PACK):
-            nc.scalar.activation(by_tile[:, t, :], th_first[0][:, t, spans[1]], ACT.Copy,
-                                 scale=gain_sb[:, 0, t:t + 1])
-        banks = [new_bank(PACK + t) for t in range(PACK)]
-        for t in range(PACK):
-            for a in range(PASSES):
-                pass_wp(banks[t], 0, 1, t, a, a == 0, False)
-        x_b1 = round_x(diff1, "v_0")
-        for t in range(PACK):
-            pass_b(banks[t], 0, 1, t, False, True)
-            nc.scalar.activation(th_first[1][:, t, :], banks[t][:], ACT.Tanh)
-
-        v_c.append(sbuf([PASSES, W], U32, "plane3"))
-        for a in range(PASSES):
-            gather_v(v_c[1], 1, a)
-        h_b0 = sbuf([W, PACK], BF16, "minus1")
-        gain_on_gpsimd(th_first[0], 0, h_b0[:, spans[0], :], spans[0])
-        nc.vector.tensor_copy(h_b0[:, spans[1], :].rearrange("p (c i) t -> p c t i", i=4),
-                              by_tile[:].rearrange("p t (c i) -> p c t i", i=4))
-        quantise(x_b1, x_q[1])
-        wr_c = sbuf([GROUPS, H], I32, "v_0")
-        nc.vector.tensor_copy(wr_c[:].rearrange("p a (g t m) -> p (a g) m t", g=GROUPS, t=PACK),
-                              wr_raw[:].rearrange("p a (g m t) -> p (a g) m t", g=GROUPS, t=PACK))
-        h_first = [mx_tiles("h0", "wr_raw"), mx_tiles("h1")]
-        quantise(h_b0[:].rearrange("p j t -> p (j t)"), h_first[0])
-        h_b1 = sbuf([W, PACK], BF16, "minus1")
-        for r in range(2):
-            gain_on_gpsimd(th_first[1], 1, h_b1[:, spans[r], :], spans[r])
+        for a in range(GROUPS):
+            for q in range(QUADRANTS):
+                move_wr_scales(a, q)
 
         def table_passes(g):
             sums = [new_bank(t) for t in range(PACK)]
-            for t in range(PACK):
-                for a in range(PASSES):
-                    pass_wp(sums[t], 1, g, t, a, a == 0, a == PASSES - 1)
+            order = [(t, a) for t in range(PACK) for a in range(PASSES)]
+            for t, a in (sorted(order, key=lambda ta: ta[1]) if g == 0 else order):
+                pass_wp(sums[t], 1, g, t, a, a == 0, a == PASSES - 1)
             return sums
 
-        def keep_b(g, on_vector):
-            kept = group_tile("b_kept%d" % g)
-            for t in range(PACK):
+        def keep_b(g, tiles, copy):
+            for t in tiles:
                 bank = new_bank(PACK + t)
                 pass_b(bank, 1, g, t, True, True)
-                if t < on_vector:
-                    nc.vector.tensor_copy(kept[:, t, :], bank[:])
-                else:
-                    nc.scalar.copy(kept[:, t, :], bank[:])
-            return kept
+                copy(b_kept[g][:, t, :], bank[:])
 
         def add_and_tanh(sums, kept, total, th):
             for t0 in range(0, PACK, 2):
@@ -274,48 +213,110 @@ def tile_list_snowpack_recurrence_kernel(tc, tab_words, tab_scales, offs, xT, of
                 nc.scalar.activation(th[:, t0:t0 + 2, :], total[:, t0:t0 + 2, :], ACT.Tanh)
             return th
 
+        def open_second_step(g, tiles):
+            banks = {t: new_bank(PACK * (1 - g) + t) for t in tiles}
+            for t in tiles:
+                pass_b(banks[t], 0, g, t, True, False)
+                pass_wr(banks[t][:], g, t, 0, h_first[0][0][:], h_first[0][1][:], False, False)
+            return banks
+
+        def close_second_step(g, banks, result):
+            for t in banks:
+                pass_wr(banks[t][:], g, t, 1, h_first[1][0][:], h_first[1][1][:], False, True)
+                nc.scalar.activation(result[:, t, :], banks[t][:], ACT.Tanh)
+                nc.sync.dma_start(out_rows[g][:, t, 0:W], result[:, t, :])
+
+        for t in range(PACK):
+            if t > 0:
+                gather_minus(0, t, "minus0%d" % t)
+            if t < 2:
+                gather_minus(1, t, "minus1%d" % t)
+            gather_diff(diff0, 0, t)
+        wx_b0 = round_wx(0)
+        wp_c = sbuf([PASSES, 2 * H], U8, "wp_c")
+        nc.scalar.copy(wp_c[:].bitcast(U16).rearrange("p a (g t m) -> p (a g) t m", g=GROUPS, t=PACK),
+                       wp_raw[:].bitcast(U16).rearrange("p a (g m t) -> p (a g) t m", g=GROUPS, t=PACK))
+        v_c = [[sbuf([W], U32, "v_0%d" % a)[:] for a in range(PASSES)]]
+        gather_v(v_c[0], 0, 0)
+        quantise(wx_b0, wx_q[0])
+        gather_v(v_c[0], 0, 1)
+        quantise(round_x(diff0, placed([W * PACK], BF16, "x_b0", 7)), x_q[0])
+        held = placed([2, W], F32, "held", 4)
+        for t in range(2, PACK):
+            minus[1, t] = held[:, t - 2, :]
+            nc.vector.tensor_copy(minus[1, t], planes[t][:].indirect(entries(list_3, 1)))
+        v_c.append([placed([W], U32, "v_10", 8)[:]])
+        gather_v(v_c[1], 1, 0)
+        wx_b1 = placed([W * PACK], BF16, "wx_b1", 10)
+        nc.gpsimd.tensor_scalar(wx_b1[:].rearrange("p (t m j) -> p t m j", t=PACK, j=PACK),
+                                wx_raw[1][:].rearrange("p j (m t) -> p t m j", t=PACK), 1.0, 0.0, ALU.mult, ALU.add)
+        quantise(wx_b1[:], wx_q[1])
+        diff1 = placed([PACK, W], F32, "diff1", 10)
+        for t in range(PACK):
+            gather_diff(diff1, 1, t)
+
+        def first_step(g):
+            th = group_tile("th_first%d" % g)
+            banks = [new_bank(t) for t in range(PACK)]
+            for tiles in ([[t] for t in range(PACK)] if g == 0 else [range(PACK)]):
+                for t in tiles:
+                    for a in range(PASSES):
+                        pass_wp(banks[t], 0, g, t, a, a == 0, False)
+                for t in tiles:
+                    pass_b(banks[t], 0, g, t, False, True)
+                    nc.scalar.activation(th[:, t, :], banks[t][:], ACT.Tanh)
+            return th
+
+        th_first = [first_step(0)]
+        by_tile = sbuf([PACK, W], BF16, "by_tile")
+        for t in range(PACK):
+            nc.scalar.activation(by_tile[:, t, :], th_first[0][:, t, :], ACT.Copy, scale=gain_sb[:, 0, t:t + 1])
+        th_first.append(first_step(1))
+        v_c[1].append(sbuf([W], U32, "plane3")[:])
+        gather_v(v_c[1], 1, 1)
+        h_b1 = [placed([RUN, PACK], BF16, "h_b1a", 4)]
+        gain_on_gpsimd(th_first[1], 1, h_b1[0][:], spans[0])
+        quantise(round_x(diff1, sbuf([W * PACK], BF16, "th_first0")), x_q[1])
+        wr_c = sbuf([GROUPS, H], I32, "th_first0")
+        nc.vector.tensor_copy(wr_c[:].rearrange("p a (g t m) -> p (a g) m t", g=GROUPS, t=PACK),
+                              wr_raw[:].rearrange("p a (g m t) -> p (a g) m t", g=GROUPS, t=PACK))
+        h_b0 = placed([W, PACK], BF16, "h_b0", 10)
+        nc.scalar.copy(h_b0[:].rearrange("p (c i) t -> p c t i", i=4),
+                       by_tile[:].rearrange("p t (c i) -> p c t i", i=4))
+        h_first = [(sbuf([W], U32, "wr_raw"), sbuf([W], U8, "h0_scales")), mx_tiles("h1")]
+        quantise(h_b0[:].rearrange("p j t -> p (j t)"), h_first[0])
+        h_b1.append(placed([RUN, PACK], BF16, "h_b1b", 10))
+        gain_on_gpsimd(th_first[1], 1, h_b1[1][:], spans[1])
         early = table_passes(0)
-        b_kept = [keep_b(0, COPIES_ON_VECTOR), keep_b(1, 0)]
-        th_second = [add_and_tanh(early, b_kept[0], group_tile("plane0"), group_tile("plane2"))]
+        b_kept = [group_tile("b_kept%d" % g) for g in range(GROUPS)]
+
+        keep_b(0, range(PACK), nc.scalar.copy)
+        keep_b(1, range(PACK - COPIES_ON_VECTOR), nc.scalar.copy)
+        th_second = [add_and_tanh(early, b_kept[0], group_tile("total"), group_tile("plane0"))]
+        keep_b(1, range(PACK - COPIES_ON_VECTOR, PACK), nc.vector.tensor_copy)
+        for r in range(2):
+            nc.vector.quantize_mx(out=h_first[1][0][:, spans[r]].bitcast(FP8X4), scales=h_first[1][1][:, spans[r]],
+                                  in_=h_b1[r][:].rearrange("p j t -> p (j t)"))
         late = table_passes(1)
-        th_second.append(add_and_tanh(late, b_kept[1], group_tile("plane1"), group_tile("minus0")))
-        quantise(h_b1[:].rearrange("p j t -> p (j t)"), h_first[1])
+        close_second_step(0, open_second_step(0, [0]), group_tile("diff0"))
+        th_second.append(add_and_tanh(late, b_kept[1], group_tile("wx_raw0"), group_tile("plane1")))
+        close_second_step(0, open_second_step(0, range(1, PACK)), group_tile("wx_raw0"))
+        close_second_step(1, open_second_step(1, range(PACK)), group_tile("plane2"))
 
-        def open_second_step(bank, g, t):
-            pass_b(bank, 0, g, t, True, False)
-            pass_wr(bank[:], g, t, 0, h_first[0][0][:], h_first[0][1][:], False, False)
-
-        def close_second_step(bank, g, t, result):
-            pass_wr(bank[:], g, t, 1, h_first[1][0][:], h_first[1][1][:], False, True)
-            nc.scalar.activation(result[:, t, :], bank[:], ACT.Tanh)
-            nc.sync.dma_start(out_rows[g][:, t, 0:W], result[:, t, :])
-
-        banks = [new_bank(PACK + t) for t in range(PACK)]
-        result = group_tile("diff0")
-        for t in range(PACK):
-            open_second_step(banks[t], 0, t)
-        for t in range(PACK):
-            close_second_step(banks[t], 0, t, result)
-        result = group_tile("tab_w0")
-        for t in range(PACK):
-            bank = new_bank(t)
-            open_second_step(bank, 1, t)
-            close_second_step(bank, 1, t, result)
-
-        rounded = sbuf([2, GROUPS, RUN, PACK], BF16, "minus1")
+        rounded = [placed([GROUPS, RUN, PACK], BF16, "h_run0", 10)[:], sbuf([GROUPS, RUN, PACK], BF16, "plane3")[:]]
         h_runs = [mx_tiles("h_run%d" % r) for r in range(2)]
+        gain_on_gpsimd(th_second[0], 0, rounded[0][:, 0, :, :], spans[0])
+        gain_on_vector(th_second[0], 0, rounded[1][:, 0, :, :], spans[1])
         for r in range(2):
-            gain_on_vector(th_second[0], 0, rounded[:, r, 0, :, :], spans[r])
-        for r in range(2):
-            gain_on_vector(th_second[1], 1, rounded[:, r, 1, :, :], spans[r])
-            quantise(rounded[:, r, :, :, :].rearrange("p g j t -> p (g j t)"), h_runs[r])
-        totals = [group_tile("tab_w1"), group_tile("wx_raw0")]
-        results = [group_tile("plane0"), group_tile("plane1")]
+            gain_on_vector(th_second[1], 1, rounded[r][:, 1, :, :], spans[r])
+            quantise(rounded[r].rearrange("p g j t -> p (g j t)"), h_runs[r])
+        totals = [group_tile("total"), group_tile("tab_w0")]
+        results = [group_tile("plane1"), group_tile("plane0")]
         for r in range(2):
             h_codes, h_scales = h_runs[r]
             for k in range(PACK):
                 g, t0 = k // 2, 2 * (k % 2)
-                bank = new_bank((1 - r) * PACK + k)
+                bank = new_bank(PACK * (1 - r) + k)
                 for t in range(t0, t0 + 2):
                     for a in range(GROUPS):
                         pass_wr(bank[:, spans[t - t0]], g, t, a, h_codes[:, spans[a]], h_scales[:, spans[a]],

@@ -26,6 +26,7 @@ GROUPS = H // (P * PACK)
 PASSES = K // (P * PACK)
 BANKS = 8
 RUN = W // 2
+EARLY_COPIES = 1
 COPIES_ON_VECTOR = 1
 
 
@@ -63,7 +64,7 @@ def tile_list_snowpack_recurrence_kernel(tc, tab_words, tab_scales, offs, xT, of
 
         wp_raw = placed([PASSES, H // 2], I32, "wp_raw", 7)
         planes = [sbuf([T], F32, "plane%d" % t) for t in range(PACK)]
-        wx_raw = [group_tile("wx_raw%d" % g) for g in range(GROUPS)]
+        wx_raw = [group_tile("wx_raw0"), group_tile("th_first0")]
         tab_w = [sbuf([T], I32, "tab_w%d" % a) for a in range(PASSES)]
         wr_raw = sbuf([GROUPS, H], I32, "wr_raw")
         gain_sb = keep.tile([P, GROUPS, PACK], F32, name="gain_sb")
@@ -248,8 +249,8 @@ def tile_list_snowpack_recurrence_kernel(tc, tab_words, tab_scales, offs, xT, of
         v_c.append([placed([W], U32, "v_10", 8)[:]])
         gather_v(v_c[1], 1, 0)
         wx_b1 = placed([W * PACK], BF16, "wx_b1", 10)
-        nc.gpsimd.tensor_scalar(wx_b1[:].rearrange("p (t m j) -> p t m j", t=PACK, j=PACK),
-                                wx_raw[1][:].rearrange("p j (m t) -> p t m j", t=PACK), 1.0, 0.0, ALU.mult, ALU.add)
+        nc.scalar.copy(wx_b1[:].rearrange("p (t m j) -> p m j t", t=PACK, j=PACK),
+                       wx_raw[1][:].rearrange("p j (m t) -> p m j t", t=PACK))
         quantise(wx_b1[:], wx_q[1])
         diff1 = placed([PACK, W], F32, "diff1", 10)
         for t in range(PACK):
@@ -283,14 +284,15 @@ def tile_list_snowpack_recurrence_kernel(tc, tab_words, tab_scales, offs, xT, of
         h_b0 = placed([W, PACK], BF16, "h_b0", 10)
         nc.scalar.copy(h_b0[:].rearrange("p (c i) t -> p c t i", i=4),
                        by_tile[:].rearrange("p t (c i) -> p c t i", i=4))
+        early = table_passes(0)
+        b_kept = [group_tile("b_kept%d" % g) for g in range(GROUPS)]
+        keep_b(0, range(EARLY_COPIES), nc.vector.tensor_copy)
         h_first = [(sbuf([W], U32, "wr_raw"), sbuf([W], U8, "h0_scales")), mx_tiles("h1")]
         quantise(h_b0[:].rearrange("p j t -> p (j t)"), h_first[0])
         h_b1.append(placed([RUN, PACK], BF16, "h_b1b", 10))
         gain_on_gpsimd(th_first[1], 1, h_b1[1][:], spans[1])
-        early = table_passes(0)
-        b_kept = [group_tile("b_kept%d" % g) for g in range(GROUPS)]
 
-        keep_b(0, range(PACK), nc.scalar.copy)
+        keep_b(0, range(EARLY_COPIES, PACK), nc.scalar.copy)
         keep_b(1, range(PACK - COPIES_ON_VECTOR), nc.scalar.copy)
         th_second = [add_and_tanh(early, b_kept[0], group_tile("total"), group_tile("plane0"))]
         keep_b(1, range(PACK - COPIES_ON_VECTOR, PACK), nc.vector.tensor_copy)

@@ -26,8 +26,9 @@ GROUPS = H // (P * PACK)
 PASSES = K // (P * PACK)
 BANKS = 8
 RUN = W // 2
-EARLY_COPIES = 1
-COPIES_ON_VECTOR = 1
+EARLY_COPIES = 2
+GAIN_TILES_ON_VECTOR = 2
+COPIES_ON_VECTOR = 0
 
 
 def tile_list_snowpack_recurrence_kernel(tc, tab_words, tab_scales, offs, xT, offs2, offs3, wp_words,
@@ -237,7 +238,7 @@ def tile_list_snowpack_recurrence_kernel(tc, tab_words, tab_scales, offs, xT, of
         wp_c = sbuf([PASSES, 2 * H], U8, "wp_c")
         nc.scalar.copy(wp_c[:].bitcast(U16).rearrange("p a (g t m) -> p (a g) t m", g=GROUPS, t=PACK),
                        wp_raw[:].bitcast(U16).rearrange("p a (g m t) -> p (a g) t m", g=GROUPS, t=PACK))
-        v_c = [[sbuf([W], U32, "v_0%d" % a)[:] for a in range(PASSES)]]
+        v_c = [[sbuf([W], U32, "v_00")[:], placed([W], U32, "v_01", 0)[:]]]
         gather_v(v_c[0], 0, 0)
         quantise(wx_b0, wx_q[0])
         gather_v(v_c[0], 0, 1)
@@ -246,8 +247,6 @@ def tile_list_snowpack_recurrence_kernel(tc, tab_words, tab_scales, offs, xT, of
         for t in range(2, PACK):
             minus[1, t] = held[:, t - 2, :]
             nc.vector.tensor_copy(minus[1, t], planes[t][:].indirect(entries(list_3, 1)))
-        v_c.append([placed([W], U32, "v_10", 8)[:]])
-        gather_v(v_c[1], 1, 0)
         wx_b1 = placed([W * PACK], BF16, "wx_b1", 10)
         nc.scalar.copy(wx_b1[:].rearrange("p (t m j) -> p m j t", t=PACK, j=PACK),
                        wx_raw[1][:].rearrange("p j (m t) -> p m j t", t=PACK))
@@ -259,60 +258,75 @@ def tile_list_snowpack_recurrence_kernel(tc, tab_words, tab_scales, offs, xT, of
         def first_step(g):
             th = group_tile("th_first%d" % g)
             banks = [new_bank(t) for t in range(PACK)]
-            for tiles in ([[t] for t in range(PACK)] if g == 0 else [range(PACK)]):
-                for t in tiles:
-                    for a in range(PASSES):
+            ahead = [(t, a) for t in range(PACK) for a in range(PASSES)][:-1] if g == 1 else []
+            for t, a in ahead:
+                pass_wp(banks[t], 0, g, t, a, a == 0, False)
+            for t in range(PACK):
+                for a in range(PASSES):
+                    if (t, a) not in ahead:
                         pass_wp(banks[t], 0, g, t, a, a == 0, False)
-                for t in tiles:
-                    pass_b(banks[t], 0, g, t, False, True)
-                    nc.scalar.activation(th[:, t, :], banks[t][:], ACT.Tanh)
+                pass_b(banks[t], 0, g, t, False, True)
+                nc.scalar.activation(th[:, t, :], banks[t][:], ACT.Tanh)
             return th
 
         th_first = [first_step(0)]
         by_tile = sbuf([PACK, W], BF16, "by_tile")
-        for t in range(PACK):
+        for t in range(PACK - GAIN_TILES_ON_VECTOR):
             nc.scalar.activation(by_tile[:, t, :], th_first[0][:, t, :], ACT.Copy, scale=gain_sb[:, 0, t:t + 1])
+        for t in range(PACK - GAIN_TILES_ON_VECTOR, PACK):
+            nc.vector.tensor_scalar(by_tile[:, t, :], th_first[0][:, t, :], gain_sb[:, 0, t:t + 1], None, ALU.mult)
         th_first.append(first_step(1))
-        v_c[1].append(sbuf([W], U32, "plane3")[:])
-        gather_v(v_c[1], 1, 1)
-        h_b1 = [placed([RUN, PACK], BF16, "h_b1a", 4)]
-        gain_on_gpsimd(th_first[1], 1, h_b1[0][:], spans[0])
-        quantise(round_x(diff1, sbuf([W * PACK], BF16, "th_first0")), x_q[1])
-        wr_c = sbuf([GROUPS, H], I32, "th_first0")
+        v_c.append([sbuf([W], U32, "plane2")[:]])
+        gather_v(v_c[1], 1, 0)
+        wr_c = sbuf([GROUPS, H], I32, "plane3")
         nc.vector.tensor_copy(wr_c[:].rearrange("p a (g t m) -> p (a g) m t", g=GROUPS, t=PACK),
                               wr_raw[:].rearrange("p a (g m t) -> p (a g) m t", g=GROUPS, t=PACK))
+        quantise(round_x(diff1, placed([W * PACK], BF16, "x_b1", 0)), x_q[1])
+        v_c[1].append(placed([W], U32, "v_11", 0)[:])
+        gather_v(v_c[1], 1, 1)
+        h_b1 = [placed([RUN, PACK], BF16, "h_b1a", 2)]
+        gain_on_gpsimd(th_first[1], 1, h_b1[0][:], spans[0])
         h_b0 = placed([W, PACK], BF16, "h_b0", 10)
         nc.scalar.copy(h_b0[:].rearrange("p (c i) t -> p c t i", i=4),
                        by_tile[:].rearrange("p t (c i) -> p c t i", i=4))
-        early = table_passes(0)
+        early = [new_bank(t) for t in range(PACK)]
+        for t in range(PACK):
+            pass_wp(early[t], 1, 0, t, 0, True, False)
         b_kept = [group_tile("b_kept%d" % g) for g in range(GROUPS)]
         keep_b(0, range(EARLY_COPIES), nc.vector.tensor_copy)
-        h_first = [(sbuf([W], U32, "wr_raw"), sbuf([W], U8, "h0_scales")), mx_tiles("h1")]
+        keep_b(0, range(EARLY_COPIES, PACK), nc.scalar.copy)
+        for t in range(PACK):
+            pass_wp(early[t], 1, 0, t, 1, False, True)
+        h1_q = mx_tiles("h1")
+
+        def quantise_run(r):
+            nc.vector.quantize_mx(out=h1_q[0][:, spans[r]].bitcast(FP8X4), scales=h1_q[1][:, spans[r]],
+                                  in_=h_b1[r][:].rearrange("p j t -> p (j t)"))
+
+        quantise_run(0)
+        h_first = [(placed([W], U32, "h0_codes", 2), sbuf([W], U8, "h0_scales")), h1_q]
         quantise(h_b0[:].rearrange("p j t -> p (j t)"), h_first[0])
         h_b1.append(placed([RUN, PACK], BF16, "h_b1b", 10))
         gain_on_gpsimd(th_first[1], 1, h_b1[1][:], spans[1])
 
-        keep_b(0, range(EARLY_COPIES, PACK), nc.scalar.copy)
         keep_b(1, range(PACK - COPIES_ON_VECTOR), nc.scalar.copy)
-        th_second = [add_and_tanh(early, b_kept[0], group_tile("total"), group_tile("plane0"))]
+        th_second = [add_and_tanh(early, b_kept[0], placed([PACK, W], F32, "total0", 12), group_tile("plane0"))]
         keep_b(1, range(PACK - COPIES_ON_VECTOR, PACK), nc.vector.tensor_copy)
-        for r in range(2):
-            nc.vector.quantize_mx(out=h_first[1][0][:, spans[r]].bitcast(FP8X4), scales=h_first[1][1][:, spans[r]],
-                                  in_=h_b1[r][:].rearrange("p j t -> p (j t)"))
+        quantise_run(1)
         late = table_passes(1)
         close_second_step(0, open_second_step(0, [0]), group_tile("diff0"))
         th_second.append(add_and_tanh(late, b_kept[1], group_tile("wx_raw0"), group_tile("plane1")))
         close_second_step(0, open_second_step(0, range(1, PACK)), group_tile("wx_raw0"))
-        close_second_step(1, open_second_step(1, range(PACK)), group_tile("plane2"))
+        close_second_step(1, open_second_step(1, range(PACK)), group_tile("tab_w0"))
 
-        rounded = [placed([GROUPS, RUN, PACK], BF16, "h_run0", 10)[:], sbuf([GROUPS, RUN, PACK], BF16, "plane3")[:]]
+        rounded = [placed([GROUPS, RUN, PACK], BF16, "h_run0", 10)[:], sbuf([GROUPS, RUN, PACK], BF16, "tab_w1")[:]]
         h_runs = [mx_tiles("h_run%d" % r) for r in range(2)]
         gain_on_gpsimd(th_second[0], 0, rounded[0][:, 0, :, :], spans[0])
         gain_on_vector(th_second[0], 0, rounded[1][:, 0, :, :], spans[1])
         for r in range(2):
             gain_on_vector(th_second[1], 1, rounded[r][:, 1, :, :], spans[r])
             quantise(rounded[r].rearrange("p g j t -> p (g j t)"), h_runs[r])
-        totals = [group_tile("total"), group_tile("tab_w0")]
+        totals = [group_tile("total"), group_tile("plane2")]
         results = [group_tile("plane1"), group_tile("plane0")]
         for r in range(2):
             h_codes, h_scales = h_runs[r]

@@ -26,9 +26,8 @@ GROUPS = H // (P * PACK)
 PASSES = K // (P * PACK)
 BANKS = 8
 RUN = W // 2
-EARLY_COPIES = 2
-GAIN_TILES_ON_VECTOR = 2
-COPIES_ON_VECTOR = 0
+EARLY_RESULTS = 1
+ROW = H // 4
 
 
 def tile_list_snowpack_recurrence_kernel(tc, tab_words, tab_scales, offs, xT, offs2, offs3, wp_words,
@@ -42,17 +41,20 @@ def tile_list_snowpack_recurrence_kernel(tc, tab_words, tab_scales, offs, xT, of
         def placed(shape, dtype, name, kib):
             return arena.tile([P] + shape, dtype, name=name, align_bytes=256, offset=kib * 1024)
 
-        def sbuf(shape, dtype, place):
-            return keep.tile([P] + shape, dtype, name=place, align_bytes=256)
+        def sbuf(shape, dtype, name):
+            return keep.tile([P] + shape, dtype, name=name, align_bytes=256)
 
-        def group_tile(place):
-            return sbuf([PACK, W], F32, place)
+        def group_tile(name, kib):
+            return placed([PACK, W], F32, name, kib)
+
+        def mx_tiles(name, kib=None):
+            codes = sbuf([W], U32, name + "_codes") if kib is None else placed([W], U32, name + "_codes", kib)
+            return codes, sbuf([W], U8, name + "_scales")
 
         list_v = keep.tile([P, S // STRIPE], U16, name="list_v")
         list_2 = keep.tile([P, S // STRIPE], U16, name="list_2")
         list_3 = keep.tile([P, S // STRIPE], U16, name="list_3")
 
-        ROW = H // 4
         tab_s = sbuf([T // 4], I32, "tab_s")
         w_s_raw = sbuf([ROW], I32, "w_s_raw")
         pass_s = [sbuf([2 * ROW], I32, "pass_s%d" % a) for a in range(PASSES)]
@@ -62,81 +64,77 @@ def tile_list_snowpack_recurrence_kernel(tc, tab_words, tab_scales, offs, xT, of
         nc.vector.memset(w_s_raw[64:P, :], 0)
         for plane in pass_s + [wr_s]:
             nc.vector.memset(plane[:], 0)
-
-        wp_raw = placed([PASSES, H // 2], I32, "wp_raw", 7)
-        planes = [sbuf([T], F32, "plane%d" % t) for t in range(PACK)]
-        wx_raw = [group_tile("wx_raw0"), group_tile("th_first0")]
-        tab_w = [sbuf([T], I32, "tab_w%d" % a) for a in range(PASSES)]
-        wr_raw = sbuf([GROUPS, H], I32, "wr_raw")
-        gain_sb = keep.tile([P, GROUPS, PACK], F32, name="gain_sb")
-        x_rows = xT.rearrange("(p t) n -> t p n", t=PACK)
-        wx_rows = wx.rearrange("(p j) c -> p j c", j=PACK)
         v_s_rows = sbuf([S], U8, "v_s_rows")
         stage = sbuf([2 * ROW], I32, "stage")
+        gain_sb = keep.tile([P, GROUPS, PACK], F32, name="gain_sb")
+
+        planes = [placed([T], F32, "plane%d" % t, 8 * t) for t in range(PACK)]
+        wx_raw = [group_tile("wx_raw%d" % g, 32 + 8 * g) for g in range(GROUPS)]
+        tab_w = [placed([T], I32, "tab_w%d" % a, 48 + 8 * a) for a in range(PASSES)]
+        wr_raw = placed([GROUPS, H], I32, "wr_raw", 65)
+        wp_raw = placed([PASSES, H // 2], I32, "wp_raw", 179)
+        x_rows = xT.rearrange("(p t) n -> t p n", t=PACK)
+        wx_rows = wx.rearrange("(p j) c -> p j c", j=PACK)
+        out_rows = out.rearrange("(g p t) j -> g p t j", g=GROUPS, t=PACK)
+        spans = [slice(r * RUN, (r + 1) * RUN) for r in range(2)]
 
         def entries(list_tile, half):
             return list_tile[:, half * (W // STRIPE):(half + 1) * (W // STRIPE)]
 
-        minus = {}
+        def gather_minus(minus, half, t):
+            nc.vector.tensor_copy(minus, planes[t][:].indirect(entries(list_3, half)))
 
-        def gather_minus(half, t, place):
-            minus[half, t] = sbuf([W], F32, place)[:]
-            nc.vector.tensor_copy(minus[half, t], planes[t][:].indirect(entries(list_3, half)))
+        def gather_diff(diff, minus, half, t):
+            nc.vector.tensor_tensor(diff, planes[t][:].indirect(entries(list_2, half)), minus, ALU.subtract)
 
-        def gather_diff(diff, half, t):
-            nc.vector.tensor_tensor(diff[:, t, :], planes[t][:].indirect(entries(list_2, half)),
-                                    minus[half, t], ALU.subtract)
+        def gather_v(words, half, a):
+            nc.vector.tensor_copy(words[:], tab_w[a][:].bitcast(U32).indirect(entries(list_v, half)))
 
-        def move_table_scales(queue, a, q):
-            queue.dma_start(pass_s[a][q:P:32, :], stage[16 * a + q:16 * a + 16:4, :])
+        def move_table_scales(a, q):
+            nc.sync.dma_start(pass_s[a][q:P:32, :], stage[16 * a + q:16 * a + 16:4, :])
 
         def move_wr_scales(a, q):
-            nc.sync.dma_start(wr_s[4 * a + q:P:32, :],
-                              stage[32 + 16 * a + q:32 + 16 * a + 16:4, ROW:2 * ROW])
+            nc.sync.dma_start(wr_s[4 * a + q:P:32, :], stage[32 + 16 * a + q:32 + 16 * a + 16:4, ROW:2 * ROW])
 
         def load_plane(t):
             nc.sync.dma_start(planes[t][:], x_rows[t])
 
+        def load_table(a):
+            nc.sync.dma_start(tab_w[a][:], tab_words[a].rearrange("p n t -> p (n t)").bitcast(I32))
+
         def load_wx(g):
             nc.sync.dma_start(wx_raw[g][:], wx_rows[:, :, g * W:(g + 1) * W])
 
-        def round_wx(g):
-            rounded = sbuf([W * PACK], BF16, "wx_b%d" % g)
+        def round_wx(g, kib):
+            rounded = placed([W * PACK], BF16, "wx_b%d" % g, kib)
             nc.scalar.copy(rounded[:].rearrange("p (t m j) -> p m j t", t=PACK, j=PACK),
                            wx_raw[g][:].rearrange("p j (m t) -> p m j t", t=PACK))
             return rounded[:]
 
-        def mx_tiles(name):
-            return sbuf([W], U32, name + "_codes"), sbuf([W], U8, name + "_scales")
+        def quantise(rounded, codes, block_scales):
+            nc.vector.quantize_mx(out=codes.bitcast(FP8X4), scales=block_scales, in_=rounded)
 
-        def quantise(rounded, operand):
-            codes, block_scales = operand
-            nc.vector.quantize_mx(out=codes[:].bitcast(FP8X4), scales=block_scales[:], in_=rounded)
-
-        def round_x(diff, rounded):
-            nc.scalar.copy(rounded[:].rearrange("p (c i t) -> p c t i", i=2, t=PACK),
-                           diff[:].rearrange("p t (c i) -> p c t i", i=2))
-            return rounded[:]
-
-        def gather_v(words, half, a):
-            nc.vector.tensor_copy(words[a], tab_w[a][:].bitcast(U32).indirect(entries(list_v, half)))
+        def interleave(copy, rows, words, step):
+            copy(words[:].rearrange("p (c i t) -> p c t i", i=step, t=PACK),
+                 rows[:].rearrange("p t (c i) -> p c t i", i=step))
+            return words[:]
 
         def new_bank(k):
             return psum.tile([P, W], F32, name="bank%d" % k)
 
-        def pass_b(bank, half, g, t, start, stop):
+        def pass_b(sums, half, g, t, span, start, stop):
             cols = slice(t * P, (t + 1) * P)
             wx_codes, wx_scales = wx_q[g]
             x_codes, x_scales = x_q[half]
-            nc.tensor.matmul_mx(bank[:], lhsT=wx_codes[:, cols].bitcast(FP8X4), lhsT_scale=wx_scales[:, cols],
-                                rhs=x_codes[:].bitcast(FP8X4), rhs_scale=x_scales[:], start=start, stop=stop)
+            nc.tensor.matmul_mx(sums, lhsT=wx_codes[:, cols].bitcast(FP8X4), lhsT_scale=wx_scales[:, cols],
+                                rhs=x_codes[:, span].bitcast(FP8X4), rhs_scale=x_scales[:, span], start=start, stop=stop)
 
         def pass_wp(bank, half, g, t, a, start, stop):
             c0 = (g * PACK + t) * P
             scale_bytes = pass_s[a][:].bitcast(U8)
             nc.tensor.matmul_mx(bank[:], lhsT=wp_c[:, a, 2 * c0:2 * (c0 + P)].bitcast(FP4X4),
                                 lhsT_scale=scale_bytes[:, S + c0:S + c0 + P],
-                                rhs=v_c[half][a].bitcast(FP8X4), rhs_scale=scale_bytes[:, half * W:(half + 1) * W],
+                                rhs=v_c[half][a][:].bitcast(FP8X4), rhs_scale=scale_bytes[:, half * W:(half + 1) * W],
                                 start=start, stop=stop)
 
         def pass_wr(sums, g, t, a, h_codes, h_scales, start, stop):
@@ -146,21 +144,14 @@ def tile_list_snowpack_recurrence_kernel(tc, tab_words, tab_scales, offs, xT, of
                                 rhs=h_codes.bitcast(FP8X4), rhs_scale=h_scales, start=start, stop=stop)
 
         def gain_on_gpsimd(th, g, rounded, cols):
-            count = cols.stop - cols.start
             nc.gpsimd.tensor_tensor(rounded, th[:, :, cols].rearrange("p t c -> p c t"),
-                                    gain_sb[:, g, :].unsqueeze(1).to_broadcast([P, count, PACK]), ALU.mult)
+                                    gain_sb[:, g, :].unsqueeze(1).to_broadcast([P, RUN, PACK]), ALU.mult)
 
         def gain_on_vector(th, g, rounded, cols):
-            pairs = (cols.stop - cols.start) // 2
             nc.vector.tensor_tensor(rounded.rearrange("p (c i) t -> p c t i", i=2),
                                     th[:, :, cols].rearrange("p t (c i) -> p c t i", i=2),
-                                    gain_sb[:, g, :].unsqueeze(1).unsqueeze(3).to_broadcast([P, pairs, PACK, 2]),
+                                    gain_sb[:, g, :].unsqueeze(1).unsqueeze(3).to_broadcast([P, RUN // 2, PACK, 2]),
                                     ALU.mult)
-
-        spans = [slice(r * RUN, (r + 1) * RUN) for r in range(2)]
-        out_rows = out.rearrange("(g p t) j -> g p t j", g=GROUPS, t=PACK)
-        wx_q = [mx_tiles("wx%d" % g) for g in range(GROUPS)]
-        x_q = [mx_tiles("x%d" % half) for half in range(HALVES)]
 
         nc.sync.dma_start(list_v[:], offs)
         nc.sync.dma_start(tab_s[0:32, :], tab_scales.rearrange("a q n -> (a q) n").bitcast(I32))
@@ -169,165 +160,160 @@ def tile_list_snowpack_recurrence_kernel(tc, tab_words, tab_scales, offs, xT, of
         nc.sync.dma_start(list_3[:], offs3)
         load_plane(0)
         nc.sync.dma_start(list_2[:], offs2)
-        nc.vector.tensor_copy(v_s_rows[:], tab_s[:].bitcast(U8).indirect(list_v[:]))
         load_plane(1)
+        nc.sync.dma_start(wp_raw[:], wp_words.rearrange("a p n -> p a n").bitcast(I32))
         load_plane(2)
-        load_plane(3)
-        diff0 = group_tile("diff0")
-        gather_minus(0, 0, "minus00")
+        nc.vector.tensor_copy(v_s_rows[:], tab_s[:].bitcast(U8).indirect(list_v[:]))
         nc.vector.tensor_copy(stage[:, ROW:2 * ROW].bitcast(U8).rearrange("p (g t m) -> p g m t", m=P, t=PACK),
                               w_s_raw[:].bitcast(U8).rearrange("p (g m t) -> p g m t", m=P, t=PACK))
         nc.vector.tensor_copy(stage[:, 0:ROW], v_s_rows[:].bitcast(I32))
-        for q in range(QUADRANTS):
-            move_table_scales(nc.sync, 0, q)
-        for q in range(2):
-            move_table_scales(nc.sync, 1, q)
+        moves = [(a, q) for a in range(PASSES) for q in range(QUADRANTS)]
+        for a, q in moves[0:3]:
+            move_table_scales(a, q)
         load_wx(0)
-        for q in range(2, QUADRANTS):
-            move_table_scales(nc.sync, 1, q)
-        nc.sync.dma_start(wp_raw[:], wp_words.rearrange("a p n -> p a n").bitcast(I32))
-        for a in range(PASSES):
-            nc.sync.dma_start(tab_w[a][:], tab_words[a].rearrange("p n t -> p (n t)").bitcast(I32))
+        for a, q in moves[3:6]:
+            move_table_scales(a, q)
+        load_table(0)
+        for a, q in moves[6:8]:
+            move_table_scales(a, q)
+        load_plane(3)
+        load_table(1)
         load_wx(1)
         nc.sync.dma_start(gain_sb[:], gain.rearrange("(g p t) -> p g t", g=GROUPS, t=PACK))
         nc.sync.dma_start(wr_raw[:], wr_words.rearrange("a p n t -> p a (n t)").bitcast(I32))
-        for a in range(GROUPS):
-            for q in range(QUADRANTS):
-                move_wr_scales(a, q)
+        for a, q in moves:
+            move_wr_scales(a, q)
 
-        def table_passes(g):
-            sums = [new_bank(t) for t in range(PACK)]
-            order = [(t, a) for t in range(PACK) for a in range(PASSES)]
-            for t, a in (sorted(order, key=lambda ta: ta[1]) if g == 0 else order):
-                pass_wp(sums[t], 1, g, t, a, a == 0, a == PASSES - 1)
-            return sums
+        wp_c = placed([PASSES, 2 * H], U8, "wp_c", 191)
+        nc.scalar.copy(wp_c[:].bitcast(U16).rearrange("p a (g t m) -> p (a g) t m", g=GROUPS, t=PACK),
+                       wp_raw[:].bitcast(U16).rearrange("p a (g m t) -> p (a g) t m", g=GROUPS, t=PACK))
+        wx_b = [round_wx(0, 147)]
+        diff_first = group_tile("diff_first", 73)
+        minus_second = [placed([W], F32, "minus_second0", 145)[:], placed([W], F32, "minus_second1", 171)[:]]
+        wx_q = [mx_tiles("wx0"), mx_tiles("wx1")]
+        v_c = [[placed([W], U32, "v_first%d" % a, 183 + 2 * a) for a in range(PASSES)],
+               [None, placed([W], U32, "v_second1", 187)]]
+        for t in range(PACK):
+            if t == PACK - 1:
+                quantise(wx_b[0], wx_q[0][0][:], wx_q[0][1][:])
+                gather_v(v_c[0][0], 0, 0)
+            minus = placed([W], F32, "minus_first%d" % t, 137 + 2 * t)[:]
+            gather_minus(minus, 0, t)
+            gather_diff(diff_first[:, t, :], minus, 0, t)
+            if t < 2:
+                gather_minus(minus_second[t], 1, t)
+        for half in range(HALVES):
+            gather_v(v_c[half][1], half, 1)
+        x_b = interleave(nc.scalar.copy, diff_first, placed([W * PACK], BF16, "x_b0", 151), 2)
+        x_q = [mx_tiles("x0", 56), mx_tiles("x1")]
+        quantise(x_b, x_q[0][0][:], x_q[0][1][:])
+        wx_b.append(round_wx(1, 98))
 
-        def keep_b(g, tiles, copy):
-            for t in tiles:
-                bank = new_bank(PACK + t)
-                pass_b(bank, 1, g, t, True, True)
-                copy(b_kept[g][:, t, :], bank[:])
+        diff_second = group_tile("diff_second", 154)
+        for t in range(2):
+            gather_diff(diff_second[:, t, :], minus_second[t], 1, t)
+        quantise(wx_b[1], wx_q[1][0][:], wx_q[1][1][:])
+        banks = [new_bank(k) for k in range(BANKS)]
+        for a in range(PASSES):
+            for k in range(BANKS):
+                pass_wp(banks[k], 0, k // PACK, k % PACK, a, a == 0, False)
+        th_first = [group_tile("th_first%d" % g, 32 + 8 * g) for g in range(GROUPS)]
+        for k in range(BANKS):
+            g, t = divmod(k, PACK)
+            pass_b(banks[k][:], 0, g, t, slice(0, W), False, True)
+            nc.scalar.activation(th_first[g][:, t, :], banks[k][:], ACT.Tanh)
 
-        def add_and_tanh(sums, kept, total, th):
+        late_minus = placed([2, W], F32, "late_minus", 101)
+        minus_second.extend([late_minus[:, 0, :], late_minus[:, 1, :]])
+        h_b0 = [placed([RUN, PACK], BF16, "h_b0a", 171)]
+        gain_on_gpsimd(th_first[0], 0, h_b0[0][:], spans[0])
+        for t in range(2, PACK):
+            gather_minus(minus_second[t], 1, t)
+        v_c[1][0] = placed([W], U32, "v_second0", 97)
+        gather_v(v_c[1][0], 1, 0)
+        for t in range(2, PACK):
+            gather_diff(diff_second[:, t, :], minus_second[t], 1, t)
+        by_tile = placed([PACK, W], BF16, "by_tile", 125)
+        for t in range(PACK):
+            nc.scalar.activation(by_tile[:, t, :], th_first[1][:, t, :], ACT.Copy, scale=gain_sb[:, 1, t:t + 1])
+        h_b1 = interleave(nc.scalar.copy, by_tile, placed([W * PACK], BF16, "h_b1", 173), 4)
+        x_b = interleave(nc.vector.tensor_copy, diff_second, placed([W * PACK], BF16, "x_b1", 105), 4)
+        quantise(x_b, x_q[1][0][:], x_q[1][1][:])
+        wr_c = placed([GROUPS, H], I32, "wr_c", 108)
+        nc.vector.tensor_copy(wr_c[:].rearrange("p a (g t m) -> p (a g) m t", g=GROUPS, t=PACK),
+                              wr_raw[:].rearrange("p a (g m t) -> p (a g) m t", g=GROUPS, t=PACK))
+
+        def quantise_run(r, kib):
+            codes, block_scales = placed([RUN], U32, "h0_codes%d" % r, kib), sbuf([RUN], U8, "h0_scales%d" % r)
+            quantise(h_b0[r][:].rearrange("p j t -> p (j t)"), codes[:], block_scales[:])
+            return codes[:], block_scales[:]
+
+        h0_runs = [quantise_run(0, 106)]
+        h1_q = mx_tiles("h1")
+        quantise(h_b1, h1_q[0][:], h1_q[1][:])
+        h_b0.append(placed([RUN, PACK], BF16, "h_b0b", 173))
+        gain_on_gpsimd(th_first[0], 0, h_b0[1][:], spans[1])
+
+        early_b = group_tile("early_b", 118)
+        b_pairs = [early_b[:, 0:2, :], early_b[:, 2:PACK, :],
+                   placed([2, W], F32, "b_pair2", 128)[:], placed([2, W], F32, "b_pair3", 175)[:]]
+
+        def keep_b(tiles, copy):
+            for k in tiles:
+                bank = new_bank(PACK + k % PACK)
+                pass_b(bank[:], 1, k // PACK, k % PACK, slice(0, W), True, True)
+                copy(b_pairs[k // 2][:, k % 2, :], bank[:])
+
+        def add_and_tanh(sums, g, total, th):
             for t0 in range(0, PACK, 2):
                 for t in range(t0, t0 + 2):
-                    nc.vector.tensor_tensor(total[:, t, :], sums[t][:], kept[:, t, :], ALU.add)
+                    nc.vector.tensor_tensor(total[:, t, :], sums[t][:], b_pairs[2 * g + t // 2][:, t % 2, :], ALU.add)
                 nc.scalar.activation(th[:, t0:t0 + 2, :], total[:, t0:t0 + 2, :], ACT.Tanh)
             return th
 
-        def open_second_step(g, tiles):
-            banks = {t: new_bank(PACK * (1 - g) + t) for t in tiles}
-            for t in tiles:
-                pass_b(banks[t], 0, g, t, True, False)
-                pass_wr(banks[t][:], g, t, 0, h_first[0][0][:], h_first[0][1][:], False, False)
-            return banks
+        def second_step_first_half(r, first_bank, result, pairs):
+            h_run = [h0_runs[r], (h1_q[0][:, spans[r]], h1_q[1][:, spans[r]])]
+            for k in pairs:
+                g, t0 = k // 2, 2 * (k % 2)
+                bank = new_bank(first_bank + k)
+                for u in range(2):
+                    pass_b(bank[:, spans[u]], 0, g, t0 + u, spans[r], u == 0, False)
+                for u in range(2):
+                    for a in range(GROUPS):
+                        pass_wr(bank[:, spans[u]], g, t0 + u, a, h_run[a][0], h_run[a][1], False,
+                                u == 1 and a == GROUPS - 1)
+                nc.scalar.activation(result[:, k, :], bank[:], ACT.Tanh)
+                nc.sync.dma_start(out_rows[g][:, t0:t0 + 2, spans[r]],
+                                  result[:, k, :].rearrange("p (t j) -> p t j", j=RUN))
 
-        def close_second_step(g, banks, result):
-            for t in banks:
-                pass_wr(banks[t][:], g, t, 1, h_first[1][0][:], h_first[1][1][:], False, True)
-                nc.scalar.activation(result[:, t, :], banks[t][:], ACT.Tanh)
-                nc.sync.dma_start(out_rows[g][:, t, 0:W], result[:, t, :])
-
-        for t in range(PACK):
-            if t > 0:
-                gather_minus(0, t, "minus0%d" % t)
-            if t < 2:
-                gather_minus(1, t, "minus1%d" % t)
-            gather_diff(diff0, 0, t)
-        wx_b0 = round_wx(0)
-        wp_c = sbuf([PASSES, 2 * H], U8, "wp_c")
-        nc.scalar.copy(wp_c[:].bitcast(U16).rearrange("p a (g t m) -> p (a g) t m", g=GROUPS, t=PACK),
-                       wp_raw[:].bitcast(U16).rearrange("p a (g m t) -> p (a g) t m", g=GROUPS, t=PACK))
-        v_c = [[sbuf([W], U32, "v_00")[:], placed([W], U32, "v_01", 0)[:]]]
-        gather_v(v_c[0], 0, 0)
-        quantise(wx_b0, wx_q[0])
-        gather_v(v_c[0], 0, 1)
-        quantise(round_x(diff0, placed([W * PACK], BF16, "x_b0", 7)), x_q[0])
-        held = placed([2, W], F32, "held", 4)
-        for t in range(2, PACK):
-            minus[1, t] = held[:, t - 2, :]
-            nc.vector.tensor_copy(minus[1, t], planes[t][:].indirect(entries(list_3, 1)))
-        wx_b1 = placed([W * PACK], BF16, "wx_b1", 10)
-        nc.scalar.copy(wx_b1[:].rearrange("p (t m j) -> p m j t", t=PACK, j=PACK),
-                       wx_raw[1][:].rearrange("p j (m t) -> p m j t", t=PACK))
-        quantise(wx_b1[:], wx_q[1])
-        diff1 = placed([PACK, W], F32, "diff1", 10)
-        for t in range(PACK):
-            gather_diff(diff1, 1, t)
-
-        def first_step(g):
-            th = group_tile("th_first%d" % g)
-            banks = [new_bank(t) for t in range(PACK)]
-            ahead = [(t, a) for t in range(PACK) for a in range(PASSES)][:-1] if g == 1 else []
-            for t, a in ahead:
-                pass_wp(banks[t], 0, g, t, a, a == 0, False)
+        def table_passes(g):
+            sums = [new_bank(t) for t in range(PACK)]
             for t in range(PACK):
-                for a in range(PASSES):
-                    if (t, a) not in ahead:
-                        pass_wp(banks[t], 0, g, t, a, a == 0, False)
-                pass_b(banks[t], 0, g, t, False, True)
-                nc.scalar.activation(th[:, t, :], banks[t][:], ACT.Tanh)
-            return th
+                for a in (1, 0):
+                    pass_wp(sums[t], 1, g, t, a, a == 1, a == 0)
+            return sums
 
-        th_first = [first_step(0)]
-        by_tile = sbuf([PACK, W], BF16, "by_tile")
-        for t in range(PACK - GAIN_TILES_ON_VECTOR):
-            nc.scalar.activation(by_tile[:, t, :], th_first[0][:, t, :], ACT.Copy, scale=gain_sb[:, 0, t:t + 1])
-        for t in range(PACK - GAIN_TILES_ON_VECTOR, PACK):
-            nc.vector.tensor_scalar(by_tile[:, t, :], th_first[0][:, t, :], gain_sb[:, 0, t:t + 1], None, ALU.mult)
-        th_first.append(first_step(1))
-        v_c.append([sbuf([W], U32, "plane2")[:]])
-        gather_v(v_c[1], 1, 0)
-        wr_c = sbuf([GROUPS, H], I32, "plane3")
-        nc.vector.tensor_copy(wr_c[:].rearrange("p a (g t m) -> p (a g) m t", g=GROUPS, t=PACK),
-                              wr_raw[:].rearrange("p a (g m t) -> p (a g) m t", g=GROUPS, t=PACK))
-        quantise(round_x(diff1, placed([W * PACK], BF16, "x_b1", 0)), x_q[1])
-        v_c[1].append(placed([W], U32, "v_11", 0)[:])
-        gather_v(v_c[1], 1, 1)
-        h_b1 = [placed([RUN, PACK], BF16, "h_b1a", 2)]
-        gain_on_gpsimd(th_first[1], 1, h_b1[0][:], spans[0])
-        h_b0 = placed([W, PACK], BF16, "h_b0", 10)
-        nc.scalar.copy(h_b0[:].rearrange("p (c i) t -> p c t i", i=4),
-                       by_tile[:].rearrange("p t (c i) -> p c t i", i=4))
-        early = [new_bank(t) for t in range(PACK)]
-        for t in range(PACK):
-            pass_wp(early[t], 1, 0, t, 0, True, False)
-        b_kept = [group_tile("b_kept%d" % g) for g in range(GROUPS)]
-        keep_b(0, range(EARLY_COPIES), nc.vector.tensor_copy)
-        keep_b(0, range(EARLY_COPIES, PACK), nc.scalar.copy)
-        for t in range(PACK):
-            pass_wp(early[t], 1, 0, t, 1, False, True)
-        h1_q = mx_tiles("h1")
+        sums = table_passes(0)
+        keep_b(range(6), nc.scalar.copy)
+        keep_b(range(6, 8), nc.vector.tensor_copy)
+        th_second = [add_and_tanh(sums, 0, group_tile("total0", 155), group_tile("th_second0", 0))]
+        h0_runs.append(quantise_run(1, 155))
+        sums = table_passes(1)
+        result = group_tile("result_first0", 16)
+        second_step_first_half(0, PACK, result, range(EARLY_RESULTS))
+        th_second.append(add_and_tanh(sums, 1, group_tile("total1", 73), group_tile("th_second1", 8)))
+        second_step_first_half(0, PACK, result, range(EARLY_RESULTS, PACK))
+        second_step_first_half(1, 0, group_tile("result_first1", 24), range(PACK))
 
-        def quantise_run(r):
-            nc.vector.quantize_mx(out=h1_q[0][:, spans[r]].bitcast(FP8X4), scales=h1_q[1][:, spans[r]],
-                                  in_=h_b1[r][:].rearrange("p j t -> p (j t)"))
-
-        quantise_run(0)
-        h_first = [(placed([W], U32, "h0_codes", 2), sbuf([W], U8, "h0_scales")), h1_q]
-        quantise(h_b0[:].rearrange("p j t -> p (j t)"), h_first[0])
-        h_b1.append(placed([RUN, PACK], BF16, "h_b1b", 10))
-        gain_on_gpsimd(th_first[1], 1, h_b1[1][:], spans[1])
-
-        keep_b(1, range(PACK - COPIES_ON_VECTOR), nc.scalar.copy)
-        th_second = [add_and_tanh(early, b_kept[0], placed([PACK, W], F32, "total0", 12), group_tile("plane0"))]
-        keep_b(1, range(PACK - COPIES_ON_VECTOR, PACK), nc.vector.tensor_copy)
-        quantise_run(1)
-        late = table_passes(1)
-        close_second_step(0, open_second_step(0, [0]), group_tile("diff0"))
-        th_second.append(add_and_tanh(late, b_kept[1], group_tile("wx_raw0"), group_tile("plane1")))
-        close_second_step(0, open_second_step(0, range(1, PACK)), group_tile("wx_raw0"))
-        close_second_step(1, open_second_step(1, range(PACK)), group_tile("tab_w0"))
-
-        rounded = [placed([GROUPS, RUN, PACK], BF16, "h_run0", 10)[:], sbuf([GROUPS, RUN, PACK], BF16, "tab_w1")[:]]
-        h_runs = [mx_tiles("h_run%d" % r) for r in range(2)]
+        rounded = [placed([GROUPS, RUN, PACK], BF16, "h_run%d" % r, 163 + 4 * r)[:] for r in range(2)]
+        h_runs = [mx_tiles("h_second%d" % r) for r in range(2)]
         gain_on_gpsimd(th_second[0], 0, rounded[0][:, 0, :, :], spans[0])
         gain_on_vector(th_second[0], 0, rounded[1][:, 0, :, :], spans[1])
         for r in range(2):
             gain_on_vector(th_second[1], 1, rounded[r][:, 1, :, :], spans[r])
-            quantise(rounded[r].rearrange("p g j t -> p (g j t)"), h_runs[r])
-        totals = [group_tile("total"), group_tile("plane2")]
-        results = [group_tile("plane1"), group_tile("plane0")]
+            quantise(rounded[r].rearrange("p g j t -> p (g j t)"), h_runs[r][0][:], h_runs[r][1][:])
+        totals = [group_tile("total_last%d" % r, 32 + 8 * r) for r in range(2)]
+        results = [group_tile("result_last0", 65), group_tile("result_last1", 81)]
         for r in range(2):
             h_codes, h_scales = h_runs[r]
             for k in range(PACK):
@@ -340,10 +326,11 @@ def tile_list_snowpack_recurrence_kernel(tc, tab_words, tab_scales, offs, xT, of
                 last = r == 1 and k == PACK - 1
                 for u in ((0, 1) if last else (None,)):
                     rows = slice(t0, t0 + 2) if u is None else slice(t0 + u, t0 + u + 1)
+                    pair_rows = slice(0, 2) if u is None else slice(u, u + 1)
                     part = slice(0, W) if u is None else spans[u]
                     total = totals[r][:, k, part].rearrange("p (t j) -> p t j", j=RUN)
                     nc.vector.tensor_tensor(total, bank[:, part].rearrange("p (t j) -> p t j", j=RUN),
-                                            b_kept[g][:, rows, spans[r]], ALU.add)
+                                            b_pairs[k][:, pair_rows, spans[r]], ALU.add)
                     nc.scalar.activation(results[r][:, k, part], totals[r][:, k, part], ACT.Tanh)
                     nc.sync.dma_start(out_rows[g][:, rows, W + r * RUN:W + (r + 1) * RUN],
                                       results[r][:, k, part].rearrange("p (t j) -> p t j", j=RUN))

@@ -39,7 +39,7 @@ def tile_list_snowpack_recurrence_kernel(tc, tab_words, tab_scales, offs, xT, of
         psum = ctx.enter_context(tc.psum_pool(name="psum", bufs=1))
 
         def placed(shape, dtype, name, kib):
-            return arena.tile([P] + shape, dtype, name=name, align_bytes=256, offset=kib * 1024)
+            return arena.tile([P] + shape, dtype, name=name, align_bytes=256, offset=int(kib * 1024))
 
         def sbuf(shape, dtype, name):
             return keep.tile([P] + shape, dtype, name=name, align_bytes=256)
@@ -139,7 +139,7 @@ def tile_list_snowpack_recurrence_kernel(tc, tab_words, tab_scales, offs, xT, of
 
         def pass_wr(sums, g, t, a, h_codes, h_scales, start, stop):
             c0 = (g * PACK + t) * P
-            nc.tensor.matmul_mx(sums, lhsT=wr_c[:, a, c0:c0 + P].bitcast(FP8X4),
+            nc.tensor.matmul_mx(sums, lhsT=wr_c[a][:, c0:c0 + P].bitcast(FP8X4),
                                 lhsT_scale=wr_s[:].bitcast(U8)[4 * a:P, c0:c0 + P],
                                 rhs=h_codes.bitcast(FP8X4), rhs_scale=h_scales, start=start, stop=stop)
 
@@ -225,11 +225,11 @@ def tile_list_snowpack_recurrence_kernel(tc, tab_words, tab_scales, offs, xT, of
 
         late_minus = placed([2, W], F32, "late_minus", 101)
         minus_second.extend([late_minus[:, 0, :], late_minus[:, 1, :]])
-        h_b0 = [placed([RUN, PACK], BF16, "h_b0a", 171)]
+        h_b0 = [placed([RUN, PACK], BF16, "h_b0a", 96.5)]
         gain_on_gpsimd(th_first[0], 0, h_b0[0][:], spans[0])
         for t in range(2, PACK):
             gather_minus(minus_second[t], 1, t)
-        v_c[1][0] = placed([W], U32, "v_second0", 97)
+        v_c[1][0] = placed([W], U32, "v_second0", 98.5)
         gather_v(v_c[1][0], 1, 0)
         for t in range(2, PACK):
             gather_diff(diff_second[:, t, :], minus_second[t], 1, t)
@@ -239,9 +239,11 @@ def tile_list_snowpack_recurrence_kernel(tc, tab_words, tab_scales, offs, xT, of
         h_b1 = interleave(nc.scalar.copy, by_tile, placed([W * PACK], BF16, "h_b1", 173), 4)
         x_b = interleave(nc.vector.tensor_copy, diff_second, placed([W * PACK], BF16, "x_b1", 105), 4)
         quantise(x_b, x_q[1][0][:], x_q[1][1][:])
-        wr_c = placed([GROUPS, H], I32, "wr_c", 108)
-        nc.vector.tensor_copy(wr_c[:].rearrange("p a (g t m) -> p (a g) m t", g=GROUPS, t=PACK),
-                              wr_raw[:].rearrange("p a (g m t) -> p (a g) m t", g=GROUPS, t=PACK))
+        wr_c = [placed([H], U32, "wr_c0", 108), placed([H], U32, "wr_c1", 40)]
+        nc.vector.tensor_copy(wr_c[0][:].bitcast(I32).rearrange("p (g t m) -> p g m t", g=GROUPS, t=PACK),
+                              wr_raw[:, 0, :].rearrange("p (g m t) -> p g m t", g=GROUPS, t=PACK))
+        nc.scalar.copy(wr_c[1][:].rearrange("p (g t m) -> p g m t", g=GROUPS, t=PACK),
+                       wr_raw[:, 1, :].bitcast(U32).rearrange("p (g m t) -> p g m t", g=GROUPS, t=PACK))
 
         def quantise_run(r, kib):
             codes, block_scales = placed([RUN], U32, "h0_codes%d" % r, kib), sbuf([RUN], U8, "h0_scales%d" % r)
@@ -256,7 +258,7 @@ def tile_list_snowpack_recurrence_kernel(tc, tab_words, tab_scales, offs, xT, of
 
         early_b = group_tile("early_b", 118)
         b_pairs = [early_b[:, 0:2, :], early_b[:, 2:PACK, :],
-                   placed([2, W], F32, "b_pair2", 128)[:], placed([2, W], F32, "b_pair3", 175)[:]]
+                   placed([2, W], F32, "b_pair2", 128)[:]]
 
         def keep_b(tiles, copy):
             for k in tiles:
@@ -264,12 +266,11 @@ def tile_list_snowpack_recurrence_kernel(tc, tab_words, tab_scales, offs, xT, of
                 pass_b(bank[:], 1, k // PACK, k % PACK, slice(0, W), True, True)
                 copy(b_pairs[k // 2][:, k % 2, :], bank[:])
 
-        def add_and_tanh(sums, g, total, th):
-            for t0 in range(0, PACK, 2):
-                for t in range(t0, t0 + 2):
-                    nc.vector.tensor_tensor(total[:, t, :], sums[t][:], b_pairs[2 * g + t // 2][:, t % 2, :], ALU.add)
-                nc.scalar.activation(th[:, t0:t0 + 2, :], total[:, t0:t0 + 2, :], ACT.Tanh)
-            return th
+        def add_and_tanh(sums, g, k, kib):
+            total = placed([2, W], F32, "total%d%d" % (g, k), kib)
+            for u in range(2):
+                nc.vector.tensor_tensor(total[:, u, :], sums[2 * k + u][:], b_pairs[2 * g + k][:, u, :], ALU.add)
+            nc.scalar.activation(th_second[g][:, 2 * k:2 * k + 2, :], total[:], ACT.Tanh)
 
         def second_step_first_half(r, first_bank, result, pairs):
             h_run = [h0_runs[r], (h1_q[0][:, spans[r]], h1_q[1][:, spans[r]])]
@@ -287,32 +288,37 @@ def tile_list_snowpack_recurrence_kernel(tc, tab_words, tab_scales, offs, xT, of
                                   result[:, k, :].rearrange("p (t j) -> p t j", j=RUN))
 
         def table_passes(g):
-            sums = [new_bank(t) for t in range(PACK)]
-            for t in range(PACK):
+            sums = [new_bank((t + 2 * g) % PACK) for t in range(PACK)]
+            for t in sorted(range(PACK), key=lambda t: (t + 2 * g) % PACK):
                 for a in (1, 0):
                     pass_wp(sums[t], 1, g, t, a, a == 1, a == 0)
             return sums
 
         sums = table_passes(0)
-        keep_b(range(6), nc.scalar.copy)
+        th_second = [group_tile("th_second%d" % g, 8 * g) for g in range(GROUPS)]
+        keep_b(range(4), nc.scalar.copy)
+        for k in range(2):
+            add_and_tanh(sums, 0, k, 155 + 4 * k)
+        b_pairs.append(placed([2, W], F32, "b_pair3", 175)[:])
         keep_b(range(6, 8), nc.vector.tensor_copy)
-        th_second = [add_and_tanh(sums, 0, group_tile("total0", 155), group_tile("th_second0", 0))]
+        keep_b(range(4, 6), nc.scalar.copy)
         h0_runs.append(quantise_run(1, 155))
         sums = table_passes(1)
         result = group_tile("result_first0", 16)
         second_step_first_half(0, PACK, result, range(EARLY_RESULTS))
-        th_second.append(add_and_tanh(sums, 1, group_tile("total1", 73), group_tile("th_second1", 8)))
+        for k in (1, 0):
+            add_and_tanh(sums, 1, k, 73 + 4 * k)
         second_step_first_half(0, PACK, result, range(EARLY_RESULTS, PACK))
         second_step_first_half(1, 0, group_tile("result_first1", 24), range(PACK))
 
-        rounded = [placed([GROUPS, RUN, PACK], BF16, "h_run%d" % r, 163 + 4 * r)[:] for r in range(2)]
+        rounded = [placed([GROUPS, RUN, PACK], BF16, "h_run0", 171)[:], placed([GROUPS, RUN, PACK], BF16, "h_run1", 163)[:]]
         h_runs = [mx_tiles("h_second%d" % r) for r in range(2)]
         gain_on_gpsimd(th_second[0], 0, rounded[0][:, 0, :, :], spans[0])
         gain_on_vector(th_second[0], 0, rounded[1][:, 0, :, :], spans[1])
         for r in range(2):
             gain_on_vector(th_second[1], 1, rounded[r][:, 1, :, :], spans[r])
             quantise(rounded[r].rearrange("p g j t -> p (g j t)"), h_runs[r][0][:], h_runs[r][1][:])
-        totals = [group_tile("total_last%d" % r, 32 + 8 * r) for r in range(2)]
+        totals = [group_tile("total_last0", 32), group_tile("total_last1", 137)]
         results = [group_tile("result_last0", 65), group_tile("result_last1", 81)]
         for r in range(2):
             h_codes, h_scales = h_runs[r]

@@ -168,16 +168,16 @@ def tile_list_snowpack_recurrence_kernel(tc, tab_words, tab_scales, offs, xT, of
                               w_s_raw[:].bitcast(U8).rearrange("p (g m t) -> p g m t", m=P, t=PACK))
         nc.vector.tensor_copy(stage[:, 0:ROW], v_s_rows[:].bitcast(I32))
         moves = [(a, q) for a in range(PASSES) for q in range(QUADRANTS)]
-        for a, q in moves[0:3]:
+        for a, q in moves[0:2]:
             move_table_scales(a, q)
         load_wx(0)
-        for a, q in moves[3:6]:
+        for a, q in moves[2:4]:
             move_table_scales(a, q)
         load_table(0)
-        for a, q in moves[6:8]:
-            move_table_scales(a, q)
         load_plane(3)
         load_table(1)
+        for a, q in moves[4:8]:
+            move_table_scales(a, q)
         load_wx(1)
         nc.sync.dma_start(gain_sb[:], gain.rearrange("(g p t) -> p g t", g=GROUPS, t=PACK))
         nc.sync.dma_start(wr_raw[:], wr_words.rearrange("a p n t -> p a (n t)").bitcast(I32))

@@ -168,15 +168,13 @@ def tile_list_snowpack_recurrence_kernel(tc, tab_words, tab_scales, offs, xT, of
                               w_s_raw[:].bitcast(U8).rearrange("p (g m t) -> p g m t", m=P, t=PACK))
         nc.vector.tensor_copy(stage[:, 0:ROW], v_s_rows[:].bitcast(I32))
         moves = [(a, q) for a in range(PASSES) for q in range(QUADRANTS)]
-        for a, q in moves[0:2]:
-            move_table_scales(a, q)
         load_wx(0)
-        for a, q in moves[2:4]:
-            move_table_scales(a, q)
         load_table(0)
         load_plane(3)
+        for a, q in moves[0:QUADRANTS]:
+            move_table_scales(a, q)
         load_table(1)
-        for a, q in moves[4:8]:
+        for a, q in moves[QUADRANTS:]:
             move_table_scales(a, q)
         load_wx(1)
         nc.sync.dma_start(gain_sb[:], gain.rearrange("(g p t) -> p g t", g=GROUPS, t=PACK))
@@ -290,8 +288,8 @@ def tile_list_snowpack_recurrence_kernel(tc, tab_words, tab_scales, offs, xT, of
         def table_passes(g):
             sums = [new_bank((t + 2 * g) % PACK) for t in range(PACK)]
             for t in sorted(range(PACK), key=lambda t: (t + 2 * g) % PACK):
-                for a in (1, 0):
-                    pass_wp(sums[t], 1, g, t, a, a == 1, a == 0)
+                for a in range(PASSES):
+                    pass_wp(sums[t], 1, g, t, a, a == 0, a == PASSES - 1)
             return sums
 
         sums = table_passes(0)

@@ -69,7 +69,8 @@ def tile_list_snowpack_recurrence_kernel(tc, tab_words, tab_scales, offs, xT, of
         gain_sb = keep.tile([P, GROUPS, PACK], F32, name="gain_sb")
 
         planes = [placed([T], F32, "plane%d" % t, 8 * t) for t in range(PACK)]
-        wx_raw = [group_tile("wx_raw%d" % g, 32 + 8 * g) for g in range(GROUPS)]
+        wx_raw = [[group_tile("wx_raw0", 32)],
+                  [placed([PACK, RUN], F32, "wx_raw1%d" % u, 40 + 4 * u) for u in range(2)]]
         tab_w = [placed([T], I32, "tab_w%d" % a, 48 + 8 * a) for a in range(PASSES)]
         wr_raw = placed([GROUPS, H], I32, "wr_raw", 65)
         wp_raw = placed([PASSES, H // 2], I32, "wp_raw", 179)
@@ -78,14 +79,17 @@ def tile_list_snowpack_recurrence_kernel(tc, tab_words, tab_scales, offs, xT, of
         out_rows = out.rearrange("(g p t) j -> g p t j", g=GROUPS, t=PACK)
         spans = [slice(r * RUN, (r + 1) * RUN) for r in range(2)]
 
-        def entries(list_tile, half):
-            return list_tile[:, half * (W // STRIPE):(half + 1) * (W // STRIPE)]
+        def entries(list_tile, half, span=slice(0, W)):
+            return list_tile[:, (half * W + span.start) // STRIPE:(half * W + span.stop) // STRIPE]
 
         def gather_minus(minus, half, t):
-            nc.vector.tensor_copy(minus, planes[t][:].indirect(entries(list_3, half)))
+            for span in (spans if half == 0 and t >= 2 else [slice(0, W)]):
+                nc.vector.tensor_copy(minus[:, span], planes[t][:].indirect(entries(list_3, half, span)))
 
         def gather_diff(diff, minus, half, t):
-            nc.vector.tensor_tensor(diff, planes[t][:].indirect(entries(list_2, half)), minus, ALU.subtract)
+            for span in (spans if t == PACK - 1 or (half == 0 and t >= 2) else [slice(0, W)]):
+                nc.vector.tensor_tensor(diff[:, span], planes[t][:].indirect(entries(list_2, half, span)),
+                                        minus[:, span], ALU.subtract)
 
         def gather_v(words, half, a):
             nc.vector.tensor_copy(words[:], tab_w[a][:].bitcast(U32).indirect(entries(list_v, half)))
@@ -103,20 +107,25 @@ def tile_list_snowpack_recurrence_kernel(tc, tab_words, tab_scales, offs, xT, of
             nc.sync.dma_start(tab_w[a][:], tab_words[a].rearrange("p n t -> p (n t)").bitcast(I32))
 
         def load_wx(g):
-            nc.sync.dma_start(wx_raw[g][:], wx_rows[:, :, g * W:(g + 1) * W])
+            width = W // len(wx_raw[g])
+            for u, piece in enumerate(wx_raw[g]):
+                nc.sync.dma_start(piece[:], wx_rows[:, :, g * W + u * width:g * W + (u + 1) * width])
 
         def round_wx(g, kib):
             rounded = placed([W * PACK], BF16, "wx_b%d" % g, kib)
-            nc.scalar.copy(rounded[:].rearrange("p (t m j) -> p m j t", t=PACK, j=PACK),
-                           wx_raw[g][:].rearrange("p j (m t) -> p m j t", t=PACK))
+            count = P // len(wx_raw[g])
+            for u, piece in enumerate(wx_raw[g]):
+                nc.scalar.copy(rounded[:].rearrange("p (t m j) -> p m j t", t=PACK, j=PACK)[:, u * count:(u + 1) * count],
+                               piece[:].rearrange("p j (m t) -> p m j t", t=PACK))
             return rounded[:]
 
         def quantise(rounded, codes, block_scales):
             nc.vector.quantize_mx(out=codes.bitcast(FP8X4), scales=block_scales, in_=rounded)
 
-        def interleave(copy, rows, words, step):
-            copy(words[:].rearrange("p (c i t) -> p c t i", i=step, t=PACK),
-                 rows[:].rearrange("p t (c i) -> p c t i", i=step))
+        def interleave(copy, rows, words, step, parts):
+            for span in parts:
+                copy(words[:, PACK * span.start:PACK * span.stop].rearrange("p (c i t) -> p c t i", i=step, t=PACK),
+                     rows[:, :, span].rearrange("p t (c i) -> p c t i", i=step))
             return words[:]
 
         def new_bank(k):
@@ -197,12 +206,12 @@ def tile_list_snowpack_recurrence_kernel(tc, tab_words, tab_scales, offs, xT, of
                 gather_v(v_c[0][0], 0, 0)
             minus = placed([W], F32, "minus_first%d" % t, 137 + 2 * t)[:]
             gather_minus(minus, 0, t)
-            gather_diff(diff_first[:, t, :], minus, 0, t)
             if t < 2:
                 gather_minus(minus_second[t], 1, t)
+            gather_diff(diff_first[:, t, :], minus, 0, t)
         for half in range(HALVES):
             gather_v(v_c[half][1], half, 1)
-        x_b = interleave(nc.scalar.copy, diff_first, placed([W * PACK], BF16, "x_b0", 151), 2)
+        x_b = interleave(nc.scalar.copy, diff_first, placed([W * PACK], BF16, "x_b0", 151), 2, spans)
         x_q = [mx_tiles("x0", 56), mx_tiles("x1")]
         quantise(x_b, x_q[0][0][:], x_q[0][1][:])
         wx_b.append(round_wx(1, 98))
@@ -234,9 +243,10 @@ def tile_list_snowpack_recurrence_kernel(tc, tab_words, tab_scales, offs, xT, of
         by_tile = placed([PACK, W], BF16, "by_tile", 125)
         for t in range(PACK):
             nc.scalar.activation(by_tile[:, t, :], th_first[1][:, t, :], ACT.Copy, scale=gain_sb[:, 1, t:t + 1])
-        h_b1 = interleave(nc.scalar.copy, by_tile, placed([W * PACK], BF16, "h_b1", 173), 4)
-        x_b = interleave(nc.vector.tensor_copy, diff_second, placed([W * PACK], BF16, "x_b1", 105), 4)
-        quantise(x_b, x_q[1][0][:], x_q[1][1][:])
+        h_b1 = interleave(nc.scalar.copy, by_tile, placed([W * PACK], BF16, "h_b1", 173), 4, [slice(0, W)])
+        x_b = interleave(nc.vector.tensor_copy, diff_second, placed([W * PACK], BF16, "x_b1", 105), 4, spans)
+        for span in spans:
+            quantise(x_b[:, PACK * span.start:PACK * span.stop], x_q[1][0][:, span], x_q[1][1][:, span])
         wr_c = [placed([H], U32, "wr_c0", 108), placed([H], U32, "wr_c1", 40)]
         nc.vector.tensor_copy(wr_c[0][:].bitcast(I32).rearrange("p (g t m) -> p g m t", g=GROUPS, t=PACK),
                               wr_raw[:, 0, :].rearrange("p (g m t) -> p g m t", g=GROUPS, t=PACK))

@@ -27,6 +27,7 @@ PASSES = K // (P * PACK)
 BANKS = 8
 RUN = W // 2
 EARLY_RESULTS = 1
+THIRD_ON_GPSIMD = 192
 ROW = H // 4
 
 
@@ -153,13 +154,15 @@ def tile_list_snowpack_recurrence_kernel(tc, tab_words, tab_scales, offs, xT, of
                                 rhs=h_codes.bitcast(FP8X4), rhs_scale=h_scales, start=start, stop=stop)
 
         def gain_on_gpsimd(th, g, rounded, cols):
+            count = cols.stop - cols.start
             nc.gpsimd.tensor_tensor(rounded, th[:, :, cols].rearrange("p t c -> p c t"),
-                                    gain_sb[:, g, :].unsqueeze(1).to_broadcast([P, RUN, PACK]), ALU.mult)
+                                    gain_sb[:, g, :].unsqueeze(1).to_broadcast([P, count, PACK]), ALU.mult)
 
         def gain_on_vector(th, g, rounded, cols):
+            pairs = (cols.stop - cols.start) // 2
             nc.vector.tensor_tensor(rounded.rearrange("p (c i) t -> p c t i", i=2),
                                     th[:, :, cols].rearrange("p t (c i) -> p c t i", i=2),
-                                    gain_sb[:, g, :].unsqueeze(1).unsqueeze(3).to_broadcast([P, RUN // 2, PACK, 2]),
+                                    gain_sb[:, g, :].unsqueeze(1).unsqueeze(3).to_broadcast([P, pairs, PACK, 2]),
                                     ALU.mult)
 
         nc.sync.dma_start(list_v[:], offs)
@@ -274,11 +277,13 @@ def tile_list_snowpack_recurrence_kernel(tc, tab_words, tab_scales, offs, xT, of
                 pass_b(bank[:], 1, k // PACK, k % PACK, slice(0, W), True, True)
                 copy(b_pairs[k // 2][:, k % 2, :], bank[:])
 
-        def add_and_tanh(sums, g, k, kib):
+        def add_and_tanh(sums, g, k, kib, singly):
             total = placed([2, W], F32, "total%d%d" % (g, k), kib)
             for u in range(2):
                 nc.vector.tensor_tensor(total[:, u, :], sums[2 * k + u][:], b_pairs[2 * g + k][:, u, :], ALU.add)
-            nc.scalar.activation(th_second[g][:, 2 * k:2 * k + 2, :], total[:], ACT.Tanh)
+            for rows in ([slice(0, 1), slice(1, 2)] if singly else [slice(0, 2)]):
+                nc.scalar.activation(th_second[g][:, 2 * k + rows.start:2 * k + rows.stop, :], total[:, rows, :],
+                                     ACT.Tanh)
 
         def second_step_first_half(r, first_bank, result, pairs):
             h_run = [h0_runs[r], (h1_q[0][:, spans[r]], h1_q[1][:, spans[r]])]
@@ -306,7 +311,7 @@ def tile_list_snowpack_recurrence_kernel(tc, tab_words, tab_scales, offs, xT, of
         th_second = [group_tile("th_second%d" % g, 8 * g) for g in range(GROUPS)]
         keep_b(range(4), nc.scalar.copy)
         for k in range(2):
-            add_and_tanh(sums, 0, k, 155 + 4 * k)
+            add_and_tanh(sums, 0, k, 155 + 4 * k, False)
         b_pairs.append(placed([2, W], F32, "b_pair3", 175)[:])
         keep_b(range(6, 8), nc.vector.tensor_copy)
         keep_b(range(4, 6), nc.scalar.copy)
@@ -315,14 +320,15 @@ def tile_list_snowpack_recurrence_kernel(tc, tab_words, tab_scales, offs, xT, of
         result = group_tile("result_first0", 16)
         second_step_first_half(0, PACK, result, range(EARLY_RESULTS))
         for k in (1, 0):
-            add_and_tanh(sums, 1, k, 73 + 4 * k)
+            add_and_tanh(sums, 1, k, 73 + 4 * k, True)
         second_step_first_half(0, PACK, result, range(EARLY_RESULTS, PACK))
         second_step_first_half(1, 0, group_tile("result_first1", 24), range(PACK))
 
         rounded = [placed([GROUPS, RUN, PACK], BF16, "h_run0", 171)[:], placed([GROUPS, RUN, PACK], BF16, "h_run1", 163)[:]]
         h_runs = [mx_tiles("h_second%d" % r) for r in range(2)]
-        gain_on_gpsimd(th_second[0], 0, rounded[0][:, 0, :, :], spans[0])
+        gain_on_gpsimd(th_second[0], 0, rounded[0][:, 0, 0:THIRD_ON_GPSIMD, :], slice(0, THIRD_ON_GPSIMD))
         gain_on_vector(th_second[0], 0, rounded[1][:, 0, :, :], spans[1])
+        gain_on_vector(th_second[0], 0, rounded[0][:, 0, THIRD_ON_GPSIMD:RUN, :], slice(THIRD_ON_GPSIMD, RUN))
         for r in range(2):
             gain_on_vector(th_second[1], 1, rounded[r][:, 1, :, :], spans[r])
             quantise(rounded[r].rearrange("p g j t -> p (g j t)"), h_runs[r][0][:], h_runs[r][1][:])

@@ -28,6 +28,7 @@ BANKS = 8
 RUN = W // 2
 EARLY_RESULTS = 1
 THIRD_ON_GPSIMD = 192
+FREED = [6, 0, 7, 5, 4, 1, 2, 3]
 ROW = H // 4
 
 
@@ -271,25 +272,25 @@ def tile_list_snowpack_recurrence_kernel(tc, tab_words, tab_scales, offs, xT, of
         b_pairs = [early_b[:, 0:2, :], early_b[:, 2:PACK, :],
                    placed([2, W], F32, "b_pair2", 128)[:]]
 
-        def keep_b(tiles, copy):
-            for k in tiles:
-                bank = new_bank(PACK + k % PACK)
+        def keep_b(tiles, b_banks, copy):
+            for k, b_bank in zip(tiles, b_banks):
+                bank = new_bank(b_bank)
                 pass_b(bank[:], 1, k // PACK, k % PACK, slice(0, W), True, True)
                 copy(b_pairs[k // 2][:, k % 2, :], bank[:])
 
         def add_and_tanh(sums, g, k, kib, singly):
             total = placed([2, W], F32, "total%d%d" % (g, k), kib)
             for u in range(2):
-                nc.vector.tensor_tensor(total[:, u, :], sums[2 * k + u][:], b_pairs[2 * g + k][:, u, :], ALU.add)
+                nc.vector.tensor_tensor(total[:, u, :], sums[PACK * g + 2 * k + u][:], b_pairs[2 * g + k][:, u, :], ALU.add)
             for rows in ([slice(0, 1), slice(1, 2)] if singly else [slice(0, 2)]):
                 nc.scalar.activation(th_second[g][:, 2 * k + rows.start:2 * k + rows.stop, :], total[:, rows, :],
                                      ACT.Tanh)
 
-        def second_step_first_half(r, first_bank, result, pairs):
+        def second_step_first_half(r, result, pairs):
             h_run = [h0_runs[r], (h1_q[0][:, spans[r]], h1_q[1][:, spans[r]])]
             for k in pairs:
                 g, t0 = k // 2, 2 * (k % 2)
-                bank = new_bank(first_bank + k)
+                bank = new_bank(FREED[PACK * r + k])
                 for u in range(2):
                     pass_b(bank[:, spans[u]], 0, g, t0 + u, spans[r], u == 0, False)
                 for u in range(2):
@@ -300,29 +301,29 @@ def tile_list_snowpack_recurrence_kernel(tc, tab_words, tab_scales, offs, xT, of
                 nc.sync.dma_start(out_rows[g][:, t0:t0 + 2, spans[r]],
                                   result[:, k, :].rearrange("p (t j) -> p t j", j=RUN))
 
-        def table_passes(g):
-            sums = [new_bank((t + 2 * g) % PACK) for t in range(PACK)]
-            for t in sorted(range(PACK), key=lambda t: (t + 2 * g) % PACK):
+        def table_passes(tiles, sum_banks):
+            for k, sum_bank in zip(tiles, sum_banks):
+                sums[k] = new_bank(sum_bank)
                 for a in range(PASSES):
-                    pass_wp(sums[t], 1, g, t, a, a == 0, a == PASSES - 1)
-            return sums
+                    pass_wp(sums[k], 1, k // PACK, k % PACK, a, a == 0, a == PASSES - 1)
 
-        sums = table_passes(0)
+        sums = {}
+        table_passes([0, 1, 2, 3, 6], range(5))
         th_second = [group_tile("th_second%d" % g, 8 * g) for g in range(GROUPS)]
-        keep_b(range(4), nc.scalar.copy)
+        keep_b(range(4), [5, 6, 7, 5], nc.scalar.copy)
         for k in range(2):
             add_and_tanh(sums, 0, k, 155 + 4 * k, False)
         b_pairs.append(placed([2, W], F32, "b_pair3", 175)[:])
-        keep_b(range(6, 8), nc.vector.tensor_copy)
-        keep_b(range(4, 6), nc.scalar.copy)
+        keep_b([6, 7], [6, 0], nc.vector.tensor_copy)
+        keep_b([4, 5], [7, 5], nc.scalar.copy)
         h0_runs.append(quantise_run(1, 155))
-        sums = table_passes(1)
+        table_passes([7, 4, 5], [1, 2, 3])
         result = group_tile("result_first0", 16)
-        second_step_first_half(0, PACK, result, range(EARLY_RESULTS))
+        second_step_first_half(0, result, range(EARLY_RESULTS))
         for k in (1, 0):
             add_and_tanh(sums, 1, k, 73 + 4 * k, True)
-        second_step_first_half(0, PACK, result, range(EARLY_RESULTS, PACK))
-        second_step_first_half(1, 0, group_tile("result_first1", 24), range(PACK))
+        second_step_first_half(0, result, range(EARLY_RESULTS, PACK))
+        second_step_first_half(1, group_tile("result_first1", 24), range(PACK))
 
         rounded = [placed([GROUPS, RUN, PACK], BF16, "h_run0", 171)[:], placed([GROUPS, RUN, PACK], BF16, "h_run1", 163)[:]]
         h_runs = [mx_tiles("h_second%d" % r) for r in range(2)]
@@ -338,7 +339,7 @@ def tile_list_snowpack_recurrence_kernel(tc, tab_words, tab_scales, offs, xT, of
             h_codes, h_scales = h_runs[r]
             for k in range(PACK):
                 g, t0 = k // 2, 2 * (k % 2)
-                bank = new_bank(PACK * (1 - r) + k)
+                bank = new_bank(FREED[PACK * r + k])
                 for t in range(t0, t0 + 2):
                     for a in range(GROUPS):
                         pass_wr(bank[:, spans[t - t0]], g, t, a, h_codes[:, spans[a]], h_scales[:, spans[a]],

@@ -21,15 +21,44 @@ PACK = 4
 QUADRANTS = 4
 STRIPE = 16
 W = 512
+RUN = W // 2
 HALVES = S // W
 GROUPS = H // (P * PACK)
 PASSES = K // (P * PACK)
 BANKS = 8
-RUN = W // 2
+ROW = H // 4
+EARLY_PLANES = 2
 EARLY_RESULTS = 1
 THIRD_ON_GPSIMD = 192
 FREED = [6, 0, 7, 5, 4, 1, 2, 3]
-ROW = H // 4
+
+PLACE = {
+    "plane": 0, "th_second": 0, "result_first": 16,
+    "wx_raw0": 32, "wx_raw1": 40, "th_first": 32, "total_last0": 32,
+    "wr_c1": 40,
+    "tab_w": 48,
+    "x0": 56,
+    "wr_raw": 65, "result_last0": 65, "diff_first": 73, "total1": 73, "result_last1": 81,
+    "wx_b1": 98,
+    "h_b0a": 96.5,
+    "v_second0": 98.5,
+    "late_minus": 101,
+    "x_b1": 105,
+    "h0_codes0": 106,
+    "wr_c0": 108,
+    "by_tile": 125,
+    "early_b": 118,
+    "b_pair2": 128,
+    "minus_first": 137, "total_last1": 137, "minus_second0": 145, "wx_b0": 147, "x_b0": 151,
+    "diff_second": 154,
+    "total0": 155,
+    "h0_codes1": 155,
+    "h_run1": 163, "minus_second1": 171, "h_b1": 173,
+    "h_b0b": 173,
+    "b_pair3": 175,
+    "h_run0": 171,
+    "wp_raw": 179, "v_first": 183, "v_second1": 187, "wp_c": 191,
+}
 
 
 def tile_list_snowpack_recurrence_kernel(tc, tab_words, tab_scales, offs, xT, offs2, offs3, wp_words,
@@ -40,17 +69,20 @@ def tile_list_snowpack_recurrence_kernel(tc, tab_words, tab_scales, offs, xT, of
         arena = ctx.enter_context(tc.tile_pool(name="arena", bufs=1))
         psum = ctx.enter_context(tc.psum_pool(name="psum", bufs=1))
 
-        def placed(shape, dtype, name, kib):
+        def at(shape, dtype, name, kib):
             return arena.tile([P] + shape, dtype, name=name, align_bytes=256, offset=int(kib * 1024))
+
+        def placed(shape, dtype, name):
+            return at(shape, dtype, name, PLACE[name])
+
+        def placed_row(shape, dtype, name, n, kib_each):
+            return at(shape, dtype, "%s%d" % (name, n), PLACE[name] + n * kib_each)
 
         def sbuf(shape, dtype, name):
             return keep.tile([P] + shape, dtype, name=name, align_bytes=256)
 
-        def group_tile(name, kib):
-            return placed([PACK, W], F32, name, kib)
-
-        def mx_tiles(name, kib=None):
-            codes = sbuf([W], U32, name + "_codes") if kib is None else placed([W], U32, name + "_codes", kib)
+        def mx_tiles(name):
+            codes = at([W], U32, name + "_codes", PLACE[name]) if name in PLACE else sbuf([W], U32, name + "_codes")
             return codes, sbuf([W], U8, name + "_scales")
 
         list_v = keep.tile([P, S // STRIPE], U16, name="list_v")
@@ -63,44 +95,48 @@ def tile_list_snowpack_recurrence_kernel(tc, tab_words, tab_scales, offs, xT, of
         wr_s = sbuf([ROW], I32, "wr_s")
         nc.vector.memset(tab_s[32:64, :], 0)
         nc.vector.memset(tab_s[64:P, :], 0)
-        nc.vector.memset(w_s_raw[64:P, :], 0)
-        for plane in pass_s + [wr_s]:
-            nc.vector.memset(plane[:], 0)
+        nc.vector.memset(w_s_raw[32:64, :], 0)
+        nc.vector.memset(w_s_raw[96:P, :], 0)
+        for scale_tile in pass_s + [wr_s]:
+            nc.vector.memset(scale_tile[:], 0)
         v_s_rows = sbuf([S], U8, "v_s_rows")
         stage = sbuf([2 * ROW], I32, "stage")
         gain_sb = keep.tile([P, GROUPS, PACK], F32, name="gain_sb")
 
-        planes = [placed([T], F32, "plane%d" % t, 8 * t) for t in range(PACK)]
-        wx_raw = [[group_tile("wx_raw0", 32)],
-                  [placed([PACK, RUN], F32, "wx_raw1%d" % u, 40 + 4 * u) for u in range(2)]]
-        tab_w = [placed([T], I32, "tab_w%d" % a, 48 + 8 * a) for a in range(PASSES)]
-        wr_raw = placed([GROUPS, H], I32, "wr_raw", 65)
-        wp_raw = placed([PASSES, H // 2], I32, "wp_raw", 179)
+        planes = [placed_row([T], F32, "plane", t, 8) for t in range(PACK)]
+        wx_raw = [[placed([PACK, W], F32, "wx_raw0")],
+                  [placed_row([PACK, RUN], F32, "wx_raw1", u, 4) for u in range(2)]]
+        tab_w = [placed_row([T], I32, "tab_w", a, 8) for a in range(PASSES)]
+        wr_raw = placed([GROUPS, H], I32, "wr_raw")
+        wp_raw = placed([PASSES, H // 2], I32, "wp_raw")
         x_rows = xT.rearrange("(p t) n -> t p n", t=PACK)
         wx_rows = wx.rearrange("(p j) c -> p j c", j=PACK)
         out_rows = out.rearrange("(g p t) j -> g p t j", g=GROUPS, t=PACK)
+        whole = slice(0, W)
         spans = [slice(r * RUN, (r + 1) * RUN) for r in range(2)]
 
-        def entries(list_tile, half, span=slice(0, W)):
+        def entries(list_tile, half, span):
             return list_tile[:, (half * W + span.start) // STRIPE:(half * W + span.stop) // STRIPE]
 
-        def gather_minus(minus, half, t):
-            for span in (spans if half == 0 and t >= 2 else [slice(0, W)]):
+        def gather_minus(minus, half, t, parts):
+            for span in parts:
                 nc.vector.tensor_copy(minus[:, span], planes[t][:].indirect(entries(list_3, half, span)))
 
-        def gather_diff(diff, minus, half, t):
-            for span in (spans if t == PACK - 1 or (half == 0 and t >= 2) else [slice(0, W)]):
-                nc.vector.tensor_tensor(diff[:, span], planes[t][:].indirect(entries(list_2, half, span)),
+        def gather_diff(diff, minus, half, t, parts):
+            for span in parts:
+                nc.vector.tensor_tensor(diff[:, t, span], planes[t][:].indirect(entries(list_2, half, span)),
                                         minus[:, span], ALU.subtract)
 
-        def gather_v(words, half, a):
-            nc.vector.tensor_copy(words[:], tab_w[a][:].bitcast(U32).indirect(entries(list_v, half)))
+        def gather_v(half, a):
+            nc.vector.tensor_copy(v_c[half, a][:], tab_w[a][:].bitcast(U32).indirect(entries(list_v, half, whole)))
 
-        def move_table_scales(a, q):
-            nc.sync.dma_start(pass_s[a][q:P:32, :], stage[16 * a + q:16 * a + 16:4, :])
+        def move_pass_scales(a):
+            for q in range(QUADRANTS):
+                nc.sync.dma_start(pass_s[a][q:P:32, :], stage[16 * a + q:16 * a + 16:4, :])
 
-        def move_wr_scales(a, q):
-            nc.sync.dma_start(wr_s[4 * a + q:P:32, :], stage[32 + 16 * a + q:32 + 16 * a + 16:4, ROW:2 * ROW])
+        def move_wr_scales(a):
+            for q in range(QUADRANTS):
+                nc.sync.dma_start(wr_s[4 * a + q:P:32, :], stage[64 + 16 * a + q:64 + 16 * a + 16:4, ROW:2 * ROW])
 
         def load_plane(t):
             nc.sync.dma_start(planes[t][:], x_rows[t])
@@ -113,11 +149,12 @@ def tile_list_snowpack_recurrence_kernel(tc, tab_words, tab_scales, offs, xT, of
             for u, piece in enumerate(wx_raw[g]):
                 nc.sync.dma_start(piece[:], wx_rows[:, :, g * W + u * width:g * W + (u + 1) * width])
 
-        def round_wx(g, kib):
-            rounded = placed([W * PACK], BF16, "wx_b%d" % g, kib)
+        def round_wx(g):
+            rounded = placed([W * PACK], BF16, "wx_b%d" % g)
+            by_column = rounded[:].rearrange("p (t m j) -> p m j t", t=PACK, j=PACK)
             count = P // len(wx_raw[g])
             for u, piece in enumerate(wx_raw[g]):
-                nc.scalar.copy(rounded[:].rearrange("p (t m j) -> p m j t", t=PACK, j=PACK)[:, u * count:(u + 1) * count],
+                nc.scalar.copy(by_column[:, u * count:(u + 1) * count],
                                piece[:].rearrange("p j (m t) -> p m j t", t=PACK))
             return rounded[:]
 
@@ -138,14 +175,15 @@ def tile_list_snowpack_recurrence_kernel(tc, tab_words, tab_scales, offs, xT, of
             wx_codes, wx_scales = wx_q[g]
             x_codes, x_scales = x_q[half]
             nc.tensor.matmul_mx(sums, lhsT=wx_codes[:, cols].bitcast(FP8X4), lhsT_scale=wx_scales[:, cols],
-                                rhs=x_codes[:, span].bitcast(FP8X4), rhs_scale=x_scales[:, span], start=start, stop=stop)
+                                rhs=x_codes[:, span].bitcast(FP8X4), rhs_scale=x_scales[:, span],
+                                start=start, stop=stop)
 
         def pass_wp(bank, half, g, t, a, start, stop):
             c0 = (g * PACK + t) * P
             scale_bytes = pass_s[a][:].bitcast(U8)
             nc.tensor.matmul_mx(bank[:], lhsT=wp_c[:, a, 2 * c0:2 * (c0 + P)].bitcast(FP4X4),
                                 lhsT_scale=scale_bytes[:, S + c0:S + c0 + P],
-                                rhs=v_c[half][a][:].bitcast(FP8X4), rhs_scale=scale_bytes[:, half * W:(half + 1) * W],
+                                rhs=v_c[half, a][:].bitcast(FP8X4), rhs_scale=scale_bytes[:, half * W:(half + 1) * W],
                                 start=start, stop=stop)
 
         def pass_wr(sums, g, t, a, h_codes, h_scales, start, stop):
@@ -169,7 +207,7 @@ def tile_list_snowpack_recurrence_kernel(tc, tab_words, tab_scales, offs, xT, of
         nc.sync.dma_start(list_v[:], offs)
         nc.sync.dma_start(tab_s[0:32, :], tab_scales.rearrange("a q n -> (a q) n").bitcast(I32))
         nc.sync.dma_start(w_s_raw[0:32, :], wp_scales.rearrange("a q n -> (a q) n").bitcast(I32))
-        nc.sync.dma_start(w_s_raw[32:64, :], wr_scales.rearrange("a q n -> (a q) n").bitcast(I32))
+        nc.sync.dma_start(w_s_raw[64:96, :], wr_scales.rearrange("a q n -> (a q) n").bitcast(I32))
         nc.sync.dma_start(list_3[:], offs3)
         load_plane(0)
         nc.sync.dma_start(list_2[:], offs2)
@@ -180,126 +218,93 @@ def tile_list_snowpack_recurrence_kernel(tc, tab_words, tab_scales, offs, xT, of
         nc.vector.tensor_copy(stage[:, ROW:2 * ROW].bitcast(U8).rearrange("p (g t m) -> p g m t", m=P, t=PACK),
                               w_s_raw[:].bitcast(U8).rearrange("p (g m t) -> p g m t", m=P, t=PACK))
         nc.vector.tensor_copy(stage[:, 0:ROW], v_s_rows[:].bitcast(I32))
-        moves = [(a, q) for a in range(PASSES) for q in range(QUADRANTS)]
         load_wx(0)
         load_table(0)
         load_plane(3)
-        for a, q in moves[0:QUADRANTS]:
-            move_table_scales(a, q)
+        move_pass_scales(0)
         load_table(1)
-        for a, q in moves[QUADRANTS:]:
-            move_table_scales(a, q)
+        move_pass_scales(1)
         load_wx(1)
         nc.sync.dma_start(gain_sb[:], gain.rearrange("(g p t) -> p g t", g=GROUPS, t=PACK))
         nc.sync.dma_start(wr_raw[:], wr_words.rearrange("a p n t -> p a (n t)").bitcast(I32))
-        for a, q in moves:
-            move_wr_scales(a, q)
+        for a in range(GROUPS):
+            move_wr_scales(a)
 
-        wp_c = placed([PASSES, 2 * H], U8, "wp_c", 191)
+        wp_c = placed([PASSES, 2 * H], U8, "wp_c")
         nc.scalar.copy(wp_c[:].bitcast(U16).rearrange("p a (g t m) -> p (a g) t m", g=GROUPS, t=PACK),
                        wp_raw[:].bitcast(U16).rearrange("p a (g m t) -> p (a g) t m", g=GROUPS, t=PACK))
-        wx_b = [round_wx(0, 147)]
-        diff_first = group_tile("diff_first", 73)
-        minus_second = [placed([W], F32, "minus_second0", 145)[:], placed([W], F32, "minus_second1", 171)[:]]
-        wx_q = [mx_tiles("wx0"), mx_tiles("wx1")]
-        v_c = [[placed([W], U32, "v_first%d" % a, 183 + 2 * a) for a in range(PASSES)],
-               [None, placed([W], U32, "v_second1", 187)]]
+        wx_b0 = round_wx(0)
+        diff_first = placed([PACK, W], F32, "diff_first")
+        minus_second = [placed([W], F32, "minus_second%d" % t)[:] for t in range(EARLY_PLANES)]
+        wx_q = [mx_tiles("wx%d" % g) for g in range(GROUPS)]
+        v_c = {(0, a): placed_row([W], U32, "v_first", a, 2) for a in range(PASSES)}
+        v_c[1, 1] = placed([W], U32, "v_second1")
         for t in range(PACK):
             if t == PACK - 1:
-                quantise(wx_b[0], wx_q[0][0][:], wx_q[0][1][:])
-                gather_v(v_c[0][0], 0, 0)
-            minus = placed([W], F32, "minus_first%d" % t, 137 + 2 * t)[:]
-            gather_minus(minus, 0, t)
-            if t < 2:
-                gather_minus(minus_second[t], 1, t)
-            gather_diff(diff_first[:, t, :], minus, 0, t)
+                quantise(wx_b0, wx_q[0][0][:], wx_q[0][1][:])
+                gather_v(0, 0)
+            minus = placed_row([W], F32, "minus_first", t, 2)[:]
+            parts = [whole] if t < EARLY_PLANES else spans
+            gather_minus(minus, 0, t, parts)
+            if t < EARLY_PLANES:
+                gather_minus(minus_second[t], 1, t, [whole])
+            gather_diff(diff_first, minus, 0, t, parts)
         for half in range(HALVES):
-            gather_v(v_c[half][1], half, 1)
-        x_b = interleave(nc.scalar.copy, diff_first, placed([W * PACK], BF16, "x_b0", 151), 2, spans)
-        x_q = [mx_tiles("x0", 56), mx_tiles("x1")]
-        quantise(x_b, x_q[0][0][:], x_q[0][1][:])
-        wx_b.append(round_wx(1, 98))
+            gather_v(half, 1)
+        x_b0 = interleave(nc.scalar.copy, diff_first, placed([W * PACK], BF16, "x_b0"), 2, spans)
+        x_q = [mx_tiles("x%d" % half) for half in range(HALVES)]
+        quantise(x_b0, x_q[0][0][:], x_q[0][1][:])
+        wx_b1 = round_wx(1)
+        diff_second = placed([PACK, W], F32, "diff_second")
+        for t in range(EARLY_PLANES):
+            gather_diff(diff_second, minus_second[t], 1, t, [whole])
+        quantise(wx_b1, wx_q[1][0][:], wx_q[1][1][:])
 
-        diff_second = group_tile("diff_second", 154)
-        for t in range(2):
-            gather_diff(diff_second[:, t, :], minus_second[t], 1, t)
-        quantise(wx_b[1], wx_q[1][0][:], wx_q[1][1][:])
         banks = [new_bank(k) for k in range(BANKS)]
         for a in range(PASSES):
             for k in range(BANKS):
                 pass_wp(banks[k], 0, k // PACK, k % PACK, a, a == 0, False)
-        th_first = [group_tile("th_first%d" % g, 32 + 8 * g) for g in range(GROUPS)]
+        th_first = [placed_row([PACK, W], F32, "th_first", g, 8) for g in range(GROUPS)]
         for k in range(BANKS):
             g, t = divmod(k, PACK)
-            pass_b(banks[k][:], 0, g, t, slice(0, W), False, True)
+            pass_b(banks[k][:], 0, g, t, whole, False, True)
             nc.scalar.activation(th_first[g][:, t, :], banks[k][:], ACT.Tanh)
 
-        late_minus = placed([2, W], F32, "late_minus", 101)
-        minus_second.extend([late_minus[:, 0, :], late_minus[:, 1, :]])
-        h_b0 = [placed([RUN, PACK], BF16, "h_b0a", 96.5)]
+        late_minus = placed([PACK - EARLY_PLANES, W], F32, "late_minus")
+        h_b0 = [placed([RUN, PACK], BF16, "h_b0a")]
         gain_on_gpsimd(th_first[0], 0, h_b0[0][:], spans[0])
-        for t in range(2, PACK):
-            gather_minus(minus_second[t], 1, t)
-        v_c[1][0] = placed([W], U32, "v_second0", 98.5)
-        gather_v(v_c[1][0], 1, 0)
-        for t in range(2, PACK):
-            gather_diff(diff_second[:, t, :], minus_second[t], 1, t)
-        by_tile = placed([PACK, W], BF16, "by_tile", 125)
+        for t in range(EARLY_PLANES, PACK):
+            gather_minus(late_minus[:, t - EARLY_PLANES, :], 1, t, [whole])
+        v_c[1, 0] = placed([W], U32, "v_second0")
+        gather_v(1, 0)
+        for t in range(EARLY_PLANES, PACK):
+            gather_diff(diff_second, late_minus[:, t - EARLY_PLANES, :], 1, t, spans if t == PACK - 1 else [whole])
+        by_tile = placed([PACK, W], BF16, "by_tile")
         for t in range(PACK):
             nc.scalar.activation(by_tile[:, t, :], th_first[1][:, t, :], ACT.Copy, scale=gain_sb[:, 1, t:t + 1])
-        h_b1 = interleave(nc.scalar.copy, by_tile, placed([W * PACK], BF16, "h_b1", 173), 4, [slice(0, W)])
-        x_b = interleave(nc.vector.tensor_copy, diff_second, placed([W * PACK], BF16, "x_b1", 105), 4, spans)
+        h_b1 = interleave(nc.scalar.copy, by_tile, placed([W * PACK], BF16, "h_b1"), 4, [whole])
+        x_b1 = interleave(nc.vector.tensor_copy, diff_second, placed([W * PACK], BF16, "x_b1"), 4, spans)
         for span in spans:
-            quantise(x_b[:, PACK * span.start:PACK * span.stop], x_q[1][0][:, span], x_q[1][1][:, span])
-        wr_c = [placed([H], U32, "wr_c0", 108), placed([H], U32, "wr_c1", 40)]
+            quantise(x_b1[:, PACK * span.start:PACK * span.stop], x_q[1][0][:, span], x_q[1][1][:, span])
+        wr_c = [placed([H], U32, "wr_c%d" % a) for a in range(GROUPS)]
         nc.vector.tensor_copy(wr_c[0][:].bitcast(I32).rearrange("p (g t m) -> p g m t", g=GROUPS, t=PACK),
                               wr_raw[:, 0, :].rearrange("p (g m t) -> p g m t", g=GROUPS, t=PACK))
         nc.scalar.copy(wr_c[1][:].rearrange("p (g t m) -> p g m t", g=GROUPS, t=PACK),
                        wr_raw[:, 1, :].bitcast(U32).rearrange("p (g m t) -> p g m t", g=GROUPS, t=PACK))
 
-        def quantise_run(r, kib):
-            codes, block_scales = placed([RUN], U32, "h0_codes%d" % r, kib), sbuf([RUN], U8, "h0_scales%d" % r)
+        def quantise_run(r):
+            codes, block_scales = placed([RUN], U32, "h0_codes%d" % r), sbuf([RUN], U8, "h0_scales%d" % r)
             quantise(h_b0[r][:].rearrange("p j t -> p (j t)"), codes[:], block_scales[:])
             return codes[:], block_scales[:]
 
-        h0_runs = [quantise_run(0, 106)]
+        h0_runs = [quantise_run(0)]
         h1_q = mx_tiles("h1")
         quantise(h_b1, h1_q[0][:], h1_q[1][:])
-        h_b0.append(placed([RUN, PACK], BF16, "h_b0b", 173))
+        h_b0.append(placed([RUN, PACK], BF16, "h_b0b"))
         gain_on_gpsimd(th_first[0], 0, h_b0[1][:], spans[1])
 
-        early_b = group_tile("early_b", 118)
-        b_pairs = [early_b[:, 0:2, :], early_b[:, 2:PACK, :],
-                   placed([2, W], F32, "b_pair2", 128)[:]]
-
-        def keep_b(tiles, b_banks, copy):
-            for k, b_bank in zip(tiles, b_banks):
-                bank = new_bank(b_bank)
-                pass_b(bank[:], 1, k // PACK, k % PACK, slice(0, W), True, True)
-                copy(b_pairs[k // 2][:, k % 2, :], bank[:])
-
-        def add_and_tanh(sums, g, k, kib, singly):
-            total = placed([2, W], F32, "total%d%d" % (g, k), kib)
-            for u in range(2):
-                nc.vector.tensor_tensor(total[:, u, :], sums[PACK * g + 2 * k + u][:], b_pairs[2 * g + k][:, u, :], ALU.add)
-            for rows in ([slice(0, 1), slice(1, 2)] if singly else [slice(0, 2)]):
-                nc.scalar.activation(th_second[g][:, 2 * k + rows.start:2 * k + rows.stop, :], total[:, rows, :],
-                                     ACT.Tanh)
-
-        def second_step_first_half(r, result, pairs):
-            h_run = [h0_runs[r], (h1_q[0][:, spans[r]], h1_q[1][:, spans[r]])]
-            for k in pairs:
-                g, t0 = k // 2, 2 * (k % 2)
-                bank = new_bank(FREED[PACK * r + k])
-                for u in range(2):
-                    pass_b(bank[:, spans[u]], 0, g, t0 + u, spans[r], u == 0, False)
-                for u in range(2):
-                    for a in range(GROUPS):
-                        pass_wr(bank[:, spans[u]], g, t0 + u, a, h_run[a][0], h_run[a][1], False,
-                                u == 1 and a == GROUPS - 1)
-                nc.scalar.activation(result[:, k, :], bank[:], ACT.Tanh)
-                nc.sync.dma_start(out_rows[g][:, t0:t0 + 2, spans[r]],
-                                  result[:, k, :].rearrange("p (t j) -> p t j", j=RUN))
+        early_b = placed([PACK, W], F32, "early_b")
+        b_pairs = [early_b[:, 0:2, :], early_b[:, 2:PACK, :], placed([2, W], F32, "b_pair2")[:]]
 
         def table_passes(tiles, sum_banks):
             for k, sum_bank in zip(tiles, sum_banks):
@@ -307,25 +312,55 @@ def tile_list_snowpack_recurrence_kernel(tc, tab_words, tab_scales, offs, xT, of
                 for a in range(PASSES):
                     pass_wp(sums[k], 1, k // PACK, k % PACK, a, a == 0, a == PASSES - 1)
 
+        def keep_b(tiles, b_banks, copy):
+            for k, b_bank in zip(tiles, b_banks):
+                bank = new_bank(b_bank)
+                pass_b(bank[:], 1, k // PACK, k % PACK, whole, True, True)
+                copy(b_pairs[k // 2][:, k % 2, :], bank[:])
+
+        def add_and_tanh(g, pair, widths):
+            total = placed_row([2, W], F32, "total%d" % g, pair, 4)
+            for u in range(2):
+                nc.vector.tensor_tensor(total[:, u, :], sums[PACK * g + 2 * pair + u][:],
+                                        b_pairs[2 * g + pair][:, u, :], ALU.add)
+            for rows in widths:
+                nc.scalar.activation(th_second[g][:, 2 * pair + rows.start:2 * pair + rows.stop, :],
+                                     total[:, rows, :], ACT.Tanh)
+
+        def second_step_first_half(r, result, pairs):
+            h_run = [h0_runs[r], (h1_q[0][:, spans[r]], h1_q[1][:, spans[r]])]
+            for pair in pairs:
+                g, t0 = pair // 2, 2 * (pair % 2)
+                bank = new_bank(FREED[PACK * r + pair])
+                for u in range(2):
+                    pass_b(bank[:, spans[u]], 0, g, t0 + u, spans[r], u == 0, False)
+                for u in range(2):
+                    for a in range(GROUPS):
+                        pass_wr(bank[:, spans[u]], g, t0 + u, a, h_run[a][0], h_run[a][1], False,
+                                u == 1 and a == GROUPS - 1)
+                nc.scalar.activation(result[:, pair, :], bank[:], ACT.Tanh)
+                nc.sync.dma_start(out_rows[g][:, t0:t0 + 2, spans[r]],
+                                  result[:, pair, :].rearrange("p (t j) -> p t j", j=RUN))
+
         sums = {}
         table_passes([0, 1, 2, 3, 6], range(5))
-        th_second = [group_tile("th_second%d" % g, 8 * g) for g in range(GROUPS)]
-        keep_b(range(4), [5, 6, 7, 5], nc.scalar.copy)
-        for k in range(2):
-            add_and_tanh(sums, 0, k, 155 + 4 * k, False)
-        b_pairs.append(placed([2, W], F32, "b_pair3", 175)[:])
+        th_second = [placed_row([PACK, W], F32, "th_second", g, 8) for g in range(GROUPS)]
+        keep_b(range(PACK), [5, 6, 7, 5], nc.scalar.copy)
+        for pair in range(2):
+            add_and_tanh(0, pair, [slice(0, 2)])
+        b_pairs.append(placed([2, W], F32, "b_pair3")[:])
         keep_b([6, 7], [6, 0], nc.vector.tensor_copy)
         keep_b([4, 5], [7, 5], nc.scalar.copy)
-        h0_runs.append(quantise_run(1, 155))
+        h0_runs.append(quantise_run(1))
         table_passes([7, 4, 5], [1, 2, 3])
-        result = group_tile("result_first0", 16)
-        second_step_first_half(0, result, range(EARLY_RESULTS))
-        for k in (1, 0):
-            add_and_tanh(sums, 1, k, 73 + 4 * k, True)
-        second_step_first_half(0, result, range(EARLY_RESULTS, PACK))
-        second_step_first_half(1, group_tile("result_first1", 24), range(PACK))
+        first_run = placed_row([PACK, W], F32, "result_first", 0, 8)
+        second_step_first_half(0, first_run, range(EARLY_RESULTS))
+        for pair in (1, 0):
+            add_and_tanh(1, pair, [slice(0, 1), slice(1, 2)])
+        second_step_first_half(0, first_run, range(EARLY_RESULTS, PACK))
+        second_step_first_half(1, placed_row([PACK, W], F32, "result_first", 1, 8), range(PACK))
 
-        rounded = [placed([GROUPS, RUN, PACK], BF16, "h_run0", 171)[:], placed([GROUPS, RUN, PACK], BF16, "h_run1", 163)[:]]
+        rounded = [placed([GROUPS, RUN, PACK], BF16, "h_run%d" % r)[:] for r in range(2)]
         h_runs = [mx_tiles("h_second%d" % r) for r in range(2)]
         gain_on_gpsimd(th_second[0], 0, rounded[0][:, 0, 0:THIRD_ON_GPSIMD, :], slice(0, THIRD_ON_GPSIMD))
         gain_on_vector(th_second[0], 0, rounded[1][:, 0, :, :], spans[1])
@@ -333,25 +368,23 @@ def tile_list_snowpack_recurrence_kernel(tc, tab_words, tab_scales, offs, xT, of
         for r in range(2):
             gain_on_vector(th_second[1], 1, rounded[r][:, 1, :, :], spans[r])
             quantise(rounded[r].rearrange("p g j t -> p (g j t)"), h_runs[r][0][:], h_runs[r][1][:])
-        totals = [group_tile("total_last0", 32), group_tile("total_last1", 137)]
-        results = [group_tile("result_last0", 65), group_tile("result_last1", 81)]
+        totals = [placed([PACK, W], F32, "total_last%d" % r) for r in range(2)]
+        results = [placed([PACK, W], F32, "result_last%d" % r) for r in range(2)]
         for r in range(2):
             h_codes, h_scales = h_runs[r]
-            for k in range(PACK):
-                g, t0 = k // 2, 2 * (k % 2)
-                bank = new_bank(FREED[PACK * r + k])
-                for t in range(t0, t0 + 2):
+            for pair in range(PACK):
+                g, t0 = pair // 2, 2 * (pair % 2)
+                bank = new_bank(FREED[PACK * r + pair])
+                for u in range(2):
                     for a in range(GROUPS):
-                        pass_wr(bank[:, spans[t - t0]], g, t, a, h_codes[:, spans[a]], h_scales[:, spans[a]],
+                        pass_wr(bank[:, spans[u]], g, t0 + u, a, h_codes[:, spans[a]], h_scales[:, spans[a]],
                                 a == 0, a == GROUPS - 1)
-                last = r == 1 and k == PACK - 1
-                for u in ((0, 1) if last else (None,)):
-                    rows = slice(t0, t0 + 2) if u is None else slice(t0 + u, t0 + u + 1)
-                    pair_rows = slice(0, 2) if u is None else slice(u, u + 1)
-                    part = slice(0, W) if u is None else spans[u]
-                    total = totals[r][:, k, part].rearrange("p (t j) -> p t j", j=RUN)
-                    nc.vector.tensor_tensor(total, bank[:, part].rearrange("p (t j) -> p t j", j=RUN),
-                                            b_pairs[k][:, pair_rows, spans[r]], ALU.add)
-                    nc.scalar.activation(results[r][:, k, part], totals[r][:, k, part], ACT.Tanh)
-                    nc.sync.dma_start(out_rows[g][:, rows, W + r * RUN:W + (r + 1) * RUN],
-                                      results[r][:, k, part].rearrange("p (t j) -> p t j", j=RUN))
+                last = r == 1 and pair == PACK - 1
+                for rows in ([slice(0, 1), slice(1, 2)] if last else [slice(0, 2)]):
+                    part = slice(rows.start * RUN, rows.stop * RUN)
+                    nc.vector.tensor_tensor(totals[r][:, pair, part].rearrange("p (t j) -> p t j", j=RUN),
+                                            bank[:, part].rearrange("p (t j) -> p t j", j=RUN),
+                                            b_pairs[pair][:, rows, spans[r]], ALU.add)
+                    nc.scalar.activation(results[r][:, pair, part], totals[r][:, pair, part], ACT.Tanh)
+                    nc.sync.dma_start(out_rows[g][:, t0 + rows.start:t0 + rows.stop, W + r * RUN:W + (r + 1) * RUN],
+                                      results[r][:, pair, part].rearrange("p (t j) -> p t j", j=RUN))

from contextlib import ExitStack

import concourse.mybir as mybir

K, K2, H, T, S = 1024, 512, 1024, 2048, 1024
FLOPS = 2 * S * H * (K + K2 + H)

F32 = mybir.dt.float32
BF16 = mybir.dt.bfloat16
I32 = mybir.dt.int32
U32 = mybir.dt.uint32
U16 = mybir.dt.uint16
U8 = mybir.dt.uint8
FP8X4 = mybir.dt.float8_e4m3fn_x4
FP4X4 = mybir.dt.float4_e2m1fn_x4
ALU = mybir.AluOpType
ACT = mybir.ActivationFunctionType

P = 128
PACK = 4
QUADRANTS = 4
STRIPE = 16
W = 512
RUN = W // 2
HALVES = S // W
GROUPS = H // (P * PACK)
PASSES = K // (P * PACK)
BANKS = 8
ROW = H // 4
EARLY_PLANES = 2
EARLY_RESULTS = 1
THIRD_ON_GPSIMD = 192
FREED = [6, 0, 7, 5, 4, 1, 2, 3]

PLACE = {
    "plane": 0, "th_second": 0, "result_first": 16,
    "wx_raw0": 32, "wx_raw1": 40, "th_first": 32, "total_last0": 32,
    "wr_c1": 40,
    "tab_w": 48,
    "x0": 56,
    "wr_raw": 65, "result_last0": 65, "diff_first": 73, "total1": 73, "result_last1": 81,
    "wx_b1": 98,
    "h_b0a": 96.5,
    "v_second0": 98.5,
    "late_minus": 101,
    "x_b1": 105,
    "h0_codes0": 106,
    "wr_c0": 108,
    "by_tile": 125,
    "early_b": 118,
    "b_pair2": 128,
    "minus_first": 137, "total_last1": 137, "minus_second0": 145, "wx_b0": 147, "x_b0": 151,
    "diff_second": 154,
    "total0": 155,
    "h0_codes1": 155,
    "h_run1": 163, "minus_second1": 171, "h_b1": 173,
    "h_b0b": 173,
    "b_pair3": 175,
    "h_run0": 171,
    "wp_raw": 179, "v_first": 183, "v_second1": 187, "wp_c": 191,
}


def tile_list_snowpack_recurrence_kernel(tc, tab_words, tab_scales, offs, xT, offs2, offs3, wp_words,
                                                   wp_scales, wx, gain, wr_words, wr_scales, out):
    nc = tc.nc
    with ExitStack() as ctx:
        keep = ctx.enter_context(tc.tile_pool(name="keep", bufs=1))
        arena = ctx.enter_context(tc.tile_pool(name="arena", bufs=1))
        psum = ctx.enter_context(tc.psum_pool(name="psum", bufs=1))

        def at(shape, dtype, name, kib):
            return arena.tile([P] + shape, dtype, name=name, align_bytes=256, offset=int(kib * 1024))

        def placed(shape, dtype, name):
            return at(shape, dtype, name, PLACE[name])

        def placed_row(shape, dtype, name, n, kib_each):
            return at(shape, dtype, "%s%d" % (name, n), PLACE[name] + n * kib_each)

        def sbuf(shape, dtype, name):
            return keep.tile([P] + shape, dtype, name=name, align_bytes=256)

        def mx_tiles(name):
            codes = at([W], U32, name + "_codes", PLACE[name]) if name in PLACE else sbuf([W], U32, name + "_codes")
            return codes, sbuf([W], U8, name + "_scales")

        list_v = keep.tile([P, S // STRIPE], U16, name="list_v")
        list_2 = keep.tile([P, S // STRIPE], U16, name="list_2")
        list_3 = keep.tile([P, S // STRIPE], U16, name="list_3")

        tab_s = sbuf([T // 4], I32, "tab_s")
        w_s_raw = sbuf([ROW], I32, "w_s_raw")
        pass_s = [sbuf([2 * ROW], I32, "pass_s%d" % a) for a in range(PASSES)]
        wr_s = sbuf([ROW], I32, "wr_s")
        nc.vector.memset(tab_s[32:64, :], 0)
        nc.vector.memset(tab_s[64:P, :], 0)
        nc.vector.memset(w_s_raw[32:64, :], 0)
        nc.vector.memset(w_s_raw[96:P, :], 0)
        for scale_tile in pass_s + [wr_s]:
            nc.vector.memset(scale_tile[:], 0)
        v_s_rows = sbuf([S], U8, "v_s_rows")
        stage = sbuf([2 * ROW], I32, "stage")
        gain_sb = keep.tile([P, GROUPS, PACK], F32, name="gain_sb")

        planes = [placed_row([T], F32, "plane", t, 8) for t in range(PACK)]
        wx_raw = [[placed([PACK, W], F32, "wx_raw0")],
                  [placed_row([PACK, RUN], F32, "wx_raw1", u, 4) for u in range(2)]]
        tab_w = [placed_row([T], I32, "tab_w", a, 8) for a in range(PASSES)]
        wr_raw = placed([GROUPS, H], I32, "wr_raw")
        wp_raw = placed([PASSES, H // 2], I32, "wp_raw")
        x_rows = xT.rearrange("(p t) n -> t p n", t=PACK)
        wx_rows = wx.rearrange("(p j) c -> p j c", j=PACK)
        out_rows = out.rearrange("(g p t) j -> g p t j", g=GROUPS, t=PACK)
        whole = slice(0, W)
        spans = [slice(r * RUN, (r + 1) * RUN) for r in range(2)]

        def entries(list_tile, half, span):
            return list_tile[:, (half * W + span.start) // STRIPE:(half * W + span.stop) // STRIPE]

        def gather_minus(minus, half, t, parts):
            for span in parts:
                nc.vector.tensor_copy(minus[:, span], planes[t][:].indirect(entries(list_3, half, span)))

        def gather_diff(diff, minus, half, t, parts):
            for span in parts:
                nc.vector.tensor_tensor(diff[:, t, span], planes[t][:].indirect(entries(list_2, half, span)),
                                        minus[:, span], ALU.subtract)

        def gather_v(half, a):
            nc.vector.tensor_copy(v_c[half, a][:], tab_w[a][:].bitcast(U32).indirect(entries(list_v, half, whole)))

        def move_pass_scales(a):
            for q in range(QUADRANTS):
                nc.sync.dma_start(pass_s[a][q:P:32, :], stage[16 * a + q:16 * a + 16:4, :])

        def move_wr_scales(a):
            for q in range(QUADRANTS):
                nc.sync.dma_start(wr_s[4 * a + q:P:32, :], stage[64 + 16 * a + q:64 + 16 * a + 16:4, ROW:2 * ROW])

        def load_plane(t):
            nc.sync.dma_start(planes[t][:], x_rows[t])

        def load_table(a):
            nc.sync.dma_start(tab_w[a][:], tab_words[a].rearrange("p n t -> p (n t)").bitcast(I32))

        def load_wx(g):
            width = W // len(wx_raw[g])
            for u, piece in enumerate(wx_raw[g]):
                nc.sync.dma_start(piece[:], wx_rows[:, :, g * W + u * width:g * W + (u + 1) * width])

        def round_wx(g):
            rounded = placed([W * PACK], BF16, "wx_b%d" % g)
            by_column = rounded[:].rearrange("p (t m j) -> p m j t", t=PACK, j=PACK)
            count = P // len(wx_raw[g])
            for u, piece in enumerate(wx_raw[g]):
                nc.scalar.copy(by_column[:, u * count:(u + 1) * count],
                               piece[:].rearrange("p j (m t) -> p m j t", t=PACK))
            return rounded[:]

        def quantise(rounded, codes, block_scales):
            nc.vector.quantize_mx(out=codes.bitcast(FP8X4), scales=block_scales, in_=rounded)

        def interleave(copy, rows, words, step, parts):
            for span in parts:
                copy(words[:, PACK * span.start:PACK * span.stop].rearrange("p (c i t) -> p c t i", i=step, t=PACK),
                     rows[:, :, span].rearrange("p t (c i) -> p c t i", i=step))
            return words[:]

        def new_bank(k):
            return psum.tile([P, W], F32, name="bank%d" % k)

        def pass_b(sums, half, g, t, span, start, stop):
            cols = slice(t * P, (t + 1) * P)
            wx_codes, wx_scales = wx_q[g]
            x_codes, x_scales = x_q[half]
            nc.tensor.matmul_mx(sums, lhsT=wx_codes[:, cols].bitcast(FP8X4), lhsT_scale=wx_scales[:, cols],
                                rhs=x_codes[:, span].bitcast(FP8X4), rhs_scale=x_scales[:, span],
                                start=start, stop=stop)

        def pass_wp(bank, half, g, t, a, start, stop):
            c0 = (g * PACK + t) * P
            scale_bytes = pass_s[a][:].bitcast(U8)
            nc.tensor.matmul_mx(bank[:], lhsT=wp_c[:, a, 2 * c0:2 * (c0 + P)].bitcast(FP4X4),
                                lhsT_scale=scale_bytes[:, S + c0:S + c0 + P],
                                rhs=v_c[half, a][:].bitcast(FP8X4), rhs_scale=scale_bytes[:, half * W:(half + 1) * W],
                                start=start, stop=stop)

        def pass_wr(sums, g, t, a, h_codes, h_scales, start, stop):
            c0 = (g * PACK + t) * P
            nc.tensor.matmul_mx(sums, lhsT=wr_c[a][:, c0:c0 + P].bitcast(FP8X4),
                                lhsT_scale=wr_s[:].bitcast(U8)[4 * a:P, c0:c0 + P],
                                rhs=h_codes.bitcast(FP8X4), rhs_scale=h_scales, start=start, stop=stop)

        def gain_on_gpsimd(th, g, rounded, cols):
            count = cols.stop - cols.start
            nc.gpsimd.tensor_tensor(rounded, th[:, :, cols].rearrange("p t c -> p c t"),
                                    gain_sb[:, g, :].unsqueeze(1).to_broadcast([P, count, PACK]), ALU.mult)

        def gain_on_vector(th, g, rounded, cols):
            pairs = (cols.stop - cols.start) // 2
            nc.vector.tensor_tensor(rounded.rearrange("p (c i) t -> p c t i", i=2),
                                    th[:, :, cols].rearrange("p t (c i) -> p c t i", i=2),
                                    gain_sb[:, g, :].unsqueeze(1).unsqueeze(3).to_broadcast([P, pairs, PACK, 2]),
                                    ALU.mult)

        nc.sync.dma_start(list_v[:], offs)
        nc.sync.dma_start(tab_s[0:32, :], tab_scales.rearrange("a q n -> (a q) n").bitcast(I32))
        nc.sync.dma_start(w_s_raw[0:32, :], wp_scales.rearrange("a q n -> (a q) n").bitcast(I32))
        nc.sync.dma_start(w_s_raw[64:96, :], wr_scales.rearrange("a q n -> (a q) n").bitcast(I32))
        nc.sync.dma_start(list_3[:], offs3)
        load_plane(0)
        nc.sync.dma_start(list_2[:], offs2)
        load_plane(1)
        nc.sync.dma_start(wp_raw[:], wp_words.rearrange("a p n -> p a n").bitcast(I32))
        load_plane(2)
        nc.vector.tensor_copy(v_s_rows[:], tab_s[:].bitcast(U8).indirect(list_v[:]))
        nc.vector.tensor_copy(stage[:, ROW:2 * ROW].bitcast(U8).rearrange("p (g t m) -> p g m t", m=P, t=PACK),
                              w_s_raw[:].bitcast(U8).rearrange("p (g m t) -> p g m t", m=P, t=PACK))
        nc.vector.tensor_copy(stage[:, 0:ROW], v_s_rows[:].bitcast(I32))
        load_wx(0)
        load_table(0)
        load_plane(3)
        move_pass_scales(0)
        load_table(1)
        move_pass_scales(1)
        load_wx(1)
        nc.sync.dma_start(gain_sb[:], gain.rearrange("(g p t) -> p g t", g=GROUPS, t=PACK))
        nc.sync.dma_start(wr_raw[:], wr_words.rearrange("a p n t -> p a (n t)").bitcast(I32))
        for a in range(GROUPS):
            move_wr_scales(a)

        wp_c = placed([PASSES, 2 * H], U8, "wp_c")
        nc.scalar.copy(wp_c[:].bitcast(U16).rearrange("p a (g t m) -> p (a g) t m", g=GROUPS, t=PACK),
                       wp_raw[:].bitcast(U16).rearrange("p a (g m t) -> p (a g) t m", g=GROUPS, t=PACK))
        wx_b0 = round_wx(0)
        diff_first = placed([PACK, W], F32, "diff_first")
        minus_second = [placed([W], F32, "minus_second%d" % t)[:] for t in range(EARLY_PLANES)]
        wx_q = [mx_tiles("wx%d" % g) for g in range(GROUPS)]
        v_c = {(0, a): placed_row([W], U32, "v_first", a, 2) for a in range(PASSES)}
        v_c[1, 1] = placed([W], U32, "v_second1")
        for t in range(PACK):
            if t == PACK - 1:
                quantise(wx_b0, wx_q[0][0][:], wx_q[0][1][:])
                gather_v(0, 0)
            minus = placed_row([W], F32, "minus_first", t, 2)[:]
            parts = [whole] if t < EARLY_PLANES else spans
            gather_minus(minus, 0, t, parts)
            if t < EARLY_PLANES:
                gather_minus(minus_second[t], 1, t, [whole])
            gather_diff(diff_first, minus, 0, t, parts)
        for half in range(HALVES):
            gather_v(half, 1)
        x_b0 = interleave(nc.scalar.copy, diff_first, placed([W * PACK], BF16, "x_b0"), 2, spans)
        x_q = [mx_tiles("x%d" % half) for half in range(HALVES)]
        quantise(x_b0, x_q[0][0][:], x_q[0][1][:])
        wx_b1 = round_wx(1)
        diff_second = placed([PACK, W], F32, "diff_second")
        for t in range(EARLY_PLANES):
            gather_diff(diff_second, minus_second[t], 1, t, [whole])
        quantise(wx_b1, wx_q[1][0][:], wx_q[1][1][:])

        banks = [new_bank(k) for k in range(BANKS)]
        for a in range(PASSES):
            for k in range(BANKS):
                pass_wp(banks[k], 0, k // PACK, k % PACK, a, a == 0, False)
        th_first = [placed_row([PACK, W], F32, "th_first", g, 8) for g in range(GROUPS)]
        for k in range(BANKS):
            g, t = divmod(k, PACK)
            pass_b(banks[k][:], 0, g, t, whole, False, True)
            nc.scalar.activation(th_first[g][:, t, :], banks[k][:], ACT.Tanh)

        late_minus = placed([PACK - EARLY_PLANES, W], F32, "late_minus")
        h_b0 = [placed([RUN, PACK], BF16, "h_b0a")]
        gain_on_gpsimd(th_first[0], 0, h_b0[0][:], spans[0])
        for t in range(EARLY_PLANES, PACK):
            gather_minus(late_minus[:, t - EARLY_PLANES, :], 1, t, [whole])
        v_c[1, 0] = placed([W], U32, "v_second0")
        gather_v(1, 0)
        for t in range(EARLY_PLANES, PACK):
            gather_diff(diff_second, late_minus[:, t - EARLY_PLANES, :], 1, t, spans if t == PACK - 1 else [whole])
        by_tile = placed([PACK, W], BF16, "by_tile")
        for t in range(PACK):
            nc.scalar.activation(by_tile[:, t, :], th_first[1][:, t, :], ACT.Copy, scale=gain_sb[:, 1, t:t + 1])
        h_b1 = interleave(nc.scalar.copy, by_tile, placed([W * PACK], BF16, "h_b1"), 4, [whole])
        x_b1 = interleave(nc.vector.tensor_copy, diff_second, placed([W * PACK], BF16, "x_b1"), 4, spans)
        for span in spans:
            quantise(x_b1[:, PACK * span.start:PACK * span.stop], x_q[1][0][:, span], x_q[1][1][:, span])
        wr_c = [placed([H], U32, "wr_c%d" % a) for a in range(GROUPS)]
        nc.vector.tensor_copy(wr_c[0][:].bitcast(I32).rearrange("p (g t m) -> p g m t", g=GROUPS, t=PACK),
                              wr_raw[:, 0, :].rearrange("p (g m t) -> p g m t", g=GROUPS, t=PACK))
        nc.scalar.copy(wr_c[1][:].rearrange("p (g t m) -> p g m t", g=GROUPS, t=PACK),
                       wr_raw[:, 1, :].bitcast(U32).rearrange("p (g m t) -> p g m t", g=GROUPS, t=PACK))

        def quantise_run(r):
            codes, block_scales = placed([RUN], U32, "h0_codes%d" % r), sbuf([RUN], U8, "h0_scales%d" % r)
            quantise(h_b0[r][:].rearrange("p j t -> p (j t)"), codes[:], block_scales[:])
            return codes[:], block_scales[:]

        h0_runs = [quantise_run(0)]
        h1_q = mx_tiles("h1")
        quantise(h_b1, h1_q[0][:], h1_q[1][:])
        h_b0.append(placed([RUN, PACK], BF16, "h_b0b"))
        gain_on_gpsimd(th_first[0], 0, h_b0[1][:], spans[1])

        early_b = placed([PACK, W], F32, "early_b")
        b_pairs = [early_b[:, 0:2, :], early_b[:, 2:PACK, :], placed([2, W], F32, "b_pair2")[:]]

        def table_passes(tiles, sum_banks):
            for k, sum_bank in zip(tiles, sum_banks):
                sums[k] = new_bank(sum_bank)
                for a in range(PASSES):
                    pass_wp(sums[k], 1, k // PACK, k % PACK, a, a == 0, a == PASSES - 1)

        def keep_b(tiles, b_banks, copy):
            for k, b_bank in zip(tiles, b_banks):
                bank = new_bank(b_bank)
                pass_b(bank[:], 1, k // PACK, k % PACK, whole, True, True)
                copy(b_pairs[k // 2][:, k % 2, :], bank[:])

        def add_and_tanh(g, pair, widths):
            total = placed_row([2, W], F32, "total%d" % g, pair, 4)
            for u in range(2):
                nc.vector.tensor_tensor(total[:, u, :], sums[PACK * g + 2 * pair + u][:],
                                        b_pairs[2 * g + pair][:, u, :], ALU.add)
            for rows in widths:
                nc.scalar.activation(th_second[g][:, 2 * pair + rows.start:2 * pair + rows.stop, :],
                                     total[:, rows, :], ACT.Tanh)

        def second_step_first_half(r, result, pairs):
            h_run = [h0_runs[r], (h1_q[0][:, spans[r]], h1_q[1][:, spans[r]])]
            for pair in pairs:
                g, t0 = pair // 2, 2 * (pair % 2)
                bank = new_bank(FREED[PACK * r + pair])
                for u in range(2):
                    pass_b(bank[:, spans[u]], 0, g, t0 + u, spans[r], u == 0, False)
                for u in range(2):
                    for a in range(GROUPS):
                        pass_wr(bank[:, spans[u]], g, t0 + u, a, h_run[a][0], h_run[a][1], False,
                                u == 1 and a == GROUPS - 1)
                nc.scalar.activation(result[:, pair, :], bank[:], ACT.Tanh)
                nc.sync.dma_start(out_rows[g][:, t0:t0 + 2, spans[r]],
                                  result[:, pair, :].rearrange("p (t j) -> p t j", j=RUN))

        sums = {}
        table_passes([0, 1, 2, 3, 6], range(5))
        th_second = [placed_row([PACK, W], F32, "th_second", g, 8) for g in range(GROUPS)]
        keep_b(range(PACK), [5, 6, 7, 5], nc.scalar.copy)
        for pair in range(2):
            add_and_tanh(0, pair, [slice(0, 2)])
        b_pairs.append(placed([2, W], F32, "b_pair3")[:])
        keep_b([6, 7], [6, 0], nc.vector.tensor_copy)
        keep_b([4, 5], [7, 5], nc.scalar.copy)
        h0_runs.append(quantise_run(1))
        table_passes([7, 4, 5], [1, 2, 3])
        first_run = placed_row([PACK, W], F32, "result_first", 0, 8)
        second_step_first_half(0, first_run, range(EARLY_RESULTS))
        for pair in (1, 0):
            add_and_tanh(1, pair, [slice(0, 1), slice(1, 2)])
        second_step_first_half(0, first_run, range(EARLY_RESULTS, PACK))
        second_step_first_half(1, placed_row([PACK, W], F32, "result_first", 1, 8), range(PACK))

        rounded = [placed([GROUPS, RUN, PACK], BF16, "h_run%d" % r)[:] for r in range(2)]
        h_runs = [mx_tiles("h_second%d" % r) for r in range(2)]
        gain_on_gpsimd(th_second[0], 0, rounded[0][:, 0, 0:THIRD_ON_GPSIMD, :], slice(0, THIRD_ON_GPSIMD))
        gain_on_vector(th_second[0], 0, rounded[1][:, 0, :, :], spans[1])
        gain_on_vector(th_second[0], 0, rounded[0][:, 0, THIRD_ON_GPSIMD:RUN, :], slice(THIRD_ON_GPSIMD, RUN))
        for r in range(2):
            gain_on_vector(th_second[1], 1, rounded[r][:, 1, :, :], spans[r])
            quantise(rounded[r].rearrange("p g j t -> p (g j t)"), h_runs[r][0][:], h_runs[r][1][:])
        totals = [placed([PACK, W], F32, "total_last%d" % r) for r in range(2)]
        results = [placed([PACK, W], F32, "result_last%d" % r) for r in range(2)]
        for r in range(2):
            h_codes, h_scales = h_runs[r]
            for pair in range(PACK):
                g, t0 = pair // 2, 2 * (pair % 2)
                bank = new_bank(FREED[PACK * r + pair])
                for u in range(2):
                    for a in range(GROUPS):
                        pass_wr(bank[:, spans[u]], g, t0 + u, a, h_codes[:, spans[a]], h_scales[:, spans[a]],
                                a == 0, a == GROUPS - 1)
                last = r == 1 and pair == PACK - 1
                for rows in ([slice(0, 1), slice(1, 2)] if last else [slice(0, 2)]):
                    part = slice(rows.start * RUN, rows.stop * RUN)
                    nc.vector.tensor_tensor(totals[r][:, pair, part].rearrange("p (t j) -> p t j", j=RUN),
                                            bank[:, part].rearrange("p (t j) -> p t j", j=RUN),
                                            b_pairs[pair][:, rows, spans[r]], ALU.add)
                    nc.scalar.activation(results[r][:, pair, part], totals[r][:, pair, part], ACT.Tanh)
                    nc.sync.dma_start(out_rows[g][:, t0 + rows.start:t0 + rows.stop, W + r * RUN:W + (r + 1) * RUN],
                                      results[r][:, pair, part].rearrange("p (t j) -> p t j", j=RUN))
